import numpy as np, ml_dtypes
CORES = [25,29,65,69,153,157,193,197]
N = 8
import mx_ref
BF = ml_dtypes.bfloat16
def entries(a):
    return np.ascontiguousarray(a.T).reshape(-1)
def table(e):
    return np.ascontiguousarray(np.reshape(e, (-1, 16)).T).astype(np.int32)
def gentries(a):
    return np.ascontiguousarray(a.reshape(8, 16, -1).transpose(0, 2, 1)).reshape(8, -1)
def gtable(e):
    e = np.asarray(e); return np.ascontiguousarray(e.reshape(8, -1, 16).transpose(0, 2, 1)).reshape(128, -1).astype(np.int32)
def gcols(t, e):
    v = np.concatenate([t.reshape(8, 16, -1, 4), np.zeros((8, 16, 1, 4), BF)], axis=2)
    return np.ascontiguousarray(np.stack([v[g][:, e[g]] for g in range(8)])).reshape(128, -1)
def tile(rs):
    return np.stack(rs, axis=2).reshape(128, -1).astype(BF)
def pick(q, e):
    c = np.concatenate([q[0].reshape(128, -1, 4), np.zeros((128, 1, 4), np.uint8)], axis=1); s = np.concatenate([q[1], np.ones((16, 1), np.uint8)], axis=1)
    return (np.ascontiguousarray(c[:, e].reshape(128, -1)), np.ascontiguousarray(s[:, e]))
def join(*qs):
    return (np.concatenate([q[0] for q in qs], axis=1), np.concatenate([q[1] for q in qs], axis=1))
def put(q, e, v):
    c, s = q[0].reshape(128, -1, 4).copy(), q[1].copy(); c[:, e] = v[0].reshape(128, -1, 4); s[:, e] = v[1]
    return (c.reshape(128, -1), s)
def pk(c, s):
    return (np.ascontiguousarray(c), mx_ref.live(s))
def emit(q):
    return q[0], q[1]
def packed(v, rng):
    q = [mx_ref.quantize(np.ascontiguousarray(v[r])) for r in range(N)]
    return np.stack([a for a, b in q]), np.stack([mx_ref.plane(b, rng) for a, b in q])
def values_of_codes():
    e, c = np.zeros((128, 128, 4), np.float32), np.zeros((128, 2, 4), np.uint8)
    e[np.arange(128), np.arange(128), 0] = 1
    c[:127, :, 0] = np.arange(256).reshape(2, 128).T[:127]
    return mx_ref.matmul(mx_ref.quantize(e.reshape(128, 512).astype(BF)), (c.reshape(128, 8), np.full((16, 2), 127, np.uint8))).T.reshape(-1).astype(np.float64)
CODE_VALUE, SCALE_VALUE = values_of_codes(), 2.0 ** (np.arange(256) - 127.0)
def decode(q):
    return (CODE_VALUE[q[0]].reshape(16, 8, -1, 4) * SCALE_VALUE[q[1]][:, None, :, None] + 0.0).reshape(128, -1).astype(np.float32)
def f(rng, *shape):
    return mx_ref.flush((rng.standard_normal(shape, dtype=np.float32) * np.exp2(rng.integers(-2, 3, shape[:-1] + (1,)))).astype(BF))
def wide(rng, *shape, cols=0):
    v = rng.standard_normal(shape, dtype=np.float32) * np.exp2(rng.integers(-12, 13, shape)).astype(np.float32)
    if cols: v *= np.repeat(np.exp2(rng.integers(-cols, cols + 1, shape[:-2] + (1, shape[-1] // 4))) * (rng.random(shape[:-2] + (1, shape[-1] // 4)) > 0.0625), 4, axis=-1).astype(np.float32)
    return mx_ref.flush(v.astype(BF))
C = 320
STEP = [4, 1, 2]
def numbers_of(rng):
    return {"x": np.array(f(rng, N, 128, 4 * C)), "u": np.array(f(rng, N, 128, 512)), "v": np.array(f(rng, N, 128, 512))}
def orders(rng):
    return rng.permuted(np.tile(np.arange(C), (N, 1)), axis=1)
def pairing(rng):
    p = rng.permuted(np.tile(np.arange(C), (N, 8, 1)), axis=2)
    m = np.zeros((N, 8, C), np.int64)
    np.put_along_axis(m, p[:, :, ::2], p[:, :, 1::2], axis=2)
    np.put_along_axis(m, p[:, :, 1::2], p[:, :, ::2], axis=2)
    return m
def stored(a, t, m):
    return {"la": np.stack([table(a[r]) for r in range(N)]), "lb": np.stack([table(t[r]) for r in range(N)]), "mt": np.stack([gtable(m[r]) for r in range(N)])}
def lists(rng):
    return stored(orders(rng), orders(rng), pairing(rng))
def layers(rng, still=[]):
    w = np.array(f(rng, N, 128, 2048)).reshape(N, 8, 16, 4, 8, 16, 4)
    for i in still:
        w[:, :, i] = 0
        w[:, :, :, :, :, i] = 0
    return w
def weights(rng, w):
    c, p = packed(np.ascontiguousarray(w).reshape(N, 128, 2048), rng)
    return {"wc": c, "ws": p}
def setup_inputs(rng):
    return {**numbers_of(rng), **lists(rng), **weights(rng, layers(rng))}
def setup_inputs_ties(rng):
    d = numbers_of(rng)
    m = pairing(rng)
    o = rng.permutation(N)
    k = rng.integers(0, 4, (N, 8, C))
    k[o[1]] += 1
    k[o[2]] = (np.arange(C) > m[o[2]]) == (rng.permutation(8) < 4)[:, None]
    k[o[3]] = 1
    h = rng.permutation(8)
    k[o[3], h[:4], C - 1] = 2
    k[o[3], h[4:], 0] = 0
    x = d["x"].reshape(N, 8, 16, C, 4)
    x[:, :, 0] = 0
    x[:, :, 0, :, 0] = k.astype(np.float32).astype(BF)
    a = np.tile(np.exp2(rng.integers(-3, 4, (1, 8, 1)).astype(np.float32)), (N, 1, C))
    x[:, :, 8:] = 0
    x[:, :, 8, :, 0] = (-1.125 * a).astype(BF)
    x[:, :, 10, :, 0] = (-0.0703125 * a).astype(BF)
    u = d["u"].reshape(N, 128, 128, 4)
    u[:, :, ::16] = 0
    for r in range(N):
        for i in range(0, 128, 16): u[r, i, i, 0] = 0.0 if r == o[0] else -1.0 if r == o[1] else 1.0
    w = layers(rng, [0])
    w[:, :, :, :, :, 8:] = 0
    for g in range(8):
        w[:, g, 8, 0, g, 8, 0] = -28.0
        for b in range(4): w[:, g, 10, b, g, 9, 0] = -2.0 ** (b - 5)
    return {"x": x.reshape(N, 128, 4 * C), "u": u.reshape(N, 128, 512), "v": d["v"], **stored(orders(rng), orders(rng), m), **weights(rng, w)}
def setup_inputs_near(rng):
    d = numbers_of(rng)
    o = np.zeros(N, np.int64)
    for n, r in enumerate(rng.permutation([r for r in range(N) if r < r ^ STEP[0]])):
        e = rng.integers(2)
        o[r], o[r ^ STEP[0]] = n % 2 * 2 + e, n % 2 * 2 + 1 - e
    x = d["x"].astype(np.float32).reshape(N, 8, 16, C, 4)
    x[:, :, 0] = 0
    x[:, :, 8:] = 0
    u = d["u"].reshape(N, 128, 128, 4)
    u[:, :, ::16] = 0
    w = layers(rng, [0, 1, 8, 9, 10, 11, 12, 13, 14, 15])
    for r in range(N):
        c = rng.choice([-1.0, 1.0], (8, 1))
        s = rng.integers(0, 16, (8, C))
        digits = ((s[:, :, None] >> np.arange(4)) & 1) * np.exp2(np.arange(4) - 23.0)
        if o[r] < 2:
            x[r, :, 0, :, 0] = c
            x[r, :, 8] = digits
            x[r, :, 11, :, 0] = 2.0 ** -10
        elif o[r] == 2:
            x[r, :, 8] = digits * rng.choice([-1.0, 1.0], (8, C, 1))
            x[r, :, 1:8] = 0
            x[r, :, 1, :, 0] = rng.choice([-1.0, 1.0], (8, C)) * 2.0 ** -30
            for g in range(8):
                w[r, g, 1, 0, g, 12, 0] = 2.0 ** -8
                w[r, g, 1, 0, g, 13, 0] = 64.0
        else:
            x[r, :, 8, :, 0] = np.where(s < 8, 1.25, 0.0) * 2.0 ** -30 * c
            x[r, :, 9, :, 0] = np.where(s < 8, 0.0, 1.125) * 2.0 ** -30 * c
            for g in rng.permutation(8)[:4]:
                e = rng.choice([-1.0, 1.0], C) * 2.0 ** -30
                x[r, g, 8, :, 0] = 1.25 * e
                x[r, g, 9, :, 0] = -1.125 * e
        at = [0, C - 1, int(rng.integers(C)), int(rng.integers(C))]
        for g, j in zip(rng.permutation(8)[:4], at): x[r, g, 0, j, 0] = 2.0 ** 29 * rng.choice([-1.0, 1.0])
        k = 1.0 if o[r] == 0 else 2.0 ** -30
        for h in range(0, 128, 16):
            u[r, h, h, 0] = k
            if o[r] < 2: u[r, h + 11, h, 0] = k
            if o[r] < 3: u[r, h + 8, h] = k
            else:
                u[r, h + 8, h, 0] = k
                u[r, h + 9, h, 0] = 1.125 * k
                u[r, h + 12, h, 0] = k
    return {"x": x.reshape(N, 128, 4 * C).astype(BF), "u": u.reshape(N, 128, 512), "v": d["v"], **lists(rng), **weights(rng, w)}
def setup_inputs_odd(rng):
    d = numbers_of(rng)
    x = (1.0 + (2 * rng.integers(0, 64, (N, 16, 8, C, 4)) + 1) * 2.0 ** -7) * np.exp2(-rng.integers(0, 7, (N, 16, 8, C, 4)).astype(np.float64)) * rng.choice([-1.0, 1.0], (N, 16, 8, C, 4))
    x[:, :, 0, :, 0] = 1.96875 * 2.0 ** 8 * rng.choice([-1.0, 1.0], (N, 16, C))
    u = d["u"].reshape(N, 16, 8, 128, 4)
    u[:, :, 0, ::16] = 0
    for r in range(N):
        for n, g in enumerate(rng.permutation(8)[:4]):
            x[r, 2 * g, 1, :, 0] = (8 + rng.integers(0, 2, C)) * 2.0 ** (n % 2 - 8)
            u[r, :, :, 16 * g] = 0
            u[r, 2 * g, 1, 16 * g, 0] = 1.0
    return {"x": x.astype(np.float32).reshape(N, 128, 4 * C).astype(BF), "u": u.reshape(N, 128, 512), "v": d["v"], **lists(rng), **weights(rng, layers(rng, [0, 8]))}
def setup_inputs_ends(rng):
    d = numbers_of(rng)
    o, e = rng.permutation(N) % 4, rng.permutation(N) % 4
    x = np.zeros((N, 8, 16, C, 4))
    u = d["u"].astype(np.float32).reshape(N, 128, 128, 4)
    v = np.zeros((N, 128, 512))
    w = np.zeros((N, 128, 4, 128, 4), np.float32)
    still = int(rng.integers(8))
    i = np.arange(128)
    for r in range(N):
        h = rng.permutation(8)
        c = np.where(h < 2, 0.0, h % 2 * 2.0 - 1.0)[None, :, None]
        large = (0.88 + 0.04 * rng.random((8, 16, C, 4))) * 2.0 ** 30
        if o[r] == 0: x[r] = -large
        if o[r] == 1: x[r] = large * rng.choice([-1.0, 1.0], (C, 1))
        if o[r] == 2: x[r] = -(1.0 + 0.125 * rng.integers(0, 8, (8, 16, C, 4))) * 2.0 ** -30
        if o[r] == 3: x[r] = d["x"][r].astype(np.float32).reshape(8, 16, C, 4)[:, :, :1]
        if o[r] < 2: u[r, :, ::16] = c * (0.9 + 0.1 * rng.random((128, 8, 4))) * 2.0 ** 30
        if o[r] == 2: u[r, :, ::16] = c * (1.0 + 0.125 * rng.integers(0, 8, (128, 8, 4))) * 2.0 ** -30
        if o[r] == 3: u[r, :, ::16] *= np.abs(c).astype(np.float32)
        v[r] = rng.choice([-1.0, 1.0], (128, 512)) * (2.0 ** 30 if o[r] < 2 else 2.0 ** -30)
        k = np.array([0.125, 0.25, 0.5])[rng.permutation(8) % 3]
        if o[r] == 2: k[:] = 32.0
        if o[r] == 3: k[k == 0.125] = 2.0 ** -8
        k[still] = 256.0 if o[r] == 2 else 0.0
        for b in range(4): w[r, i, b, i, b] = k[i // 16]
    a, t, m = orders(rng), orders(rng), pairing(rng)
    j = np.arange(C)
    a[e == 0] = j
    t[e == 0] = j
    m[e == 0] = j ^ 1
    a[e == 1] = C - 1 - j
    t[e == 1] = C - 1 - j
    m[e == 1] = C - 1 - j
    a[e == 2] = (j + 1) % C
    t[e == 2] = (j + C - 1) % C
    m[e == 2] = (j + C // 2) % C
    return {"x": x.astype(np.float32).reshape(N, 128, 4 * C).astype(BF), "u": u.reshape(N, 128, 512).astype(BF), "v": v.astype(np.float32).astype(BF), **stored(a, t, m), **weights(rng, w.astype(BF))}
def setup_inputs_spread(rng):
    d = setup_inputs(rng)
    d["x"] = wide(rng, N, 128, 4 * C, cols=6)
    return d
def check_inputs(d):
    b = []
    for k in ("x", "u", "v"):
        a = np.abs(d[k].astype(np.float32))
        if not (np.isfinite(a).all() and ((a == 0) | (a >= 2.0 ** -30) & (a <= 2.0 ** 30)).all()): b.append("a value of " + k)
    none, least, most = [emit(mx_ref.quantize(np.full((128, 16), k, np.float32).astype(BF)))[1][0, 0] for k in (0.0, 2.0 ** -8, 2.0 ** 8)]
    for r in range(N):
        for k in ("la", "lb"):
            if (np.sort(entries(d[k][r])) != np.arange(C)).any(): b.append(k + ": not every number once")
        m = gentries(d["mt"][r])
        if not ((m >= 0) & (m < C)).all(): b.append("an entry of mt")
        elif (np.take_along_axis(m, m, axis=1) != np.arange(C)).any() or (m == np.arange(C)).any(): b.append("mt: not in pairs")
        if ((d["wc"][r] == 0x7F) | (d["wc"][r] == 0xFF)).any(): b.append("wc: a code that is no number")
        s = mx_ref.live(d["ws"][r])
        if ((s != none) & ((s < least) | (s > most))).any(): b.append("ws: a scale out of range")
        if (((d["wc"][r].reshape(16, 8, 512, 4) & 0x7F) != 0) & (s == none)[:, None, :, None]).any(): b.append("wc: a code other than zero under the scale of zeros")
    return b
def reference(x, u, v, la, lb, mt, wc, ws):
    qu = [mx_ref.quantize(u[r]) for r in range(N)]
    lay = [pk(wc[r], ws[r]) for r in range(N)]
    mate = [gentries(mt[r]) for r in range(N)]
    kept = [[entries(la[r]), entries(lb[r])] for r in range(N)]
    now = [x[r] for r in range(N)]
    here = np.tile(np.arange(C), (8, 1))
    ll = np.zeros((N, 8, C), np.float32)
    for step in STEP:
        went, sent = [], []
        for r in range(N):
            s = mx_ref.matmul(qu[r], mx_ref.quantize(now[r]))[::16] + np.float32(0.0)
            t = np.take_along_axis(s, mate[r], axis=1)
            crossed = np.where(here < mate[r], s < t, t < s)
            e = np.where(crossed, mate[r], here)
            a = [kept[r][0][e[0]], kept[r][1][e[7]]]
            kept[r] = a[:2]
            for g in range(1, 7):
                k = e[g][a[g]]
                a.append(a[g - 1][k[k]])
            went.append(np.stack(a))
            ll[r] = went[r]
            z = mx_ref.quantize(gcols(now[r], went[r]))
            sent.append(mx_ref.quantize(tile([mx_ref.matmul(pick(lay[r], np.arange(128 * b, 128 * b + 128)), z) * np.float32(0.03125) for b in range(4)])))
        made = []
        for r in range(N):
            far = gcols(decode(sent[r ^ step]).astype(BF), went[r][::-1])
            made.append((now[r].astype(np.float32) + far.astype(np.float32)).astype(BF))
        now = made
    y = np.zeros((N, 128, C), np.float32)
    oc, osc = np.zeros((N, 128, 4 * C), np.uint8), np.zeros((N, 16, C), np.uint8)
    for r in range(N):
        q = mx_ref.quantize(now[r])
        y[r] = mx_ref.matmul(mx_ref.quantize(v[r]), q)
        oc[r], osc[r] = emit(q)
    return {"y": y, "ll": ll, "oc": oc, "osc": osc}

@@ -1,0 +1,434 @@
+from concourse.bass import DstId, RemoteDMATransfer, IndirectOffsetOnAxis
+from concourse.mybir import dt, AluOpType, AxisListType, ActivationFunctionType
+
+C, HALF, ROUNDS, STEP = 320, 160, 3, [4, 1, 2]
+MID = 160
+X4 = "float8_e4m3fn_x4"
+SCRATCH = {
+    "xi": ("sbuf", [128, 4 * C], "bfloat16"), "xp": ("sbuf", [128, 4 * C], "bfloat16"),
+    "zt": ("sbuf", [128, 4 * C], "bfloat16"), "ht": ("sbuf", [128, 4 * C], "bfloat16"),
+    "ut": ("sbuf", [128, 512], "bfloat16"), "vt": ("sbuf", [128, 512], "bfloat16"), "et": ("sbuf", [128, 4096], "bfloat16"),
+    "uq": ("sbuf", [128, 128], X4), "us": ("sbuf", [128, 128], "uint8"), "u2q": ("sbuf", [128, 128], X4), "u2s": ("sbuf", [128, 128], "uint8"),
+    "vq": ("sbuf", [128, 128], X4), "vs": ("sbuf", [128, 128], "uint8"),
+    "wq": ("sbuf", [128, 512], X4), "wp": ("sbuf", [128, 512], "uint8"),
+    "eq": ("sbuf", [128, 1024], X4), "es": ("sbuf", [128, 1024], "uint8"),
+    "xq": ("sbuf", [128, C], X4), "xs": ("sbuf", [128, C], "uint8"),
+    "zq": ("sbuf", [128, C], X4), "zs": ("sbuf", [128, C], "uint8"),
+    "ssb": ("sbuf", [128, C], "float32"), "ssm": ("sbuf", [128, C], "float32"), "dd": ("sbuf", [128, C], "bfloat16"), "xt": ("sbuf", [128, C], "bfloat16"),
+    "dm": ("sbuf", [128, 32], "float32"), "q0": ("sbuf", [128, 32], "float32"), "q1": ("sbuf", [128, 32], "float32"), "q2": ("sbuf", [128, 32], "float32"),
+    "cb": ("sbuf", [128, 32], "float32"), "e32": ("sbuf", [128, 32], "bfloat16"), "xx": ("sbuf", [128, 64], "bfloat16"), "oo": ("sbuf", [128, 64], "bfloat16"),
+    "eo": ("sbuf", [128, 64], "uint16"), "e7": ("sbuf", [128, 32], "uint16"), "do": ("sbuf", [128, 64], "uint16"),
+    "idw": ("sbuf", [128, C], "bfloat16"), "mask": ("sbuf", [128, C], "bfloat16"), "keep": ("sbuf", [128, C], "bfloat16"),
+    "ia": ("sbuf", [128, C], "int32"), "ib": ("sbuf", [128, C], "int32"), "ic": ("sbuf", [128, 512], "int32"), "pi": ("sbuf", [128, 32], "int32"), "pj": ("sbuf", [128, 32], "int32"), "pk": ("sbuf", [128, 32], "int32"), "ii": ("sbuf", [128, 32], "int32"),
+    "pm": ("sbuf", [128, 8], "float32"), "pf": ("sbuf", [128, 32], "float32"),
+    "mti": ("sbuf", [128, 32], "int32"), "mo": ("sbuf", [128, 32], "uint16"), "lab": ("sbuf", [128, 64], "int32"), "lao": ("sbuf", [128, 64], "uint16"), "uo": ("sbuf", [128, 16], "uint16"), "ui": ("sbuf", [128, 16], "int32"),
+    "ee0": ("sbuf", [128, C], "bfloat16"), "ee1": ("sbuf", [128, C], "bfloat16"), "dd0": ("sbuf", [128, C], "bfloat16"), "dd1": ("sbuf", [128, C], "bfloat16"), "e6": ("sbuf", [128, C], "bfloat16"),
+    "vv": ("sbuf", [128, C], "bfloat16"), "mm0": ("sbuf", [128, C], "bfloat16"), "mm1": ("sbuf", [128, C], "bfloat16"), "sc0": ("sbuf", [128, C], "bfloat16"), "sc1": ("sbuf", [128, C], "bfloat16"),
+    "le": ("sbuf", [128, 32], "uint16"), "lo": ("sbuf", [128, 32], "uint16"), "pa": ("sbuf", [128, 32], "uint16"), "pb": ("sbuf", [128, 32], "uint16"), "ls": ("sbuf", [128, 32], "uint16"),
+    "t0": ("sbuf", [128, 32], "float32"), "t1": ("sbuf", [128, 32], "float32"), "t2": ("sbuf", [128, 32], "float32"),
+    "lle": ("sbuf", [128, C], "float32"), "llo": ("sbuf", [128, C], "float32"), "ysb": ("sbuf", [128, C], "float32"),
+    "rlq": ("sbuf", [128, HALF], X4), "rls": ("sbuf", [128, HALF], "uint8"),
+    "ps": ("psum", [128, 4096], "float32"),
+}
+for _k in range(1, 7):
+    SCRATCH["w%d" % _k] = ("sbuf", [128, C], "bfloat16")
+for _k in range(7):
+    SCRATCH["k%d" % _k] = ("sbuf", [128, 32], "uint16")
+for _r in range(ROUNDS):
+    for _n in ("hq", "ld", "ga", "gb"):
+        SCRATCH["%sc%d" % (_n, _r)] = ("sbuf", [128, C], X4)
+        SCRATCH["%ss%d" % (_n, _r)] = ("sbuf", [128, C], "uint8")
+QUEUES = ("V", "S", "P", "G")
+SEMAPHORES = ["qV", "qS", "qP", "qG"] + ["dm%d" % k for k in range(16)] + ["arr%d" % r for r in range(ROUNDS)] + ["sent%d" % r for r in range(ROUNDS)] + ["hopq", "hops", "hopsent", "stored"]
+
+
+def relays(core, dst, T, topo):
+    return [c for c in topo.cores_of(core) if c != core and T.rank_of(c) is None and topo.die(c) == topo.die(core) and topo.may_write(c, dst)][:2]
+
+
+def hand_on(g, core, T, topo):
+    for r, s in enumerate(STEP):
+        for i in range(len(T.cores)):
+            src, dst = T.cores[i], T.cores[i ^ s]
+            if topo.may_write(src, dst):
+                continue
+            rel = relays(src, dst, T, topo)
+            if core not in rel:
+                continue
+            a = HALF * rel.index(core)
+            n_in, m = len(topo.engines(src, core)), topo.mask(core, dst)
+            rid, pid = topo.addr(dst, core)
+            g.wait_ge(T.sem.hopq, n_in)
+            g.remote_dma(T["ldc%d" % r][:, a:a + HALF].bitcast(dt.uint8), T.rlq[:, 0:HALF].bitcast(dt.uint8), T.sem["arr%d" % r], T.sem.hopsent, pid, rid, m)
+            g.wait_ge(T.sem.hops, n_in)
+            g.remote_dma(T["lds%d" % r][:, a:a + HALF], T.rls[:, 0:HALF], T.sem["arr%d" % r], T.sem.hopsent, pid, rid, m)
+            g.wait_ge(T.sem.hopsent, 2 * len(topo.engines(core, dst)))
+
+
+def rank_program(g, core, T, topo):
+    rank = T.rank_of(core)
+    if rank is None:
+        return hand_on(g, core, T, topo)
+    A, AF = AluOpType, ActivationFunctionType
+    eng = {"V": g.vector, "S": g.scalar, "P": g.tensor, "G": g, "Y": g.sync}
+    cnt, known, snap = {}, {q: {} for q in eng}, {}
+    writers, readers = [], []
+
+    def R(name, c0=0, c1=None, step=1, p0=0, p1=128, cast=None):
+        c1 = (C if c1 is None else c1)
+        ap = T[name][p0:p1, c0:c1] if step == 1 else T[name][p0:p1, c0:c1:step]
+        if cast is not None:
+            ap = ap.bitcast(cast)
+        return ((name, p0, p1, c0, c1, step), ap)
+
+    def hit(a, b):
+        return (a[0] == b[0] and a[1] < b[2] and b[1] < a[2] and a[3] < b[4] and b[3] < a[4]
+                and not (a[5] == b[5] and a[5] > 1 and (a[3] - b[3]) % a[5]))
+
+    def inside(a, b):
+        return a[0] == b[0] and b[1] <= a[1] and a[2] <= b[2] and b[3] <= a[3] and a[4] <= b[4] and (b[5] == 1 or (a[5] == b[5] and (a[3] - b[3]) % a[5] == 0))
+
+    def waits(q, W, Rd, own_waw=True):
+        need = {}
+        for r in Rd:
+            for (b, s, n) in writers:
+                if hit(r[0], b):
+                    need[s] = max(need.get(s, 0), n)
+        for w in W:
+            for (b, s, n) in writers + readers:
+                if hit(w[0], b) and (own_waw or s != "q" + q):
+                    need[s] = max(need.get(s, 0), n)
+        k = known[q]
+        need = {s: n for s, n in need.items() if k.get(s, 0) < n}
+        for s in list(need):
+            for s2 in list(need):
+                if s2 != s and s in need and snap.get((s2, need[s2]), {}).get(s, 0) >= need[s]:
+                    del need[s]
+        for s, n in need.items():
+            eng[q].wait_ge(T.sem[s], n)
+            for a, b in snap.get((s, n), {}).items():
+                k[a] = max(k.get(a, 0), b)
+            k[s] = max(k.get(s, 0), n)
+
+    def note(W, Rd, s, n):
+        for w in W:
+            writers[:] = [e for e in writers if not inside(e[0], w[0])]
+            readers[:] = [e for e in readers if not inside(e[0], w[0])]
+            writers.append((w[0], s, n))
+        for r in Rd:
+            readers[:] = [e for e in readers if not (e[1] == s and inside(e[0], r[0]))]
+            readers.append((r[0], s, n))
+
+    def op(q, call, W, Rd, own_waw=True):
+        waits(q, W, Rd, own_waw)
+        s = "q" + q
+        cnt[s] = cnt.get(s, 0) + 1
+        call().then_inc(T.sem[s], 1)
+        snap[(s, cnt[s])] = dict(known[q])
+        note(W, Rd, s, cnt[s])
+
+    nd = [0]
+
+    def dma(q, dst, src, ap=None, s=None):
+        waits(q, [dst], [src] if src is not None else [])
+        s = "dm%d" % nd[0]
+        nd[0] += 1
+        eng[q].dma_start(dst[1], src[1] if ap is None else ap).then_inc(T.sem[s], 16)
+        snap[(s, 16)] = dict(known[q])
+        note([dst], [], s, 16)
+
+    stores = [0]
+
+    def store(q, out, src):
+        waits(q, [], [src])
+        eng[q].dma_start(out, src[1]).then_inc(T.sem.stored, 16)
+        stores[0] += 16
+
+    def tt(o, a, b, f, q="V", off=None):
+        op(q, lambda: eng[q].tensor_tensor(o[1], a[1] if off is None else a[1].indirect(off[1]), b[1], f), [o], [a, b] + ([off] if off else []))
+
+    def ts(o, a, s1, f, s2=None, f2=None, extra=[]):
+        if f2 is None:
+            op("V", lambda: g.vector.tensor_scalar(o[1], a[1], s1, None, f), [o], [a] + extra)
+        else:
+            op("V", lambda: g.vector.tensor_scalar(o[1], a[1], s1, s2, f, f2), [o], [a] + extra)
+
+    def cp(q, o, a, off=None, scale=None, bias=None):
+        src = a[1] if off is None else a[1].indirect(off[1])
+        rd = [a] + ([off] if off else [])
+        if q == "V":
+            op("V", lambda: g.vector.tensor_copy(o[1], src), [o], rd)
+        elif bias is not None:
+            op("S", lambda: g.scalar.activation(o[1], src, AF.Identity, bias=bias), [o], rd)
+        elif scale is not None:
+            op("S", lambda: g.scalar.activation(o[1], src, AF.Copy, scale=scale), [o], rd)
+        else:
+            op("S", lambda: g.scalar.activation(o[1], src, AF.Copy), [o], rd)
+
+    def tr(o, a):
+        op("V", lambda: g.vector.transpose(o[1], a[1]), [o], [a])
+
+    def fill(o, v):
+        op("V", lambda: g.vector.memset(o[1], v), [o], [])
+
+    def iota(o, pat, base, cm, flag=False):
+        if flag:
+            op("G", lambda: g.iota(o[1], pat, base, cm, allow_small_or_imprecise_dtypes=True), [o], [])
+        else:
+            op("G", lambda: g.iota(o[1], pat, base, cm), [o], [])
+
+    def quant(qc, qs, a, b, tile, ta=None):
+        ta = 4 * a if ta is None else ta
+        o, s, i = R(qc, a, b), R(qs, a, b), R(tile, ta, ta + 4 * (b - a))
+        op("V", lambda: g.vector.quantize_mx(o[1], s[1], i[1]), [o, s], [i])
+
+    def mm(bank, n, lq, lsc, la, rq, rsc, ra, start=True, stop=True):
+        o = R("ps", 512 * bank, 512 * bank + n)
+        a, b, c, d = R(lq, la, la + 128), R(lsc, la, la + 128), R(rq, ra, ra + n), R(rsc, ra, ra + n)
+        op("P", lambda: g.tensor.matmul_mx(o[1], a[1], b[1], c[1], d[1], start, stop), [o], [a, b, c, d], own_waw=start)
+
+    def bank(k, n=HALF):
+        return R("ps", 512 * k, 512 * k + n)
+
+    def offs(name, a=0):
+        return R(name, a, a + 20)
+
+    def fold(win, off, k):
+        tt(R("mm%d" % k), R(win), R("mask"), A.mult, off=off)
+
+    def scan(k):
+        o, d0, d1 = R("sc%d" % k), R("keep"), R("mm%d" % k)
+        op("V", lambda: g.vector.tensor_tensor_scan(o[1], d0[1], d1[1], 0.0, A.mult, A.add), [o], [d0, d1])
+
+    def conv(dst, blk, k, src):
+        ts(R(dst, 0, 20, 1, 32 * blk, 32 * blk + 32), R("sc%d" % k, 15, C, 16, 32 * src, 32 * src + 32), float(MID), A.add)
+
+    L = lambda name: ((name + "!", 0, 1, 0, 1, 1), T[name])
+    fill(R("lab", 0, 64), 0)
+    for n in ("k0", "k1", "k2", "k3", "k4", "k5", "k6", "le", "lo", "e7", "pa", "pb"):
+        fill(R(n, 0, 32), 0)
+    fill(R("e32", 0, 32), 0.0)
+    fill(R("e6"), 0.0)
+    dma("Y", R("xi", 0, 640), None, T.x[:, 0:640])
+    dma("S", R("xi", 640, 1280), None, T.x[:, 640:1280])
+    dma("Y", R("ut", 0, 512), None, T.u[:, :])
+    dma("S", R("mti", 0, 20), None, T.mt[:, :])
+    for h in range(2):
+        dma("Y", R("lab", 0, 20, 1, 16 * h, 16 * h + 16), None, T.la[:, :])
+        dma("S", R("lab", 20, 40, 1, 16 * h, 16 * h + 16), None, T.lb[:, :])
+    dma("Y", R("wq", 0, 512, cast=dt.uint8), None, T.wc[:, :])
+    dma("Y", R("wp", 0, 512), None, T.ws[:, :])
+    dma("Y", R("vt", 0, 512), None, T.v[:, :])
+    iota(R("idw"), [[1, C]], -MID, 0, True)
+    iota(R("ui", 0, 8), [[16, 8]], 0, 0)
+    iota(R("pi", 0, 20), [[0, 20]], 0, 1)
+    iota(R("pj", 0, 20), [[32, 10], [0, 2]], -MID, 0)
+    iota(R("pk", 0, 20), [[16, 20]], 0, 0)
+    iota(R("ia"), [[-1, C]], 336, 1)
+    iota(R("ib"), [[1, C]], 0, 0)
+    iota(R("ic", 0, 512), [[1, 512]], 0, -4)
+    cp("V", R("uo", 0, 8), R("ui", 0, 8))
+    ts(R("ii", 0, 20), R("pi", 0, 20), 31, A.bitwise_and)
+    tt(R("cb", 0, 20), R("ii", 0, 20), R("pj", 0, 20), A.add)
+    ts(R("ii", 0, 20), R("pi", 0, 20), 15, A.bitwise_and)
+    tt(R("pf", 0, 20), R("ii", 0, 20), R("pk", 0, 20), A.add)
+    cp("V", R("do", 0, 20), R("pf", 0, 20))
+    cp("V", R("do", 20, 40), R("pf", 0, 20))
+    ts(R("ii", 0, 4), R("pi", 0, 4), 16, A.bitwise_and)
+    ts(R("pm", 0, 4), R("ii", 0, 4), 0.0, A.is_equal)
+    ts(R("pm", 4, 8), R("ii", 0, 4), 0.0, A.is_gt)
+    quant("uq", "us", 0, 128, "ut")
+    op("V", lambda: g.vector.tensor_copy(T.u2q[:, 0:128].bitcast(dt.uint32), T.uq[:, 0:128].bitcast(dt.uint32).indirect(T.uo[:, 0:8])), [R("u2q", 0, 128)], [R("uq", 0, 128), R("uo", 0, 8)])
+    op("V", lambda: g.vector.tensor_copy(T.u2s[:, 0:128], T.us[:, 0:128].indirect(T.uo[:, 0:8])), [R("u2s", 0, 128)], [R("us", 0, 128), R("uo", 0, 8)])
+    m0, m1 = R("pm", 0, 1), R("pm", 4, 5)
+
+    def scores():
+        for h in range(2):
+            quant("xq", "xs", HALF * h, HALF * h + HALF, "xi")
+            mm(4 * h, HALF, "u2q", "u2s", 0, "xq", "xs", HALF * h)
+
+    scores()
+    cp("V", R("mo", 0, 20), R("mti", 0, 20))
+    cp("V", R("lao", 0, 40), R("lab", 0, 40))
+    cp("S", R("w1"), R("idw"), offs("lao"))
+    cp("S", R("w2"), R("idw"), offs("lao", 20))
+    cp("V", R("vv"), R("idw"), offs("mo"))
+    tr(R("xt"), R("vv"))
+    tt(R("dm", 0, 20), R("xt", 0, C, 16), R("cb", 0, 20), A.subtract)
+    ts(R("ia"), R("ia"), 15, A.bitwise_and)
+    ts(R("mask"), R("ia"), 0.0, A.is_equal)
+    ts(R("ib"), R("ib"), 15, A.bitwise_and)
+    ts(R("keep"), R("ib"), 0.0, A.is_gt)
+
+    def send(r, h):
+        dst = T.cores[rank ^ STEP[r]]
+        a = HALF * h
+        ld = ("ldc%d" % r, "lds%d" % r, T.sem["arr%d" % r], T.sem["arr%d" % r], a)
+        to = dst
+        if not topo.may_write(core, dst):
+            to = relays(core, dst, T, topo)[h]
+            ld = ("rlq", "rls", T.sem.hopq, T.sem.hops, 0)
+        rid, pid = topo.addr(to, core)
+        m = topo.mask(core, to)
+        hc, hs = R("hqc%d" % r, a, a + HALF, cast=dt.uint8), R("hqs%d" % r, a, a + HALF)
+        waits("G", [], [hc, hs])
+        g.remote_dma(T[ld[0]][:, ld[4]:ld[4] + HALF].bitcast(dt.uint8), hc[1], ld[2], T.sem["sent%d" % r], pid, rid, m)
+        g.remote_dma(T[ld[1]][:, ld[4]:ld[4] + HALF], hs[1], ld[3], T.sem["sent%d" % r], pid, rid, m)
+        return 2 * len(topo.engines(core, to))
+
+    def arrivals(r):
+        src = T.cores[rank ^ STEP[r]]
+        n = 0
+        for h in range(2):
+            via = src if topo.may_write(src, core) else relays(src, core, T, topo)[h]
+            n += 2 * len(topo.engines(via, core))
+        return n
+
+    sent = []
+    for r in range(ROUNDS):
+        last = r == ROUNDS - 1
+        cp("S", R("ssb", 0, HALF), bank(0))
+        cp("V", R("ssb", HALF, C), bank(4))
+        cp("V", R("ssm", 0, HALF), R("ssb"), R("mo", 0, 10))
+        cp("S", R("ssm", HALF, C), R("ssb"), R("mo", 10, 20))
+        tt(R("dd", 0, HALF), R("ssm", 0, HALF), bank(0), A.subtract)
+        tt(R("dd", HALF, C), R("ssm", HALF, C), bank(4), A.subtract)
+        for t in range(4):
+            cp("S", R("xp", C * t, C * t + C), R("xi", t, 4 * C, 4))
+        tr(R("xt"), R("dd"))
+        tt(R("q0", 0, 20), R("xt", 0, C, 16), R("dm", 0, 20), A.mult)
+        ts(R("q1", 0, 20), R("q0", 0, 20), 0.0, A.is_gt)
+        tt(R("q2", 0, 20), R("q1", 0, 20), R("dm", 0, 20), A.mult)
+        tt(R("e32", 0, 10), R("q2", 0, 20, 2), R("cb", 0, 20, 2), A.add)
+        tt(R("e32", 10, 20), R("q2", 1, 20, 2), R("cb", 0, 20, 2), A.add)
+        tr(R("xx", 16, 48), R("e32", 0, 32))
+        cp("V", R("xx", 0, 16), R("xx", 16, 32))
+        cp("V", R("xx", 48, 64), R("xx", 32, 48))
+        tr(R("oo", 0, 64), R("xx", 0, 64))
+        ts(R("eo", 0, 40, 2), R("oo", 0, 20), float(MID), A.add)
+        ts(R("eo", 1, 40, 2), R("oo", 32, 52), float(MID), A.add)
+        cp("S", R("ee0"), R("idw"), offs("eo"))
+        cp("S", R("ee1"), R("idw"), offs("eo", 20))
+        iota(R("ee0", 0, C, 1, 0, 32), [[1, C]], -MID, 0, True)
+        fold("w1", offs("eo"), 0)
+        cp("V", R("e7", 0, 20, 1, 0, 32), R("eo", 20, 40, 1, 96, 128))
+        scan(0)
+        fold("w2", offs("e7"), 1)
+        conv("k0", 0, 0, 0)
+        conv("k0", 1, 0, 0)
+        scan(1)
+        conv("le", 0, 0, 0)
+        conv("lo", 0, 1, 0)
+        for b in range(3):
+            cp("V", R("do", 0, 40, 1, 32 * b + 32, 32 * b + 64), R("eo", 0, 40, 1, 32 * b, 32 * b + 32))
+        cp("S", R("w1"), R("ee0"), offs("k0"))
+        fold("ee1", offs("lo"), 0)
+        cp("S", R("dd1"), R("ee1"), offs("do", 20))
+        scan(0)
+        conv("k1", 0, 0, 0)
+        conv("k1", 1, 0, 0)
+        cp("S", R("dd0"), R("ee0"), offs("do"))
+        nextwin = {1: "dd1", 2: "ee0", 3: "ee1", 4: "dd0", 5: "e6"}
+        kblock = {1: 1, 2: 1, 3: 0, 4: 0, 5: 0}
+        split = {1: 0, 2: 96, 3: 160, 4: 160, 5: 160, 6: 192}
+        for s in range(1, 7):
+            k, w = "k%d" % s, "w%d" % s
+            n = C - split[s]
+            cp("V", R("vv", 0, n), R(w), R(k, 0, n // 16))
+            if split[s]:
+                cp("S", R("vv", n, C), R(w), R(k, n // 16, 20))
+            if s < 6:
+                cp("S", R("w%d" % (s + 1)), R(nextwin[s]), offs(k))
+            if s == 1:
+                cp("S", R("ee0", 0, C, 1, 0, 32), R("dd0", 0, C, 1, 64, 96))
+            if s == 2:
+                cp("S", R("ee1", 0, C, 1, 0, 32), R("dd1", 0, C, 1, 64, 96))
+            if s == 3:
+                cp("S", R("dd0", 0, C, 1, 0, 32), R("dd0", 0, C, 1, 96, 128))
+                cp("S", R("dd0", 0, C, 1, 32, 64), R("ee0", 0, C, 1, 64, 96))
+            if s == 4:
+                cp("S", R("e6", 0, C, 1, 0, 32), R("ee1", 0, C, 1, 64, 96))
+            fold("vv", offs(k), s % 2)
+            scan(s % 2)
+            if s < 6:
+                kb = kblock[s]
+                conv("k%d" % (s + 1), 0, s % 2, kb)
+                conv("k%d" % (s + 1), 1, s % 2, kb)
+                li = s + 1
+                conv("le" if li % 2 == 0 else "lo", li // 2, s % 2, 1 - kb)
+                if s == 5:
+                    ts(R("t0", 0, 20), R("le", 0, 20), m0[1], A.mult, extra=[m0])
+                    ts(R("t1", 0, 20, 1, 0, 64), R("lo", 0, 20, 1, 0, 64), T.pm[0:64, 4:5], A.mult, extra=[m1])
+                    ts(R("t1", 0, 20, 1, 64, 96), R("lo", 0, 20, 1, 64, 96), T.pm[64:96, 4:5], A.mult, extra=[m1])
+            else:
+                ts(R("t1", 0, 20, 1, 96, 128), R("sc0", 15, C, 16, 0, 32), float(MID), A.add, T.pm[0:32, 4:5], A.mult, extra=[m1])
+                tt(R("t2", 0, 20), R("t0", 0, 20), R("t1", 0, 20), A.add)
+                cp("V", R("ls", 0, 20), R("t2", 0, 20))
+        for h in range(2):
+            for t in range(4):
+                cp("V" if t < 2 else "S", R("zt", 640 * h + t, 640 * h + 640, 4), R("xp", C * t, C * t + C), R("ls", 10 * h, 10 * h + 10))
+            quant("zq", "zs", HALF * h, HALF * h + HALF, "zt")
+            for b in range(4):
+                mm(4 * h + b, HALF, "wq", "wp", 128 * b, "zq", "zs", HALF * h)
+        for b in range(4):
+            cp("S", R("ht", b, 640, 4), bank(b), scale=0.03125)
+        n_sent = 0
+        for h in range(2):
+            if h == 1:
+                for b in range(4):
+                    ts(R("ht", 640 + b, 1280, 4), bank(4 + b), 0.03125, A.mult)
+            quant("hqc%d" % r, "hqs%d" % r, HALF * h, HALF * h + HALF, "ht")
+            n_sent += send(r, h)
+        sent.append(n_sent)
+        conv("lo", 3, 0, 0)
+        for b in range(4):
+            cp("V", R("pa", 0, 20, 1, 32 * b, 32 * b + 32), R("lo", 0, 20, 1, 96 - 32 * b, 128 - 32 * b))
+            cp("V", R("pb", 0, 20, 1, 32 * b, 32 * b + 32), R("le", 0, 20, 1, 96 - 32 * b, 128 - 32 * b))
+        if r == 0:
+            for par in range(2):
+                for b in range(4):
+                    k = 4 * par + b
+                    ts(R("et", 512 * k, 512 * k + 512), R("ic", 0, 512), float(b), A.is_equal, (m0, m1)[par][1], A.mult, extra=[(m0, m1)[par]])
+                    quant("eq", "es", 128 * k, 128 * k + 128, "et")
+            quant("vq", "vs", 0, 128, "vt")
+        if last:
+            cp("S", R("lle"), R("idw"), offs("le"), bias=float(MID))
+            cp("S", R("llo"), R("idw"), offs("lo"), bias=float(MID))
+            for b in range(4):
+                store("Y", T.ll[2 * b:2 * b + 1, :], R("lle", 0, C, 1, 32 * b, 32 * b + 1))
+                store("Y", T.ll[2 * b + 1:2 * b + 2, :], R("llo", 0, C, 1, 32 * b, 32 * b + 1))
+        ldc, lds = R("ldc%d" % r, cast=dt.uint32), R("lds%d" % r)
+        note([ldc, lds], [], "arr%d" % r, arrivals(r))
+        for h in range(2):
+            for n, ls in (("ga", "pa"), ("gb", "pb")):
+                off = R(ls, 10 * h, 10 * h + 10)
+                cp("V", R("%sc%d" % (n, r), HALF * h, HALF * h + HALF, cast=dt.uint32), ldc, off)
+                cp("S", R("%ss%d" % (n, r), HALF * h, HALF * h + HALF), lds, off)
+        for h in range(2):
+            for b in range(4):
+                mm(4 * h + b, HALF, "eq", "es", 128 * b, "gac%d" % r, "gas%d" % r, HALF * h, True, False)
+                mm(4 * h + b, HALF, "eq", "es", 512 + 128 * b, "gbc%d" % r, "gbs%d" % r, HALF * h, False, True)
+        for h in range(2):
+            for b in range(4):
+                x = R("xi", 640 * h + b, 640 * h + 640, 4)
+                tt(x, bank(4 * h + b), x, A.add)
+            quant("xq", "xs", HALF * h, HALF * h + HALF, "xi")
+            if last:
+                mm(4 * h, HALF, "vq", "vs", 0, "xq", "xs", HALF * h)
+            else:
+                mm(4 * h, HALF, "u2q", "u2s", 0, "xq", "xs", HALF * h)
+    for h in range(2):
+        a = HALF * h
+        cp("S" if h == 0 else "V", R("ysb", a, a + HALF), bank(4 * h))
+        store("Y", T.oc[:, 4 * a:4 * a + 4 * HALF], R("xq", a, a + HALF, cast=dt.uint8))
+        for k in range(4):
+            store("S" if k % 2 else "Y", T.osc[4 * k:4 * k + 4, a:a + HALF], R("xs", a, a + HALF, 1, 32 * k, 32 * k + 4))
+        store("Y", T.y[:, a:a + HALF], R("ysb", a, a + HALF))
+    for r in range(ROUNDS):
+        g.wait_ge(T.sem["sent%d" % r], sent[r])
+    for q in QUEUES:
+        if cnt.get("q" + q, 0):
+            g.wait_ge(T.sem["q" + q], cnt["q" + q])
+    for k in range(nd[0]):
+        g.wait_ge(T.sem["dm%d" % k], 16)
+    g.wait_ge(T.sem.stored, stores[0])

@@ -1,49 +1,59 @@
 from concourse.bass import DstId, RemoteDMATransfer, IndirectOffsetOnAxis
 from concourse.mybir import dt, AluOpType, AxisListType, ActivationFunctionType
 
-C, HALF, ROUNDS, STEP = 320, 160, 3, [4, 1, 2]
+C, ROUNDS, STEP = 320, 3, [4, 1, 2]
+CUT = [0, 160, 320]
+CX = [0, 192, 320]
+QUART = 80
 MID = 160
+NS, WW = 21, 336
+SLOT = [1, 7, 2, 0, 3, 5, 4, 6]
+ID, EB, DD, EA = 0, WW, 2 * WW, 3 * WW
+VV = [4 * WW] + [4 * WW + 352 + WW * s for s in range(7)]
 X4 = "float8_e4m3fn_x4"
 SCRATCH = {
     "xi": ("sbuf", [128, 4 * C], "bfloat16"), "xp": ("sbuf", [128, 4 * C], "bfloat16"),
     "zt": ("sbuf", [128, 4 * C], "bfloat16"), "ht": ("sbuf", [128, 4 * C], "bfloat16"),
-    "ut": ("sbuf", [128, 512], "bfloat16"), "vt": ("sbuf", [128, 512], "bfloat16"), "et": ("sbuf", [128, 4096], "bfloat16"),
+    "ut": ("sbuf", [128, 512], "bfloat16"), "vt": ("sbuf", [128, 512], "bfloat16"),
+    "icb": ("sbuf", [128, 520], "bfloat16"), "et": ("sbuf", [128, 4 * 520], "bfloat16"),
     "uq": ("sbuf", [128, 128], X4), "us": ("sbuf", [128, 128], "uint8"), "u2q": ("sbuf", [128, 128], X4), "u2s": ("sbuf", [128, 128], "uint8"),
     "vq": ("sbuf", [128, 128], X4), "vs": ("sbuf", [128, 128], "uint8"),
     "wq": ("sbuf", [128, 512], X4), "wp": ("sbuf", [128, 512], "uint8"),
     "eq": ("sbuf", [128, 1024], X4), "es": ("sbuf", [128, 1024], "uint8"),
     "xq": ("sbuf", [128, C], X4), "xs": ("sbuf", [128, C], "uint8"),
     "zq": ("sbuf", [128, C], X4), "zs": ("sbuf", [128, C], "uint8"),
-    "ssb": ("sbuf", [128, C], "float32"), "ssm": ("sbuf", [128, C], "float32"), "dd": ("sbuf", [128, C], "bfloat16"), "xt": ("sbuf", [128, C], "bfloat16"),
-    "dm": ("sbuf", [128, 32], "float32"), "q0": ("sbuf", [128, 32], "float32"), "q1": ("sbuf", [128, 32], "float32"), "q2": ("sbuf", [128, 32], "float32"),
-    "cb": ("sbuf", [128, 32], "float32"), "e32": ("sbuf", [128, 32], "bfloat16"), "xx": ("sbuf", [128, 64], "bfloat16"), "oo": ("sbuf", [128, 64], "bfloat16"),
-    "eo": ("sbuf", [128, 64], "uint16"), "e7": ("sbuf", [128, 32], "uint16"), "do": ("sbuf", [128, 64], "uint16"),
-    "idw": ("sbuf", [128, C], "bfloat16"), "mask": ("sbuf", [128, C], "bfloat16"), "keep": ("sbuf", [128, C], "bfloat16"),
-    "ia": ("sbuf", [128, C], "int32"), "ib": ("sbuf", [128, C], "int32"), "ic": ("sbuf", [128, 512], "int32"), "pi": ("sbuf", [128, 32], "int32"), "pj": ("sbuf", [128, 32], "int32"), "pk": ("sbuf", [128, 32], "int32"), "ii": ("sbuf", [128, 32], "int32"),
-    "pm": ("sbuf", [128, 8], "float32"), "pf": ("sbuf", [128, 32], "float32"),
-    "mti": ("sbuf", [128, 32], "int32"), "mo": ("sbuf", [128, 32], "uint16"), "lab": ("sbuf", [128, 64], "int32"), "lao": ("sbuf", [128, 64], "uint16"), "uo": ("sbuf", [128, 16], "uint16"), "ui": ("sbuf", [128, 16], "int32"),
-    "ee0": ("sbuf", [128, C], "bfloat16"), "ee1": ("sbuf", [128, C], "bfloat16"), "dd0": ("sbuf", [128, C], "bfloat16"), "dd1": ("sbuf", [128, C], "bfloat16"), "e6": ("sbuf", [128, C], "bfloat16"),
-    "vv": ("sbuf", [128, C], "bfloat16"), "mm0": ("sbuf", [128, C], "bfloat16"), "mm1": ("sbuf", [128, C], "bfloat16"), "sc0": ("sbuf", [128, C], "bfloat16"), "sc1": ("sbuf", [128, C], "bfloat16"),
-    "le": ("sbuf", [128, 32], "uint16"), "lo": ("sbuf", [128, 32], "uint16"), "pa": ("sbuf", [128, 32], "uint16"), "pb": ("sbuf", [128, 32], "uint16"), "ls": ("sbuf", [128, 32], "uint16"),
-    "t0": ("sbuf", [128, 32], "float32"), "t1": ("sbuf", [128, 32], "float32"), "t2": ("sbuf", [128, 32], "float32"),
-    "lle": ("sbuf", [128, C], "float32"), "llo": ("sbuf", [128, C], "float32"), "ysb": ("sbuf", [128, C], "float32"),
-    "rlq": ("sbuf", [128, HALF], X4), "rls": ("sbuf", [128, HALF], "uint8"),
+    "ssb": ("sbuf", [128, C], "float32"), "ssm": ("sbuf", [128, C], "float32"),
+    "df": ("sbuf", [128, 352], "bfloat16"), "ta": ("sbuf", [128, C], "bfloat16"), "tb": ("sbuf", [128, 352], "bfloat16"),
+    "d0": ("sbuf", [128, 88], "float32"), "d1": ("sbuf", [128, 88], "float32"), "sc": ("sbuf", [128, 88], "float32"),
+    "ct": ("sbuf", [128, 48], "float32"), "lo": ("sbuf", [128, 48], "float32"), "hi": ("sbuf", [128, 48], "float32"), "thr": ("sbuf", [128, 48], "float32"),
+    "mtt": ("sbuf", [128, 48], "int32"), "lab": ("sbuf", [128, 24], "int32"), "pi": ("sbuf", [128, 8], "int32"), "pm": ("sbuf", [128, 8], "float32"),
+    "mo": ("sbuf", [128, 24], "uint16"), "lh": ("sbuf", [128, 48], "uint16"), "uo": ("sbuf", [128, 8], "uint16"),
+    "ea": ("sbuf", [128, 24], "uint16"), "eb": ("sbuf", [128, 24], "uint16"), "ec": ("sbuf", [128, 24], "uint16"), "ed": ("sbuf", [128, 24], "uint16"),
+    "kk": ("sbuf", [128, 24 * 7], "uint16"), "ls": ("sbuf", [128, 24], "uint16"), "pa": ("sbuf", [128, 24], "uint16"), "pb": ("sbuf", [128, 24], "uint16"),
+    "idn": ("sbuf", [128, WW], "bfloat16"), "wb": ("sbuf", [128, VV[7]], "bfloat16"), "uu": ("sbuf", [128, 352], "bfloat16"),
+    "aw": ("sbuf", [128, WW], "bfloat16"), "glo": ("sbuf", [128, 352], "bfloat16"), "ghi": ("sbuf", [128, 352], "bfloat16"),
+    "tlo": ("sbuf", [128, 352], "bfloat16"), "thi": ("sbuf", [128, 352], "bfloat16"),
+    "idf": ("sbuf", [128, C], "float32"), "llw": ("sbuf", [128, C], "float32"), "ysb": ("sbuf", [128, C], "float32"),
+    "rlq": ("sbuf", [128, 2 * QUART], X4), "rls": ("sbuf", [128, 2 * QUART], "uint8"),
     "ps": ("psum", [128, 4096], "float32"),
 }
-for _k in range(1, 7):
-    SCRATCH["w%d" % _k] = ("sbuf", [128, C], "bfloat16")
 for _k in range(7):
-    SCRATCH["k%d" % _k] = ("sbuf", [128, 32], "uint16")
+    SCRATCH["t%d" % _k] = ("sbuf", [128, 352], "bfloat16")
 for _r in range(ROUNDS):
     for _n in ("hq", "ld", "ga", "gb"):
         SCRATCH["%sc%d" % (_n, _r)] = ("sbuf", [128, C], X4)
         SCRATCH["%ss%d" % (_n, _r)] = ("sbuf", [128, C], "uint8")
 QUEUES = ("V", "S", "P", "G")
-SEMAPHORES = ["qV", "qS", "qP", "qG"] + ["dm%d" % k for k in range(16)] + ["arr%d" % r for r in range(ROUNDS)] + ["sent%d" % r for r in range(ROUNDS)] + ["hopq", "hops", "hopsent", "stored"]
+SEMAPHORES = (["qV", "qS", "qP", "qG"] + ["dm%d" % k for k in range(8)] + ["arr%d" % r for r in range(ROUNDS)] + ["sent%d" % r for r in range(ROUNDS)]
+              + ["hop0", "hop1", "hop2", "hopsent", "stored"])
 
 
 def relays(core, dst, T, topo):
     return [c for c in topo.cores_of(core) if c != core and T.rank_of(c) is None and topo.die(c) == topo.die(core) and topo.may_write(c, dst)][:2]
+
+
+def half_mask(core, to, k, topo):
+    return sum(1 << e for e in topo.engines(core, to)[k::2])
 
 
 def hand_on(g, core, T, topo):
@@ -55,14 +65,16 @@ def hand_on(g, core, T, topo):
             rel = relays(src, dst, T, topo)
             if core not in rel:
                 continue
-            a = HALF * rel.index(core)
-            n_in, m = len(topo.engines(src, core)), topo.mask(core, dst)
+            k = rel.index(core)
+            n_in, m = len(topo.engines(src, core)) // 2, topo.mask(core, dst)
             rid, pid = topo.addr(dst, core)
-            g.wait_ge(T.sem.hopq, n_in)
-            g.remote_dma(T["ldc%d" % r][:, a:a + HALF].bitcast(dt.uint8), T.rlq[:, 0:HALF].bitcast(dt.uint8), T.sem["arr%d" % r], T.sem.hopsent, pid, rid, m)
-            g.wait_ge(T.sem.hops, n_in)
-            g.remote_dma(T["lds%d" % r][:, a:a + HALF], T.rls[:, 0:HALF], T.sem["arr%d" % r], T.sem.hopsent, pid, rid, m)
-            g.wait_ge(T.sem.hopsent, 2 * len(topo.engines(core, dst)))
+            for h in range(2):
+                a = CUT[h] + QUART * k
+                g.wait_ge(T.sem["hop%d" % h], n_in)
+                g.remote_dma(T["ldc%d" % r][:, a:a + QUART].bitcast(dt.uint8), T.rlq[:, QUART * h:QUART * h + QUART].bitcast(dt.uint8), T.sem["arr%d" % r], T.sem.hopsent, pid, rid, m)
+            g.wait_ge(T.sem.hop2, n_in)
+            g.remote_dma(T["lds%d" % r][:, CUT[k]:CUT[k + 1]], T.rls[:, 0:2 * QUART], T.sem["arr%d" % r], T.sem.hopsent, pid, rid, m)
+            g.wait_ge(T.sem.hopsent, 3 * len(topo.engines(core, dst)))
 
 
 def rank_program(g, core, T, topo):
@@ -127,15 +139,15 @@ def rank_program(g, core, T, topo):
         snap[(s, cnt[s])] = dict(known[q])
         note(W, Rd, s, cnt[s])
 
-    nd = [0]
+    loaded = []
 
-    def dma(q, dst, src, ap=None, s=None):
-        waits(q, [dst], [src] if src is not None else [])
-        s = "dm%d" % nd[0]
-        nd[0] += 1
-        eng[q].dma_start(dst[1], src[1] if ap is None else ap).then_inc(T.sem[s], 16)
-        snap[(s, 16)] = dict(known[q])
-        note([dst], [], s, 16)
+    def load(items):
+        s = "dm%d" % len(loaded)
+        for q, dst, src in items:
+            waits(q, [dst], [])
+            eng[q].dma_start(dst[1], src).then_inc(T.sem[s], 16)
+        loaded.append(16 * len(items))
+        note([dst for q, dst, src in items], [], s, loaded[-1])
 
     stores = [0]
 
@@ -144,22 +156,22 @@ def rank_program(g, core, T, topo):
         eng[q].dma_start(out, src[1]).then_inc(T.sem.stored, 16)
         stores[0] += 16
 
-    def tt(o, a, b, f, q="V", off=None):
-        op(q, lambda: eng[q].tensor_tensor(o[1], a[1] if off is None else a[1].indirect(off[1]), b[1], f), [o], [a, b] + ([off] if off else []))
+    def tt(o, a, b, f, off=None):
+        op("V", lambda: g.vector.tensor_tensor(o[1], a[1] if off is None else a[1].indirect(off[1]), b[1], f), [o], [a, b] + ([off] if off else []))
 
-    def ts(o, a, s1, f, s2=None, f2=None, extra=[]):
+    def ts(o, a, s1, f, s2=None, f2=None):
+        cols = [s for s in (s1, s2) if isinstance(s, tuple)]
+        v1, v2 = [s[1] if isinstance(s, tuple) else s for s in (s1, s2)]
         if f2 is None:
-            op("V", lambda: g.vector.tensor_scalar(o[1], a[1], s1, None, f), [o], [a] + extra)
+            op("V", lambda: g.vector.tensor_scalar(o[1], a[1], v1, None, f), [o], [a] + cols)
         else:
-            op("V", lambda: g.vector.tensor_scalar(o[1], a[1], s1, s2, f, f2), [o], [a] + extra)
+            op("V", lambda: g.vector.tensor_scalar(o[1], a[1], v1, v2, f, f2), [o], [a] + cols)
 
-    def cp(q, o, a, off=None, scale=None, bias=None):
+    def cp(q, o, a, off=None, scale=None):
         src = a[1] if off is None else a[1].indirect(off[1])
         rd = [a] + ([off] if off else [])
         if q == "V":
             op("V", lambda: g.vector.tensor_copy(o[1], src), [o], rd)
-        elif bias is not None:
-            op("S", lambda: g.scalar.activation(o[1], src, AF.Identity, bias=bias), [o], rd)
         elif scale is not None:
             op("S", lambda: g.scalar.activation(o[1], src, AF.Copy, scale=scale), [o], rd)
         else:
@@ -171,264 +183,289 @@ def rank_program(g, core, T, topo):
     def fill(o, v):
         op("V", lambda: g.vector.memset(o[1], v), [o], [])
 
-    def iota(o, pat, base, cm, flag=False):
-        if flag:
-            op("G", lambda: g.iota(o[1], pat, base, cm, allow_small_or_imprecise_dtypes=True), [o], [])
-        else:
+    def iota(o, pat, base, cm, whole=False):
+        if whole:
             op("G", lambda: g.iota(o[1], pat, base, cm), [o], [])
+        else:
+            op("G", lambda: g.iota(o[1], pat, base, cm, allow_small_or_imprecise_dtypes=True), [o], [])
 
     def quant(qc, qs, a, b, tile, ta=None):
         ta = 4 * a if ta is None else ta
         o, s, i = R(qc, a, b), R(qs, a, b), R(tile, ta, ta + 4 * (b - a))
         op("V", lambda: g.vector.quantize_mx(o[1], s[1], i[1]), [o, s], [i])
 
-    def mm(bank, n, lq, lsc, la, rq, rsc, ra, start=True, stop=True):
-        o = R("ps", 512 * bank, 512 * bank + n)
-        a, b, c, d = R(lq, la, la + 128), R(lsc, la, la + 128), R(rq, ra, ra + n), R(rsc, ra, ra + n)
+    def bank(k, cut=CX):
+        return R("ps", 512 * k, 512 * k + cut[k // 4 + 1] - cut[k // 4])
+
+    def mm(k, lq, lsc, la, rq, rsc, start=True, stop=True, cut=CX):
+        o, r0, r1 = bank(k, cut), cut[k // 4], cut[k // 4 + 1]
+        a, b, c, d = R(lq, la, la + 128), R(lsc, la, la + 128), R(rq, r0, r1), R(rsc, r0, r1)
         op("P", lambda: g.tensor.matmul_mx(o[1], a[1], b[1], c[1], d[1], start, stop), [o], [a, b, c, d], own_waw=start)
 
-    def bank(k, n=HALF):
-        return R("ps", 512 * k, 512 * k + n)
+    def shift(b, n=1):
+        return R("pm", 0, 1, 1, 32 * b, 32 * (b + n))
 
-    def offs(name, a=0):
-        return R(name, a, a + 20)
+    def gather(q, out, at, win, w0, w1, off, o0=0):
+        for e, a, b in {"V": [("V", 0, NS)], "S": [("S", 0, NS)], "VS": [("S", 0, 10), ("V", 10, NS)]}[q]:
+            cp(e, R(out, at + 16 * a, at + 16 * b), R(win, w0, w1), R(off, o0 + a, o0 + b))
 
-    def fold(win, off, k):
-        tt(R("mm%d" % k), R(win), R("mask"), A.mult, off=off)
+    def from_scan(dst, to, src, side, n=1, at=0):
+        ts(R(dst, at, at + NS, 1, 32 * to, 32 * (to + n)), R("sc", 2 * NS * side + 1, 2 * NS * side + 2 * NS, 2, 32 * src, 32 * (src + n)), shift(src, n), A.add)
 
-    def scan(k):
-        o, d0, d1 = R("sc%d" % k), R("keep"), R("mm%d" % k)
-        op("V", lambda: g.vector.tensor_tensor_scan(o[1], d0[1], d1[1], 0.0, A.mult, A.add), [o], [d0, d1])
+    def from_turn(s, to, src, base):
+        ts(R("kk", 24 * (s + 1), 24 * (s + 1) + NS, 1, 32 * to, 32 * to + 32), R("t%d" % s, 0, WW, 16, 32 * src, 32 * src + 32), float(MID + base), A.add, shift(src), A.add)
 
-    def conv(dst, blk, k, src):
-        ts(R(dst, 0, 20, 1, 32 * blk, 32 * blk + 32), R("sc%d" % k, 15, C, 16, 32 * src, 32 * src + 32), float(MID), A.add)
+    HELD = {0: 1, 1: 0, 2: 1, 3: 2, 4: 3, 5: 0, 6: 3, 7: 0}
 
-    L = lambda name: ((name + "!", 0, 1, 0, 1, 1), T[name])
-    fill(R("lab", 0, 64), 0)
-    for n in ("k0", "k1", "k2", "k3", "k4", "k5", "k6", "le", "lo", "e7", "pa", "pb"):
-        fill(R(n, 0, 32), 0)
-    fill(R("e32", 0, 32), 0.0)
-    fill(R("e6"), 0.0)
-    dma("Y", R("xi", 0, 640), None, T.x[:, 0:640])
-    dma("S", R("xi", 640, 1280), None, T.x[:, 640:1280])
-    dma("Y", R("ut", 0, 512), None, T.u[:, :])
-    dma("S", R("mti", 0, 20), None, T.mt[:, :])
+    def plain(dst, to, li, first):
+        n, k, src = (16, 1, HELD[li]) if first else (32, 0, HELD[li])
+        o = R(dst, 0, 20, 1, 32 * to, 32 * to + n)
+        if li < 2:
+            cp("V", o, R("sc", 2 * NS + 2 * k + 1, 2 * NS + 2 * k + 40, 2, 32 * src, 32 * src + n))
+        else:
+            ts(o, R("t%d" % min(li, 6), 16 * k, 16 * k + C, 16, 32 * src, 32 * src + n), float(MID), A.add)
+
+    def order_tables():
+        return [lambda: tr(R("tlo", 0, 352, 1, 0, 64), R("glo", 0, 352, 1, 0, 64)), lambda: tr(R("thi", 0, 352, 1, 0, 64), R("ghi", 0, 352, 1, 0, 64)),
+                lambda: ts(R("d1", 2 * NS + 1, 4 * NS, 2, 0, 64), R("tlo", 0, WW, 16, 0, 64), float(MID), A.add),
+                lambda: tt(R("d0", 2 * NS + 1, 4 * NS, 2, 0, 64), R("thi", 0, WW, 16, 0, 64), R("tlo", 0, WW, 16, 0, 64), A.subtract)]
+
+    fill(R("mtt", 0, 48), 0)
+    fill(R("lab", 0, 24), 0)
+    load([("Y", R("ut", 0, 512), T.u[:, :])])
+    load([("YS"[k], R("lab", 1 - k, 21 - k, 1, 32 * b + 16 * k, 32 * b + 16 * k + 16), (T.lb, T.la)[b][:, :]) for b in range(2) for k in range(2)])
+    load([("YS"[k], R("mtt", NS * side + 1 - k, NS * side + 21 - k, 1, 32 * b + 16 * k, 32 * b + 16 * k + 16), T.mt[16 * SLOT[2 * b + side]:16 * SLOT[2 * b + side] + 16, :])
+          for b in range(4) for side in range(2) for k in range(2)])
     for h in range(2):
-        dma("Y", R("lab", 0, 20, 1, 16 * h, 16 * h + 16), None, T.la[:, :])
-        dma("S", R("lab", 20, 40, 1, 16 * h, 16 * h + 16), None, T.lb[:, :])
-    dma("Y", R("wq", 0, 512, cast=dt.uint8), None, T.wc[:, :])
-    dma("Y", R("wp", 0, 512), None, T.ws[:, :])
-    dma("Y", R("vt", 0, 512), None, T.v[:, :])
-    iota(R("idw"), [[1, C]], -MID, 0, True)
-    iota(R("ui", 0, 8), [[16, 8]], 0, 0)
-    iota(R("pi", 0, 20), [[0, 20]], 0, 1)
-    iota(R("pj", 0, 20), [[32, 10], [0, 2]], -MID, 0)
-    iota(R("pk", 0, 20), [[16, 20]], 0, 0)
-    iota(R("ia"), [[-1, C]], 336, 1)
-    iota(R("ib"), [[1, C]], 0, 0)
-    iota(R("ic", 0, 512), [[1, 512]], 0, -4)
-    cp("V", R("uo", 0, 8), R("ui", 0, 8))
-    ts(R("ii", 0, 20), R("pi", 0, 20), 31, A.bitwise_and)
-    tt(R("cb", 0, 20), R("ii", 0, 20), R("pj", 0, 20), A.add)
-    ts(R("ii", 0, 20), R("pi", 0, 20), 15, A.bitwise_and)
-    tt(R("pf", 0, 20), R("ii", 0, 20), R("pk", 0, 20), A.add)
-    cp("V", R("do", 0, 20), R("pf", 0, 20))
-    cp("V", R("do", 20, 40), R("pf", 0, 20))
-    ts(R("ii", 0, 4), R("pi", 0, 4), 16, A.bitwise_and)
-    ts(R("pm", 0, 4), R("ii", 0, 4), 0.0, A.is_equal)
-    ts(R("pm", 4, 8), R("ii", 0, 4), 0.0, A.is_gt)
+        load([("YS"[h], R("xi", 4 * CX[h], 4 * CX[h + 1]), T.x[:, 4 * CX[h]:4 * CX[h + 1]])])
+    load([("Y", R("wq", 0, 512, cast=dt.uint8), T.wc[:, :]), ("Y", R("wp", 0, 512), T.ws[:, :])])
+    load([("Y", R("vt", 0, 512), T.v[:, :])])
+    iota(R("pi", 0, 2), [[0, 2]], 0, 1, True)
+    iota(R("idn", 0, WW), [[1, WW]], -MID, 0)
+    iota(R("ct", 0, 2 * NS), [[0, 2], [16, NS]], -16, 1)
+    iota(R("icb", 0, 516), [[1, 516]], 0, -4)
+    iota(R("idf"), [[1, C]], 0, 0)
+    for k in range(8):
+        fill(R("uo", k, k + 1), 16 * SLOT[k])
+    ts(R("pi", 2, 4), R("pi", 0, 2), 16, A.bitwise_and)
+    ts(R("pi", 4, 6), R("pi", 0, 2), 96, A.bitwise_and)
+    fill(R("kk", 0, 24 * 7), 0)
+    fill(R("d0", 0, 88), 0.0)
+    cp("V", R("pm", 6, 8), R("pi", 4, 6))
+    ts(R("pm", 0, 2), R("pi", 2, 4), 0.0, A.is_equal, 16.0, A.mult)
+    ts(R("pm", 2, 4), R("pi", 2, 4), 0.0, A.is_equal)
+    ts(R("pm", 4, 6), R("pi", 2, 4), 0.0, A.is_gt)
+    for n, a in (("df", 0), ("df", WW), ("uu", WW), ("glo", WW), ("ghi", WW), ("wb", VV[0] + WW)):
+        fill(R(n, a, a + 16), 0.0)
+    ts(R("wb", ID, ID + WW), R("idn", 0, WW), shift(0, 4), A.subtract)
+    ts(R("ct", 0, 2 * NS), R("ct", 0, 2 * NS), R("pm", 6, 7), A.subtract)
+    ts(R("ed", 0, NS, 1, 0, 32), R("ct", 0, NS, 1, 0, 32), shift(0), A.add)
+    ts(R("eb", 0, NS), R("lab", 0, NS), shift(0, 4), A.add)
+    gather("S", "aw", 0, "wb", ID, ID + WW, "eb")
     quant("uq", "us", 0, 128, "ut")
-    op("V", lambda: g.vector.tensor_copy(T.u2q[:, 0:128].bitcast(dt.uint32), T.uq[:, 0:128].bitcast(dt.uint32).indirect(T.uo[:, 0:8])), [R("u2q", 0, 128)], [R("uq", 0, 128), R("uo", 0, 8)])
-    op("V", lambda: g.vector.tensor_copy(T.u2s[:, 0:128], T.us[:, 0:128].indirect(T.uo[:, 0:8])), [R("u2s", 0, 128)], [R("us", 0, 128), R("uo", 0, 8)])
-    m0, m1 = R("pm", 0, 1), R("pm", 4, 5)
+    tt(R("lo", 0, 2 * NS), R("mtt", 0, 2 * NS), R("ct", 0, 2 * NS), A.min)
+    tt(R("hi", 0, 2 * NS), R("mtt", 0, 2 * NS), R("ct", 0, 2 * NS), A.max)
+    cp("V", R("mo", 0, 20), R("mtt", NS, NS + 20))
+    ts(R("lh", 0, NS), R("lo", NS, 2 * NS), shift(0, 4), A.add)
+    ts(R("lh", 22, 22 + NS), R("hi", NS, 2 * NS), shift(0, 4), A.add)
+    for b in range(4):
+        cp("V", R("mo", 0, 20, 1, 32 * b, 32 * b + 16), R("mtt", 1, 21, 1, 32 * b, 32 * b + 16))
+    gather("S", "ghi", 0, "aw", 0, WW, "lh", 22)
+    gather("V", "glo", 0, "aw", 0, WW, "lh")
+    cp("V", R("u2q", 0, 128, cast=dt.uint32), R("uq", 0, 128, cast=dt.uint32), R("uo", 0, 8))
+    cp("S", R("u2s", 0, 128), R("us", 0, 128), R("uo", 0, 8))
+    tt(R("thr", 0, 2 * NS), R("mtt", 0, 2 * NS), R("ct", 0, 2 * NS), A.is_lt)
+    cp("V", R("d1", 1, 4 * NS, 2), R("lo", 0, 2 * NS))
+    tt(R("d0", 1, 4 * NS, 2), R("hi", 0, 2 * NS), R("lo", 0, 2 * NS), A.subtract)
+    ts(R("thr", 0, 2 * NS), R("thr", 0, 2 * NS), -2.0 ** -99, A.mult)
+    for f in order_tables():
+        f()
+    for h in range(2):
+        quant("xq", "xs", CX[h], CX[h + 1], "xi")
+        mm(4 * h, "u2q", "u2s", 0, "xq", "xs")
 
-    def scores():
-        for h in range(2):
-            quant("xq", "xs", HALF * h, HALF * h + HALF, "xi")
-            mm(4 * h, HALF, "u2q", "u2s", 0, "xq", "xs", HALF * h)
+    def first_scores():
+        cp("S", R("ssb", 0, CX[1]), bank(0))
+        cp("S", R("ssm", 0, CX[1]), bank(0))
 
-    scores()
-    cp("V", R("mo", 0, 20), R("mti", 0, 20))
-    cp("V", R("lao", 0, 40), R("lab", 0, 40))
-    cp("S", R("w1"), R("idw"), offs("lao"))
-    cp("S", R("w2"), R("idw"), offs("lao", 20))
-    cp("V", R("vv"), R("idw"), offs("mo"))
-    tr(R("xt"), R("vv"))
-    tt(R("dm", 0, 20), R("xt", 0, C, 16), R("cb", 0, 20), A.subtract)
-    ts(R("ia"), R("ia"), 15, A.bitwise_and)
-    ts(R("mask"), R("ia"), 0.0, A.is_equal)
-    ts(R("ib"), R("ib"), 15, A.bitwise_and)
-    ts(R("keep"), R("ib"), 0.0, A.is_gt)
+    first_scores()
 
     def send(r, h):
         dst = T.cores[rank ^ STEP[r]]
-        a = HALF * h
-        ld = ("ldc%d" % r, "lds%d" % r, T.sem["arr%d" % r], T.sem["arr%d" % r], a)
-        to = dst
-        if not topo.may_write(core, dst):
-            to = relays(core, dst, T, topo)[h]
-            ld = ("rlq", "rls", T.sem.hopq, T.sem.hops, 0)
-        rid, pid = topo.addr(to, core)
-        m = topo.mask(core, to)
-        hc, hs = R("hqc%d" % r, a, a + HALF, cast=dt.uint8), R("hqs%d" % r, a, a + HALF)
-        waits("G", [], [hc, hs])
-        g.remote_dma(T[ld[0]][:, ld[4]:ld[4] + HALF].bitcast(dt.uint8), hc[1], ld[2], T.sem["sent%d" % r], pid, rid, m)
-        g.remote_dma(T[ld[1]][:, ld[4]:ld[4] + HALF], hs[1], ld[3], T.sem["sent%d" % r], pid, rid, m)
-        return 2 * len(topo.engines(core, to))
+        a, b = CUT[h], CUT[h + 1]
+        hc, sent, arr = "hqc%d" % r, T.sem["sent%d" % r], T.sem["arr%d" % r]
+        waits("G", [], [R(hc, a, b)])
+        if topo.may_write(core, dst):
+            rid, pid = topo.addr(dst, core)
+            g.remote_dma(T["ldc%d" % r][:, a:b].bitcast(dt.uint8), T[hc][:, a:b].bitcast(dt.uint8), arr, sent, pid, rid, topo.mask(core, dst))
+            if h == 1:
+                g.remote_dma(T["lds%d" % r][:, 0:C], T["hqs%d" % r][:, 0:C], arr, sent, pid, rid, topo.mask(core, dst))
+            return (1 + h) * len(topo.engines(core, dst))
+        rel = relays(core, dst, T, topo)
+        ids = [[DstId(rid=topo.addr(to, core)[0], pnc=topo.addr(to, core)[1])] for to in rel]
+        g.remote_dma_fused([RemoteDMATransfer(dst_ids=ids[k], dma_engine_mask=half_mask(core, to, k, topo), remote_sem=T.sem["hop%d" % h],
+                                              src=T[hc][:, a + QUART * k:a + QUART * k + QUART].bitcast(dt.uint8), dst=T.rlq[:, QUART * h:QUART * h + QUART].bitcast(dt.uint8))
+                            for k, to in enumerate(rel)], local_sem=sent)
+        if h == 1:
+            g.remote_dma_fused([RemoteDMATransfer(dst_ids=ids[k], dma_engine_mask=half_mask(core, to, k, topo), remote_sem=T.sem.hop2,
+                                                  src=T["hqs%d" % r][:, CUT[k]:CUT[k + 1]], dst=T.rls[:, 0:2 * QUART]) for k, to in enumerate(rel)], local_sem=sent)
+        return (1 + h) * len(topo.engines(core, rel[0]))
 
     def arrivals(r):
         src = T.cores[rank ^ STEP[r]]
-        n = 0
-        for h in range(2):
-            via = src if topo.may_write(src, core) else relays(src, core, T, topo)[h]
-            n += 2 * len(topo.engines(via, core))
-        return n
+        if topo.may_write(src, core):
+            return 3 * len(topo.engines(src, core))
+        return sum(3 * len(topo.engines(via, core)) for via in relays(src, core, T, topo))
 
+    KB = {1: 1, 2: 2, 3: 1, 4: 2, 5: 3, 6: 0}
+    WB = {1: 2, 2: 1, 3: 2, 4: 3, 5: 0, 6: 3}
+    W0 = {1: EA, 2: DD, 3: DD, 4: DD, 5: EB, 6: ID}
+    SHARE = 208
     sent = []
     for r in range(ROUNDS):
         last = r == ROUNDS - 1
-        cp("S", R("ssb", 0, HALF), bank(0))
-        cp("V", R("ssb", HALF, C), bank(4))
-        cp("V", R("ssm", 0, HALF), R("ssb"), R("mo", 0, 10))
-        cp("S", R("ssm", HALF, C), R("ssb"), R("mo", 10, 20))
-        tt(R("dd", 0, HALF), R("ssm", 0, HALF), bank(0), A.subtract)
-        tt(R("dd", HALF, C), R("ssm", HALF, C), bank(4), A.subtract)
+        cp("V", R("ssb", CX[1], C), bank(4))
+        cp("S", R("ssm", CX[1], C), R("ssb"), R("mo", CX[1] // 16, 20))
+        tt(R("df", 16, 16 + CX[1]), R("ssb"), R("ssm", 0, CX[1]), A.subtract, off=R("mo", 0, CX[1] // 16))
+        tt(R("df", 16 + CX[1], 16 + C), R("ssm", CX[1], C), bank(4), A.subtract)
         for t in range(4):
             cp("S", R("xp", C * t, C * t + C), R("xi", t, 4 * C, 4))
-        tr(R("xt"), R("dd"))
-        tt(R("q0", 0, 20), R("xt", 0, C, 16), R("dm", 0, 20), A.mult)
-        ts(R("q1", 0, 20), R("q0", 0, 20), 0.0, A.is_gt)
-        tt(R("q2", 0, 20), R("q1", 0, 20), R("dm", 0, 20), A.mult)
-        tt(R("e32", 0, 10), R("q2", 0, 20, 2), R("cb", 0, 20, 2), A.add)
-        tt(R("e32", 10, 20), R("q2", 1, 20, 2), R("cb", 0, 20, 2), A.add)
-        tr(R("xx", 16, 48), R("e32", 0, 32))
-        cp("V", R("xx", 0, 16), R("xx", 16, 32))
-        cp("V", R("xx", 48, 64), R("xx", 32, 48))
-        tr(R("oo", 0, 64), R("xx", 0, 64))
-        ts(R("eo", 0, 40, 2), R("oo", 0, 20), float(MID), A.add)
-        ts(R("eo", 1, 40, 2), R("oo", 32, 52), float(MID), A.add)
-        cp("S", R("ee0"), R("idw"), offs("eo"))
-        cp("S", R("ee1"), R("idw"), offs("eo", 20))
-        iota(R("ee0", 0, C, 1, 0, 32), [[1, C]], -MID, 0, True)
-        fold("w1", offs("eo"), 0)
-        cp("V", R("e7", 0, 20, 1, 0, 32), R("eo", 20, 40, 1, 96, 128))
-        scan(0)
-        fold("w2", offs("e7"), 1)
-        conv("k0", 0, 0, 0)
-        conv("k0", 1, 0, 0)
-        scan(1)
-        conv("le", 0, 0, 0)
-        conv("lo", 0, 1, 0)
-        for b in range(3):
-            cp("V", R("do", 0, 40, 1, 32 * b + 32, 32 * b + 64), R("eo", 0, 40, 1, 32 * b, 32 * b + 32))
-        cp("S", R("w1"), R("ee0"), offs("k0"))
-        fold("ee1", offs("lo"), 0)
-        cp("S", R("dd1"), R("ee1"), offs("do", 20))
-        scan(0)
-        conv("k1", 0, 0, 0)
-        conv("k1", 1, 0, 0)
-        cp("S", R("dd0"), R("ee0"), offs("do"))
-        nextwin = {1: "dd1", 2: "ee0", 3: "ee1", 4: "dd0", 5: "e6"}
-        kblock = {1: 1, 2: 1, 3: 0, 4: 0, 5: 0}
-        split = {1: 0, 2: 96, 3: 160, 4: 160, 5: 160, 6: 192}
+        tr(R("ta"), R("df", 16, 16 + C))
+        tr(R("tb", 0, 352), R("df", 0, 352))
+        for side in range(2):
+            tt(R("d1", 2 * (NS * side + 1), 2 * NS * (side + 1), 4), R("ta", 16 * side, C, 32), R("thr", NS * side + 1, NS * (side + 1), 2), A.is_gt)
+        for side in range(2):
+            tt(R("d1", 2 * NS * side, 2 * NS * (side + 1), 4), R("tb", 16 * side, 352, 32), R("thr", NS * side, NS * (side + 1), 2), A.is_gt)
+        o, d0, d1 = R("sc", 0, 4 * NS), R("d0", 0, 4 * NS), R("d1", 0, 4 * NS)
+        op("V", lambda: g.vector.tensor_tensor_scan(o[1], d0[1], d1[1], 0.0, A.mult, A.add), [o], [d0, d1])
+        from_scan("ea", 0, 0, 0, 4)
+        from_scan("eb", 0, 0, 1, 4)
+        gather("VS", "wb", EA, "wb", ID, ID + WW, "ea")
+        from_scan("ec", 2, 2, 1, 2)
+        from_scan("ec", 0, 2, 1)
+        gather("VS", "wb", VV[0], "wb", EA, EA + WW, "eb")
+        from_scan("ec", 1, 3, 0)
+        from_scan("kk", 2, 0, 1, at=24)
+        gather("S", "wb", EB, "wb", ID, ID + WW, "ec")
+        tr(R("t0", 0, 352, 1, 0, 32), R("wb", VV[0], VV[0] + 352, 1, 0, 32))
+        from_scan("ed", 2, 2, 0, 2)
+        from_turn(0, KB[1], 0, VV[0] - W0[1])
+        from_scan("ed", 1, 1, 0)
+        def lays(li):
+            b, p = (7 - li) // 2, ("pb", "pa")[li % 2]
+            return [lambda: plain(p, b, li, False), lambda: plain(p, b, li, True)]
+        spare = {1: [lambda: plain("ls", 0, 1, False)] + lays(1)[:1] + [lambda: plain("ls", 0, 0, True)] + lays(1)[1:],
+                 2: lays(0) + [None, None], 3: lays(2) + [None, None],
+                 4: [lambda: plain("ls", 1, 3, False)] + lays(3)[:1] + [lambda: plain("ls", 1, 2, True)] + lays(3)[1:],
+                 5: lays(4) + ([None, None] if last else order_tables()[:1] + [None]),
+                 6: [lambda: plain("ls", 2, 5, False)] + ([None] if last else order_tables()[1:2]) + [lambda: plain("ls", 2, 4, True)]}
+        behind = {1: lambda: gather("S", "wb", DD, "wb", EB, EB + WW, "ed")}
+        if not last:
+            behind[2] = lambda: gather("S", "aw", 0, "wb", ID, ID + WW, "eb")
+            behind[3] = lambda: gather("S", "glo", 0, "aw", 0, WW, "lh")
+            behind[4] = lambda: gather("S", "ghi", 0, "aw", 0, WW, "lh", 22)
         for s in range(1, 7):
-            k, w = "k%d" % s, "w%d" % s
-            n = C - split[s]
-            cp("V", R("vv", 0, n), R(w), R(k, 0, n // 16))
-            if split[s]:
-                cp("S", R("vv", n, C), R(w), R(k, n // 16, 20))
+            sp = [f or (lambda: None) for f in spare[s]]
+            gather("VS", "wb", VV[s], "wb", W0[s], VV[s - 1] + WW, "kk", 24 * s)
+            sp[0]()
+            gather("VS", "uu", 0, "wb", W0[s] + VV[s] - VV[s - 1], VV[s] + WW, "kk", 24 * s)
+            if s in behind:
+                behind[s]()
+            sp[1]()
+            tr(R("t%d" % s, 0, 352), R("uu", 0, 352))
+            sp[2]()
             if s < 6:
-                cp("S", R("w%d" % (s + 1)), R(nextwin[s]), offs(k))
-            if s == 1:
-                cp("S", R("ee0", 0, C, 1, 0, 32), R("dd0", 0, C, 1, 64, 96))
-            if s == 2:
-                cp("S", R("ee1", 0, C, 1, 0, 32), R("dd1", 0, C, 1, 64, 96))
-            if s == 3:
-                cp("S", R("dd0", 0, C, 1, 0, 32), R("dd0", 0, C, 1, 96, 128))
-                cp("S", R("dd0", 0, C, 1, 32, 64), R("ee0", 0, C, 1, 64, 96))
-            if s == 4:
-                cp("S", R("e6", 0, C, 1, 0, 32), R("ee1", 0, C, 1, 64, 96))
-            fold("vv", offs(k), s % 2)
-            scan(s % 2)
-            if s < 6:
-                kb = kblock[s]
-                conv("k%d" % (s + 1), 0, s % 2, kb)
-                conv("k%d" % (s + 1), 1, s % 2, kb)
-                li = s + 1
-                conv("le" if li % 2 == 0 else "lo", li // 2, s % 2, 1 - kb)
-                if s == 5:
-                    ts(R("t0", 0, 20), R("le", 0, 20), m0[1], A.mult, extra=[m0])
-                    ts(R("t1", 0, 20, 1, 0, 64), R("lo", 0, 20, 1, 0, 64), T.pm[0:64, 4:5], A.mult, extra=[m1])
-                    ts(R("t1", 0, 20, 1, 64, 96), R("lo", 0, 20, 1, 64, 96), T.pm[64:96, 4:5], A.mult, extra=[m1])
-            else:
-                ts(R("t1", 0, 20, 1, 96, 128), R("sc0", 15, C, 16, 0, 32), float(MID), A.add, T.pm[0:32, 4:5], A.mult, extra=[m1])
-                tt(R("t2", 0, 20), R("t0", 0, 20), R("t1", 0, 20), A.add)
-                cp("V", R("ls", 0, 20), R("t2", 0, 20))
-        for h in range(2):
-            for t in range(4):
-                cp("V" if t < 2 else "S", R("zt", 640 * h + t, 640 * h + 640, 4), R("xp", C * t, C * t + C), R("ls", 10 * h, 10 * h + 10))
-            quant("zq", "zs", HALF * h, HALF * h + HALF, "zt")
+                from_turn(s, KB[s + 1], KB[s], VV[s] - W0[s + 1])
+                from_turn(s, WB[s + 1], KB[s], 0)
+                sp[3]()
+        plain("ls", 3, 7, False)
+        lays(5)[0]()
+        plain("ls", 3, 6, True)
+        lays(5)[1]()
+        def zed(q, h, t):
+            cp(q, R("zt", 4 * CUT[h] + t, 4 * CUT[h + 1], 4), R("xp", C * t, C * t + C), R("ls", CUT[h] // 16, CUT[h + 1] // 16))
+
+        def layer(h):
+            quant("zq", "zs", CUT[h], CUT[h + 1], "zt")
             for b in range(4):
-                mm(4 * h + b, HALF, "wq", "wp", 128 * b, "zq", "zs", HALF * h)
-        for b in range(4):
-            cp("S", R("ht", b, 640, 4), bank(b), scale=0.03125)
-        n_sent = 0
-        for h in range(2):
-            if h == 1:
-                for b in range(4):
-                    ts(R("ht", 640 + b, 1280, 4), bank(4 + b), 0.03125, A.mult)
-            quant("hqc%d" % r, "hqs%d" % r, HALF * h, HALF * h + HALF, "ht")
-            n_sent += send(r, h)
-        sent.append(n_sent)
-        conv("lo", 3, 0, 0)
-        for b in range(4):
-            cp("V", R("pa", 0, 20, 1, 32 * b, 32 * b + 32), R("lo", 0, 20, 1, 96 - 32 * b, 128 - 32 * b))
-            cp("V", R("pb", 0, 20, 1, 32 * b, 32 * b + 32), R("le", 0, 20, 1, 96 - 32 * b, 128 - 32 * b))
+                mm(4 * h + b, "wq", "wp", 128 * b, "zq", "zs", cut=CUT)
+
+        def out(q, h, b):
+            o = R("ht", 4 * CUT[h] + b, 4 * CUT[h + 1], 4)
+            if q == "S":
+                cp("S", o, bank(4 * h + b, CUT), scale=0.03125)
+            else:
+                ts(o, bank(4 * h + b, CUT), 0.03125, A.mult)
+
+        def leave(h):
+            quant("hqc%d" % r, "hqs%d" % r, CUT[h], CUT[h + 1], "ht")
+            return send(r, h)
+
+        for q, h, t in (("V", 0, 0), ("S", 0, 2), ("V", 0, 1), ("S", 0, 3), ("S", 1, 2), ("V", 1, 0)):
+            zed(q, h, t)
+        layer(0)
+        zed("S", 1, 3)
+        zed("V", 1, 1)
+        out("S", 0, 0)
+        out("S", 0, 1)
+        layer(1)
+        out("V", 0, 3)
+        out("S", 0, 2)
+        n_sent = leave(0)
+        for q, b in (("S", 0), ("S", 1), ("V", 2), ("V", 3)):
+            out(q, 1, b)
+        sent.append(n_sent + leave(1))
+        for f in lays(7)[:1] + lays(6)[:1] + lays(7)[1:] + lays(6)[1:] + ([] if last else order_tables()[2:]):
+            f()
         if r == 0:
+            for par in range(2):
+                for odd in range(2):
+                    k = 2 * par + odd
+                    ts(R("et", 520 * k, 520 * k + 516), R("icb", 0, 516), float(2 + odd), A.is_equal, R("pm", 2 + 2 * par, 3 + 2 * par), A.mult)
             for par in range(2):
                 for b in range(4):
                     k = 4 * par + b
-                    ts(R("et", 512 * k, 512 * k + 512), R("ic", 0, 512), float(b), A.is_equal, (m0, m1)[par][1], A.mult, extra=[(m0, m1)[par]])
-                    quant("eq", "es", 128 * k, 128 * k + 128, "et")
+                    quant("eq", "es", 128 * k, 128 * k + 128, "et", 520 * (2 * par + b % 2) + 2 - 2 * (b // 2))
+        if r == 1:
             quant("vq", "vs", 0, 128, "vt")
         if last:
-            cp("S", R("lle"), R("idw"), offs("le"), bias=float(MID))
-            cp("S", R("llo"), R("idw"), offs("lo"), bias=float(MID))
-            for b in range(4):
-                store("Y", T.ll[2 * b:2 * b + 1, :], R("lle", 0, C, 1, 32 * b, 32 * b + 1))
-                store("Y", T.ll[2 * b + 1:2 * b + 2, :], R("llo", 0, C, 1, 32 * b, 32 * b + 1))
+            cp("S", R("llw"), R("idf"), R("ls", 0, 20))
+            for k in range(8):
+                store("Y", T.ll[k:k + 1, :], R("llw", 0, C, 1, 16 * k, 16 * k + 1))
         ldc, lds = R("ldc%d" % r, cast=dt.uint32), R("lds%d" % r)
         note([ldc, lds], [], "arr%d" % r, arrivals(r))
         for h in range(2):
             for n, ls in (("ga", "pa"), ("gb", "pb")):
-                off = R(ls, 10 * h, 10 * h + 10)
-                cp("V", R("%sc%d" % (n, r), HALF * h, HALF * h + HALF, cast=dt.uint32), ldc, off)
-                cp("S", R("%ss%d" % (n, r), HALF * h, HALF * h + HALF), lds, off)
+                off = R(ls, CX[h] // 16, CX[h + 1] // 16)
+                cp("V", R("%sc%d" % (n, r), CX[h], CX[h + 1], cast=dt.uint32), ldc, off)
+                cp("S", R("%ss%d" % (n, r), CX[h], CX[h + 1]), lds, off)
         for h in range(2):
             for b in range(4):
-                mm(4 * h + b, HALF, "eq", "es", 128 * b, "gac%d" % r, "gas%d" % r, HALF * h, True, False)
-                mm(4 * h + b, HALF, "eq", "es", 512 + 128 * b, "gbc%d" % r, "gbs%d" % r, HALF * h, False, True)
+                mm(4 * h + b, "eq", "es", 128 * b, "gac%d" % r, "gas%d" % r, True, False)
+                mm(4 * h + b, "eq", "es", 512 + 128 * b, "gbc%d" % r, "gbs%d" % r, False, True)
         for h in range(2):
             for b in range(4):
-                x = R("xi", 640 * h + b, 640 * h + 640, 4)
+                x = R("xi", 4 * CX[h] + b, 4 * CX[h + 1], 4)
                 tt(x, bank(4 * h + b), x, A.add)
-            quant("xq", "xs", HALF * h, HALF * h + HALF, "xi")
+            quant("xq", "xs", CX[h], CX[h + 1], "xi")
             if last:
-                mm(4 * h, HALF, "vq", "vs", 0, "xq", "xs", HALF * h)
+                mm(4 * h, "vq", "vs", 0, "xq", "xs")
+                a, b = CX[h], CX[h + 1]
+                store("Y", T.oc[:, 4 * a:4 * b], R("xq", a, b, cast=dt.uint8))
+                cp("S" if h == 0 else "V", R("ysb", a, b), bank(4 * h))
+                if h == 1:
+                    for k in range(4):
+                        store("S", T.osc[4 * k:4 * k + 4, :], R("xs", 0, C, 1, 32 * k, 32 * k + 4))
+                store("Y", T.y[:, a:b], R("ysb", a, b))
             else:
-                mm(4 * h, HALF, "u2q", "u2s", 0, "xq", "xs", HALF * h)
-    for h in range(2):
-        a = HALF * h
-        cp("S" if h == 0 else "V", R("ysb", a, a + HALF), bank(4 * h))
-        store("Y", T.oc[:, 4 * a:4 * a + 4 * HALF], R("xq", a, a + HALF, cast=dt.uint8))
-        for k in range(4):
-            store("S" if k % 2 else "Y", T.osc[4 * k:4 * k + 4, a:a + HALF], R("xs", a, a + HALF, 1, 32 * k, 32 * k + 4))
-        store("Y", T.y[:, a:a + HALF], R("ysb", a, a + HALF))
+                mm(4 * h, "u2q", "u2s", 0, "xq", "xs")
+                if h == 0:
+                    first_scores()
     for r in range(ROUNDS):
         g.wait_ge(T.sem["sent%d" % r], sent[r])
     for q in QUEUES:
         if cnt.get("q" + q, 0):
             g.wait_ge(T.sem["q" + q], cnt["q" + q])
-    for k in range(nd[0]):
-        g.wait_ge(T.sem["dm%d" % k], 16)
+    for k, n in enumerate(loaded):
+        g.wait_ge(T.sem["dm%d" % k], n)
     g.wait_ge(T.sem.stored, stores[0])

@@ -10,6 +10,14 @@ NS, WW = 21, 336
 SLOT = [1, 7, 2, 0, 3, 5, 4, 6]
 ID, EB, DD, EA = 0, WW, 2 * WW, 3 * WW
 VV = [4 * WW] + [4 * WW + 352 + WW * s for s in range(7)]
+RUN = 10
+FIRST = [("S", 0, 6), ("V", 6, 10), ("S", 10, 14), ("V", 14, NS)]
+SECOND = [("S", 0, 6), ("V", 6, 10), ("S", 10, 14), ("V", 14, NS)]
+LAST = [("S", 0, 6), ("V", 6, 12), ("S", 12, 16), ("V", 16, NS)]
+UNPACK = [[(0, 0), (0, 1), (0, 2), (1, 0), (1, 1), (0, 3), (1, 2), (1, 3)], [(k % 2, k // 2) for k in range(8)]]
+ADDS = [8, 6]
+OWN = True
+LOADS = "ulm01"
 X4 = "float8_e4m3fn_x4"
 SCRATCH = {
     "xi": ("sbuf", [128, 4 * C], "bfloat16"), "xp": ("sbuf", [128, 4 * C], "bfloat16"),
@@ -132,7 +140,7 @@ def rank_program(g, core, T, topo):
             readers.append((r[0], s, n))
 
     def op(q, call, W, Rd, own_waw=True):
-        waits(q, W, Rd, own_waw)
+        waits(q, W, Rd, own_waw and OWN)
         s = "q" + q
         cnt[s] = cnt.get(s, 0) + 1
         call().then_inc(T.sem[s], 1)
@@ -205,25 +213,29 @@ def rank_program(g, core, T, topo):
     def shift(b, n=1):
         return R("pm", 0, 1, 1, 32 * b, 32 * (b + n))
 
-    def gather(q, out, at, win, w0, w1, off, o0=0):
-        for e, a, b in {"V": [("V", 0, NS)], "S": [("S", 0, NS)], "VS": [("S", 0, 10), ("V", 10, NS)]}[q]:
+    def gather(shares, out, at, win, w0, w1, off, o0=0):
+        for e, a, b in shares:
             cp(e, R(out, at + 16 * a, at + 16 * b), R(win, w0, w1), R(off, o0 + a, o0 + b))
 
     def from_scan(dst, to, src, side, n=1, at=0):
         ts(R(dst, at, at + NS, 1, 32 * to, 32 * (to + n)), R("sc", 2 * NS * side + 1, 2 * NS * side + 2 * NS, 2, 32 * src, 32 * (src + n)), shift(src, n), A.add)
 
-    def from_turn(s, to, src, base):
-        ts(R("kk", 24 * (s + 1), 24 * (s + 1) + NS, 1, 32 * to, 32 * to + 32), R("t%d" % s, 0, WW, 16, 32 * src, 32 * src + 32), float(MID + base), A.add, shift(src), A.add)
+    def turn(s, src, at, cut, p1=128):
+        for a, b in ((0, cut), (cut, NS + 1)):
+            tr(R("t%d" % s, 16 * a, 16 * b, 1, 0, p1), R(src, at + 16 * a, at + 16 * b, 1, 0, p1))
+
+    def from_turn(s, to, src, base, a, b):
+        ts(R("kk", 24 * (s + 1) + a, 24 * (s + 1) + b, 1, 32 * to, 32 * to + 32), R("t%d" % s, 16 * a, 16 * b, 16, 32 * src, 32 * src + 32), float(MID + base), A.add, shift(src), A.add)
 
     HELD = {0: 1, 1: 0, 2: 1, 3: 2, 4: 3, 5: 0, 6: 3, 7: 0}
 
-    def plain(dst, to, li, first):
+    def plain(dst, to, li, first, a=0, b=20):
         n, k, src = (16, 1, HELD[li]) if first else (32, 0, HELD[li])
-        o = R(dst, 0, 20, 1, 32 * to, 32 * to + n)
+        o = R(dst, a, b, 1, 32 * to, 32 * to + n)
         if li < 2:
-            cp("V", o, R("sc", 2 * NS + 2 * k + 1, 2 * NS + 2 * k + 40, 2, 32 * src, 32 * src + n))
+            cp("V", o, R("sc", 2 * NS + 2 * (k + a) + 1, 2 * NS + 2 * (k + b), 2, 32 * src, 32 * src + n))
         else:
-            ts(o, R("t%d" % min(li, 6), 16 * k, 16 * k + C, 16, 32 * src, 32 * src + n), float(MID), A.add)
+            ts(o, R("t%d" % min(li, 6), 16 * (k + a), 16 * (k + b), 16, 32 * src, 32 * src + n), float(MID), A.add)
 
     def order_tables():
         return [lambda: tr(R("tlo", 0, 352, 1, 0, 64), R("glo", 0, 352, 1, 0, 64)), lambda: tr(R("thi", 0, 352, 1, 0, 64), R("ghi", 0, 352, 1, 0, 64)),
@@ -232,12 +244,17 @@ def rank_program(g, core, T, topo):
 
     fill(R("mtt", 0, 48), 0)
     fill(R("lab", 0, 24), 0)
-    load([("Y", R("ut", 0, 512), T.u[:, :])])
-    load([("YS"[k], R("lab", 1 - k, 21 - k, 1, 32 * b + 16 * k, 32 * b + 16 * k + 16), (T.lb, T.la)[b][:, :]) for b in range(2) for k in range(2)])
-    load([("YS"[k], R("mtt", NS * side + 1 - k, NS * side + 21 - k, 1, 32 * b + 16 * k, 32 * b + 16 * k + 16), T.mt[16 * SLOT[2 * b + side]:16 * SLOT[2 * b + side] + 16, :])
-          for b in range(4) for side in range(2) for k in range(2)])
-    for h in range(2):
-        load([("YS"[h], R("xi", 4 * CX[h], 4 * CX[h + 1]), T.x[:, 4 * CX[h]:4 * CX[h + 1]])])
+    for what in LOADS:
+        if what == "u":
+            load([("S", R("ut", 0, 512), T.u[:, :])])
+        if what == "l":
+            load([("YS"[k], R("lab", 1 - k, 21 - k, 1, 32 * b + 16 * k, 32 * b + 16 * k + 16), (T.lb, T.la)[b][:, :]) for b in range(2) for k in range(2)])
+        if what == "m":
+            load([("YS"[k], R("mtt", NS * side + 1 - k, NS * side + 21 - k, 1, 32 * b + 16 * k, 32 * b + 16 * k + 16), T.mt[16 * SLOT[2 * b + side]:16 * SLOT[2 * b + side] + 16, :])
+                  for b in range(4) for side in range(2) for k in range(2)])
+        if what in "01":
+            h = int(what)
+            load([("YS"[h], R("xi", 4 * CX[h], 4 * CX[h + 1]), T.x[:, 4 * CX[h]:4 * CX[h + 1]])])
     load([("Y", R("wq", 0, 512, cast=dt.uint8), T.wc[:, :]), ("Y", R("wp", 0, 512), T.ws[:, :])])
     load([("Y", R("vt", 0, 512), T.v[:, :])])
     iota(R("pi", 0, 2), [[0, 2]], 0, 1, True)
@@ -260,26 +277,22 @@ def rank_program(g, core, T, topo):
     ts(R("wb", ID, ID + WW), R("idn", 0, WW), shift(0, 4), A.subtract)
     ts(R("ct", 0, 2 * NS), R("ct", 0, 2 * NS), R("pm", 6, 7), A.subtract)
     ts(R("ed", 0, NS, 1, 0, 32), R("ct", 0, NS, 1, 0, 32), shift(0), A.add)
+    ALL_S = [("S", 0, NS)]
     ts(R("eb", 0, NS), R("lab", 0, NS), shift(0, 4), A.add)
-    gather("S", "aw", 0, "wb", ID, ID + WW, "eb")
+    gather(ALL_S, "aw", 0, "wb", ID, ID + WW, "eb")
     quant("uq", "us", 0, 128, "ut")
     tt(R("lo", 0, 2 * NS), R("mtt", 0, 2 * NS), R("ct", 0, 2 * NS), A.min)
     tt(R("hi", 0, 2 * NS), R("mtt", 0, 2 * NS), R("ct", 0, 2 * NS), A.max)
-    cp("V", R("mo", 0, 20), R("mtt", NS, NS + 20))
+    cp("V", R("u2q", 0, 128, cast=dt.uint32), R("uq", 0, 128, cast=dt.uint32), R("uo", 0, 8))
     ts(R("lh", 0, NS), R("lo", NS, 2 * NS), shift(0, 4), A.add)
     ts(R("lh", 22, 22 + NS), R("hi", NS, 2 * NS), shift(0, 4), A.add)
-    for b in range(4):
-        cp("V", R("mo", 0, 20, 1, 32 * b, 32 * b + 16), R("mtt", 1, 21, 1, 32 * b, 32 * b + 16))
-    gather("S", "ghi", 0, "aw", 0, WW, "lh", 22)
-    gather("V", "glo", 0, "aw", 0, WW, "lh")
-    cp("V", R("u2q", 0, 128, cast=dt.uint32), R("uq", 0, 128, cast=dt.uint32), R("uo", 0, 8))
     cp("S", R("u2s", 0, 128), R("us", 0, 128), R("uo", 0, 8))
+    gather(ALL_S, "glo", 0, "aw", 0, WW, "lh")
+    gather(ALL_S, "ghi", 0, "aw", 0, WW, "lh", 22)
+    cp("V", R("mo", 0, 20), R("mtt", NS, NS + 20))
     tt(R("thr", 0, 2 * NS), R("mtt", 0, 2 * NS), R("ct", 0, 2 * NS), A.is_lt)
     cp("V", R("d1", 1, 4 * NS, 2), R("lo", 0, 2 * NS))
     tt(R("d0", 1, 4 * NS, 2), R("hi", 0, 2 * NS), R("lo", 0, 2 * NS), A.subtract)
-    ts(R("thr", 0, 2 * NS), R("thr", 0, 2 * NS), -2.0 ** -99, A.mult)
-    for f in order_tables():
-        f()
     for h in range(2):
         quant("xq", "xs", CX[h], CX[h + 1], "xi")
         mm(4 * h, "u2q", "u2s", 0, "xq", "xs")
@@ -289,6 +302,10 @@ def rank_program(g, core, T, topo):
         cp("S", R("ssm", 0, CX[1]), bank(0))
 
     first_scores()
+    for b in range(4):
+        cp("V", R("mo", 0, 20, 1, 32 * b, 32 * b + 16), R("mtt", 1, 21, 1, 32 * b, 32 * b + 16))
+    ts(R("thr", 0, 2 * NS), R("thr", 0, 2 * NS), -2.0 ** -99, A.mult)
+    order_tables()[0]()
 
     def send(r, h):
         dst = T.cores[rank ^ STEP[r]]
@@ -325,63 +342,70 @@ def rank_program(g, core, T, topo):
     for r in range(ROUNDS):
         last = r == ROUNDS - 1
         cp("V", R("ssb", CX[1], C), bank(4))
+        if r == 0:
+            order_tables()[1]()
         cp("S", R("ssm", CX[1], C), R("ssb"), R("mo", CX[1] // 16, 20))
         tt(R("df", 16, 16 + CX[1]), R("ssb"), R("ssm", 0, CX[1]), A.subtract, off=R("mo", 0, CX[1] // 16))
+        if r == 0:
+            for f in order_tables()[2:]:
+                f()
         tt(R("df", 16 + CX[1], 16 + C), R("ssm", CX[1], C), bank(4), A.subtract)
         for t in range(4):
             cp("S", R("xp", C * t, C * t + C), R("xi", t, 4 * C, 4))
-        tr(R("ta"), R("df", 16, 16 + C))
-        tr(R("tb", 0, 352), R("df", 0, 352))
+        for a, b in ((0, CX[1]), (CX[1], 352)):
+            tr(R("ta", a, min(b, C)), R("df", 16 + a, 16 + min(b, C)))
+            tr(R("tb", a, b), R("df", a, b))
         for side in range(2):
             tt(R("d1", 2 * (NS * side + 1), 2 * NS * (side + 1), 4), R("ta", 16 * side, C, 32), R("thr", NS * side + 1, NS * (side + 1), 2), A.is_gt)
-        for side in range(2):
             tt(R("d1", 2 * NS * side, 2 * NS * (side + 1), 4), R("tb", 16 * side, 352, 32), R("thr", NS * side, NS * (side + 1), 2), A.is_gt)
-        o, d0, d1 = R("sc", 0, 4 * NS), R("d0", 0, 4 * NS), R("d1", 0, 4 * NS)
-        op("V", lambda: g.vector.tensor_tensor_scan(o[1], d0[1], d1[1], 0.0, A.mult, A.add), [o], [d0, d1])
+        for side in range(2):
+            o, d0, d1 = [R(n, 2 * NS * side, 2 * NS * (side + 1)) for n in ("sc", "d0", "d1")]
+            op("V", lambda: g.vector.tensor_tensor_scan(o[1], d0[1], d1[1], 0.0, A.mult, A.add), [o], [d0, d1])
         from_scan("ea", 0, 0, 0, 4)
         from_scan("eb", 0, 0, 1, 4)
-        gather("VS", "wb", EA, "wb", ID, ID + WW, "ea")
+        gather([("S", 0, 10), ("V", 10, NS)], "wb", EA, "wb", ID, ID + WW, "ea")
         from_scan("ec", 2, 2, 1, 2)
         from_scan("ec", 0, 2, 1)
-        gather("VS", "wb", VV[0], "wb", EA, EA + WW, "eb")
         from_scan("ec", 1, 3, 0)
+        gather(SECOND, "wb", VV[0], "wb", EA, EA + WW, "eb")
+        gather(ALL_S, "wb", EB, "wb", ID, ID + WW, "ec")
         from_scan("kk", 2, 0, 1, at=24)
-        gather("S", "wb", EB, "wb", ID, ID + WW, "ec")
-        tr(R("t0", 0, 352, 1, 0, 32), R("wb", VV[0], VV[0] + 352, 1, 0, 32))
+        turn(0, "wb", VV[0], RUN, 32)
         from_scan("ed", 2, 2, 0, 2)
-        from_turn(0, KB[1], 0, VV[0] - W0[1])
+        from_turn(0, KB[1], 0, VV[0] - W0[1], 0, RUN)
         from_scan("ed", 1, 1, 0)
-        def lays(li):
-            b, p = (7 - li) // 2, ("pb", "pa")[li % 2]
-            return [lambda: plain(p, b, li, False), lambda: plain(p, b, li, True)]
-        spare = {1: [lambda: plain("ls", 0, 1, False)] + lays(1)[:1] + [lambda: plain("ls", 0, 0, True)] + lays(1)[1:],
-                 2: lays(0) + [None, None], 3: lays(2) + [None, None],
-                 4: [lambda: plain("ls", 1, 3, False)] + lays(3)[:1] + [lambda: plain("ls", 1, 2, True)] + lays(3)[1:],
-                 5: lays(4) + ([None, None] if last else order_tables()[:1] + [None]),
-                 6: [lambda: plain("ls", 2, 5, False)] + ([None] if last else order_tables()[1:2]) + [lambda: plain("ls", 2, 4, True)]}
-        behind = {1: lambda: gather("S", "wb", DD, "wb", EB, EB + WW, "ed")}
+        from_turn(0, KB[1], 0, VV[0] - W0[1], RUN, NS)
+        def own(b, first):
+            return lambda: plain("ls", b, 2 * b + 1 - first, first)
+
+        def lay(li, first):
+            return lambda: plain(("pb", "pa")[li % 2], (7 - li) // 2, li, first)
+        spare = {1: [own(0, 0), lay(1, 0), lay(0, 0)], 2: [own(0, 1), lay(1, 1), lay(0, 1)], 3: [lay(2, 0)], 4: [own(1, 0), lay(3, 0), lay(2, 1)],
+                 5: [own(1, 1), lay(3, 1), lay(4, 0)], 6: [own(2, 0), lay(5, 0), lay(4, 1)]}
+        behind = {1: lambda: gather(ALL_S, "wb", DD, "wb", EB, EB + WW, "ed")}
         if not last:
-            behind[2] = lambda: gather("S", "aw", 0, "wb", ID, ID + WW, "eb")
-            behind[3] = lambda: gather("S", "glo", 0, "aw", 0, WW, "lh")
-            behind[4] = lambda: gather("S", "ghi", 0, "aw", 0, WW, "lh", 22)
+            behind[2] = lambda: gather(ALL_S, "aw", 0, "wb", ID, ID + WW, "eb")
+            behind[3] = lambda: gather(ALL_S, "glo", 0, "aw", 0, WW, "lh")
+            behind[4] = lambda: gather(ALL_S, "ghi", 0, "aw", 0, WW, "lh", 22)
         for s in range(1, 7):
-            sp = [f or (lambda: None) for f in spare[s]]
-            gather("VS", "wb", VV[s], "wb", W0[s], VV[s - 1] + WW, "kk", 24 * s)
-            sp[0]()
-            gather("VS", "uu", 0, "wb", W0[s] + VV[s] - VV[s - 1], VV[s] + WW, "kk", 24 * s)
+            gather(FIRST, "wb", VV[s], "wb", W0[s], VV[s - 1] + WW, "kk", 24 * s)
+            for f in spare[s]:
+                f()
+            gather(SECOND if s < 6 else LAST, "uu", 0, "wb", W0[s] + VV[s] - VV[s - 1], VV[s] + WW, "kk", 24 * s)
             if s in behind:
                 behind[s]()
-            sp[1]()
-            tr(R("t%d" % s, 0, 352), R("uu", 0, 352))
-            sp[2]()
+            if s == 6:
+                own(2, 1)()
+            turn(s, "uu", 0, RUN if s < 6 else CUT[1] // 16 + 2)
             if s < 6:
-                from_turn(s, KB[s + 1], KB[s], VV[s] - W0[s + 1])
-                from_turn(s, WB[s + 1], KB[s], 0)
-                sp[3]()
-        plain("ls", 3, 7, False)
-        lays(5)[0]()
-        plain("ls", 3, 6, True)
-        lays(5)[1]()
+                for a, b in ((0, RUN), (RUN, NS)):
+                    from_turn(s, KB[s + 1], KB[s], VV[s] - W0[s + 1], a, b)
+                    from_turn(s, WB[s + 1], KB[s], 0, a, b)
+        for first in range(2):
+            for h in range(2):
+                plain("ls", 3, 7 - first, first, CUT[h] // 16, CUT[h + 1] // 16)
+            if not first:
+                lay(5, 1)()
         def zed(q, h, t):
             cp(q, R("zt", 4 * CUT[h] + t, 4 * CUT[h + 1], 4), R("xp", C * t, C * t + C), R("ls", CUT[h] // 16, CUT[h + 1] // 16))
 
@@ -406,16 +430,14 @@ def rank_program(g, core, T, topo):
         layer(0)
         zed("S", 1, 3)
         zed("V", 1, 1)
-        out("S", 0, 0)
-        out("S", 0, 1)
         layer(1)
-        out("V", 0, 3)
-        out("S", 0, 2)
+        for b in range(4):
+            out("VSSV"[b], 0, b)
         n_sent = leave(0)
-        for q, b in (("S", 0), ("S", 1), ("V", 2), ("V", 3)):
-            out(q, 1, b)
+        for b in range(4):
+            out("SSSV"[b], 1, b)
         sent.append(n_sent + leave(1))
-        for f in lays(7)[:1] + lays(6)[:1] + lays(7)[1:] + lays(6)[1:] + ([] if last else order_tables()[2:]):
+        for f in [lay(7, 0), lay(6, 0)] + ([] if last else order_tables()[:2]) + [lay(7, 1), lay(6, 1)] + ([] if last else order_tables()[2:]):
             f()
         if r == 0:
             for par in range(2):
@@ -430,8 +452,8 @@ def rank_program(g, core, T, topo):
             quant("vq", "vs", 0, 128, "vt")
         if last:
             cp("S", R("llw"), R("idf"), R("ls", 0, 20))
-            for k in range(8):
-                store("Y", T.ll[k:k + 1, :], R("llw", 0, C, 1, 16 * k, 16 * k + 1))
+            g.sync.wait_ge(T.sem["sent%d" % r], sent[r])
+            store("Y", T.ll[:, :], (R("llw")[0], T.llw[0:128:16, 0:C]))
         ldc, lds = R("ldc%d" % r, cast=dt.uint32), R("lds%d" % r)
         note([ldc, lds], [], "arr%d" % r, arrivals(r))
         for h in range(2):
@@ -440,13 +462,17 @@ def rank_program(g, core, T, topo):
                 cp("V", R("%sc%d" % (n, r), CX[h], CX[h + 1], cast=dt.uint32), ldc, off)
                 cp("S", R("%ss%d" % (n, r), CX[h], CX[h + 1]), lds, off)
         for h in range(2):
-            for b in range(4):
-                mm(4 * h + b, "eq", "es", 128 * b, "gac%d" % r, "gas%d" % r, True, False)
-                mm(4 * h + b, "eq", "es", 512 + 128 * b, "gbc%d" % r, "gbs%d" % r, False, True)
+            for par, b in UNPACK[h]:
+                n = ("ga", "gb")[par]
+                mm(4 * h + b, "eq", "es", 512 * par + 128 * b, "%sc%d" % (n, r), "%ss%d" % (n, r), par == 0, par == 1)
+
+        def add(k):
+            x = R("xi", 4 * CX[k // 4] + k % 4, 4 * CX[k // 4 + 1], 4)
+            tt(x, bank(k), x, A.add)
+
         for h in range(2):
-            for b in range(4):
-                x = R("xi", 4 * CX[h] + b, 4 * CX[h + 1], 4)
-                tt(x, bank(4 * h + b), x, A.add)
+            for k in range(*((0, ADDS[last]), (ADDS[last], 8))[h]):
+                add(k)
             quant("xq", "xs", CX[h], CX[h + 1], "xi")
             if last:
                 mm(4 * h, "vq", "vs", 0, "xq", "xs")
@@ -455,8 +481,8 @@ def rank_program(g, core, T, topo):
                 cp("S" if h == 0 else "V", R("ysb", a, b), bank(4 * h))
                 if h == 1:
                     for k in range(4):
-                        store("S", T.osc[4 * k:4 * k + 4, :], R("xs", 0, C, 1, 32 * k, 32 * k + 4))
-                store("Y", T.y[:, a:b], R("ysb", a, b))
+                        store("Y", T.osc[4 * k:4 * k + 4, :], R("xs", 0, C, 1, 32 * k, 32 * k + 4))
+                store("S", T.y[:, a:b], R("ysb", a, b))
             else:
                 mm(4 * h, "u2q", "u2s", 0, "xq", "xs")
                 if h == 0:

@@ -2,7 +2,7 @@ from concourse.bass import DstId, RemoteDMATransfer, IndirectOffsetOnAxis
 from concourse.mybir import dt, AluOpType, AxisListType, ActivationFunctionType
 
 C, ROUNDS, STEP = 320, 3, [4, 1, 2]
-CUT = [0, 160, 320]
+CUT = [0, 128, 320]
 CX = [0, 192, 320]
 QUART = 80
 MID = 160
@@ -10,79 +10,91 @@ NS, WW = 21, 336
 SLOT = [1, 7, 2, 0, 3, 5, 4, 6]
 ID, EB, DD, EA = 0, WW, 2 * WW, 3 * WW
 VV = [4 * WW] + [4 * WW + 352 + WW * s for s in range(7)]
-RUN = 10
-FIRST = [("S", 0, 6), ("V", 6, 10), ("S", 10, 14), ("V", 14, NS)]
-SECOND = [("S", 0, 6), ("V", 6, 10), ("S", 10, 14), ("V", 14, NS)]
-LAST = [("S", 0, 6), ("V", 6, 12), ("S", 12, 16), ("V", 16, NS)]
+EC, ED = 24 * 7, 24 * 8
+AWAY = 16
+RUN = 8
+FIRST = [("S", 0, 4), ("V", 4, 8), ("S", 8, 14), ("V", 14, NS)]
+SECOND = [("V", 0, 8), ("S", 10, NS), ("V", 8, 10)]
+CZ = [0, 192, 320]
+LAST = [[("S", 0, 4), ("V", 4, 8), ("S", 8, 14), ("V", 14, 20)], [("S", 0, 6), ("V", 6, 12), ("S", 12, 16), ("V", 16, 20)]]
 UNPACK = [[(0, 0), (0, 1), (0, 2), (1, 0), (1, 1), (0, 3), (1, 2), (1, 3)], [(k % 2, k // 2) for k in range(8)]]
-ADDS = [8, 6]
-OWN = True
+ADDS = [4, 8, 6]
+AHEAD = [True, True, False]
+CS = CX
+OUTS = "VSSVSVSV"
+LAID = [("S", 0, 0), ("V", 0, 1), ("S", 0, 2), ("V", 0, 3), ("S", 1, 0)]
+LAID2 = [("S", 1, 2), ("V", 1, 1), ("S", 1, 3)]
+OUTS2 = "SSSVSVSV"
+ZED = [((("V", 1, 0),), (("S", 1, 3), ("V", 1, 1)))] * 2
+PIECES = [(0, 0, 64, 0, 0), (0, 64, 128, 0, 1), (0, 128, 320, 1, 0), (1, 0, 320, 1, 1)]
+PARTS = [(0, 6, 1), (6, 12, 0), (12, 16, 13), (16, 21, 12)]
+SCANS = [(0, 192), (192, 384), (384, 512), (512, 672)]
+LEVEL = SECOND
+OPEN = [("S", 0, 12), ("V", 12, NS)]
+OWN = False
 LOADS = "ulm01"
 X4 = "float8_e4m3fn_x4"
 SCRATCH = {
     "xi": ("sbuf", [128, 4 * C], "bfloat16"), "xp": ("sbuf", [128, 4 * C], "bfloat16"),
     "zt": ("sbuf", [128, 4 * C], "bfloat16"), "ht": ("sbuf", [128, 4 * C], "bfloat16"),
     "ut": ("sbuf", [128, 512], "bfloat16"), "vt": ("sbuf", [128, 512], "bfloat16"),
-    "icb": ("sbuf", [128, 520], "bfloat16"), "et": ("sbuf", [128, 4 * 520], "bfloat16"),
+    "icb": ("sbuf", [128, 520], "float32"), "icd": ("sbuf", [128, 520], "bfloat16"), "et": ("sbuf", [128, 6 * 520], "bfloat16"), "hp": ("sbuf", [128, 4 * C], "bfloat16"),
     "uq": ("sbuf", [128, 128], X4), "us": ("sbuf", [128, 128], "uint8"), "u2q": ("sbuf", [128, 128], X4), "u2s": ("sbuf", [128, 128], "uint8"),
     "vq": ("sbuf", [128, 128], X4), "vs": ("sbuf", [128, 128], "uint8"),
     "wq": ("sbuf", [128, 512], X4), "wp": ("sbuf", [128, 512], "uint8"),
-    "eq": ("sbuf", [128, 1024], X4), "es": ("sbuf", [128, 1024], "uint8"),
+    "eq": ("sbuf", [128, 1536], X4), "es": ("sbuf", [128, 1536], "uint8"),
     "xq": ("sbuf", [128, C], X4), "xs": ("sbuf", [128, C], "uint8"),
     "zq": ("sbuf", [128, C], X4), "zs": ("sbuf", [128, C], "uint8"),
     "ssb": ("sbuf", [128, C], "float32"), "ssm": ("sbuf", [128, C], "float32"),
-    "df": ("sbuf", [128, 352], "bfloat16"), "ta": ("sbuf", [128, C], "bfloat16"), "tb": ("sbuf", [128, 352], "bfloat16"),
-    "d0": ("sbuf", [128, 88], "float32"), "d1": ("sbuf", [128, 88], "float32"), "sc": ("sbuf", [128, 88], "float32"),
-    "ct": ("sbuf", [128, 48], "float32"), "lo": ("sbuf", [128, 48], "float32"), "hi": ("sbuf", [128, 48], "float32"), "thr": ("sbuf", [128, 48], "float32"),
-    "mtt": ("sbuf", [128, 48], "int32"), "lab": ("sbuf", [128, 24], "int32"), "pi": ("sbuf", [128, 8], "int32"), "pm": ("sbuf", [128, 8], "float32"),
+    "df": ("sbuf", [128, 352], "bfloat16"), "tu": ("sbuf", [128, 352 + C], "bfloat16"), "tq": ("sbuf", [128, 64], "float32"),
+    "d1": ("sbuf", [128, 8 * NS], "float32"), "sc": ("sbuf", [128, 8 * NS], "float32"), "so": ("sbuf", [128, 4], "uint16"),
+    "ct": ("sbuf", [128, 24], "float32"), "lo": ("sbuf", [128, 48], "float32"), "cq": ("sbuf", [128, 64], "float32"), "mq": ("sbuf", [128, 64], "float32"),
+    "dq": ("sbuf", [128, 48], "float32"), "ng": ("sbuf", [128, 48], "float32"),
+    "mtt": ("sbuf", [128, 48], "int32"), "lab": ("sbuf", [128, 24], "int32"), "pi": ("sbuf", [128, 8], "int32"), "pm": ("sbuf", [128, 24], "float32"),
     "mo": ("sbuf", [128, 24], "uint16"), "lh": ("sbuf", [128, 48], "uint16"), "uo": ("sbuf", [128, 8], "uint16"),
-    "ea": ("sbuf", [128, 24], "uint16"), "eb": ("sbuf", [128, 24], "uint16"), "ec": ("sbuf", [128, 24], "uint16"), "ed": ("sbuf", [128, 24], "uint16"),
-    "kk": ("sbuf", [128, 24 * 7], "uint16"), "ls": ("sbuf", [128, 24], "uint16"), "pa": ("sbuf", [128, 24], "uint16"), "pb": ("sbuf", [128, 24], "uint16"),
+    "ea": ("sbuf", [128, 24], "uint16"), "eb": ("sbuf", [128, 24], "uint16"), "uf": ("sbuf", [128, 8], "float32"),
+    "kk": ("sbuf", [128, 24 * 9], "uint16"), "wo": ("sbuf", [128, 32], "uint16"), "wi": ("sbuf", [128, 32], "float32"),
+    "tm": ("sbuf", [128, C], "bfloat16"), "w2q": ("sbuf", [128, 512], X4), "w2s": ("sbuf", [128, 512], "uint8"), "pa": ("sbuf", [128, 24], "uint16"), "pb": ("sbuf", [128, 24], "uint16"),
     "idn": ("sbuf", [128, WW], "bfloat16"), "wb": ("sbuf", [128, VV[7]], "bfloat16"), "uu": ("sbuf", [128, 352], "bfloat16"),
     "aw": ("sbuf", [128, WW], "bfloat16"), "glo": ("sbuf", [128, 352], "bfloat16"), "ghi": ("sbuf", [128, 352], "bfloat16"),
     "tlo": ("sbuf", [128, 352], "bfloat16"), "thi": ("sbuf", [128, 352], "bfloat16"),
     "idf": ("sbuf", [128, C], "float32"), "llw": ("sbuf", [128, C], "float32"), "ysb": ("sbuf", [128, C], "float32"),
-    "rlq": ("sbuf", [128, 2 * QUART], X4), "rls": ("sbuf", [128, 2 * QUART], "uint8"),
+    "rlq": ("sbuf", [128, C], X4), "rls": ("sbuf", [128, C], "uint8"),
     "ps": ("psum", [128, 4096], "float32"),
 }
 for _k in range(7):
     SCRATCH["t%d" % _k] = ("sbuf", [128, 352], "bfloat16")
 for _r in range(ROUNDS):
+    SCRATCH["ls%d" % _r] = SCRATCH["pn%d" % _r] = ("sbuf", [128, 24], "uint16")
     for _n in ("hq", "ld", "ga", "gb"):
         SCRATCH["%sc%d" % (_n, _r)] = ("sbuf", [128, C], X4)
         SCRATCH["%ss%d" % (_n, _r)] = ("sbuf", [128, C], "uint8")
 QUEUES = ("V", "S", "P", "G")
-SEMAPHORES = (["qV", "qS", "qP", "qG"] + ["dm%d" % k for k in range(8)] + ["arr%d" % r for r in range(ROUNDS)] + ["sent%d" % r for r in range(ROUNDS)]
-              + ["hop0", "hop1", "hop2", "hopsent", "stored"])
+SEMAPHORES = (["qV", "qS", "qP", "qG"] + ["dm%d" % k for k in range(8)] + ["arr%d%d" % (r, k) for r in range(ROUNDS) for k in range(2)] + ["sent%d" % r for r in range(ROUNDS)]
+              + ["list%d" % r for r in range(ROUNDS)] + ["hop0", "hop1", "hop2", "hop3", "hop4", "hop5", "hopsent", "stored"])
 
 
 def relays(core, dst, T, topo):
     return [c for c in topo.cores_of(core) if c != core and T.rank_of(c) is None and topo.die(c) == topo.die(core) and topo.may_write(c, dst)][:2]
 
 
-def half_mask(core, to, k, topo):
-    return sum(1 << e for e in topo.engines(core, to)[k::2])
+def piece(T, k, codes, plane):
+    kind, a, b = PIECES[k][:3]
+    return T[plane][:, a:b] if kind else T[codes][:, a:b].bitcast(dt.uint8)
 
 
 def hand_on(g, core, T, topo):
     for r, s in enumerate(STEP):
         for i in range(len(T.cores)):
             src, dst = T.cores[i], T.cores[i ^ s]
-            if topo.may_write(src, dst):
+            if topo.may_write(src, dst) or core not in relays(src, dst, T, topo):
                 continue
-            rel = relays(src, dst, T, topo)
-            if core not in rel:
-                continue
-            k = rel.index(core)
-            n_in, m = len(topo.engines(src, core)) // 2, topo.mask(core, dst)
+            mine = [k for k, p in enumerate(PIECES) if relays(src, dst, T, topo)[p[4]] == core]
             rid, pid = topo.addr(dst, core)
-            for h in range(2):
-                a = CUT[h] + QUART * k
-                g.wait_ge(T.sem["hop%d" % h], n_in)
-                g.remote_dma(T["ldc%d" % r][:, a:a + QUART].bitcast(dt.uint8), T.rlq[:, QUART * h:QUART * h + QUART].bitcast(dt.uint8), T.sem["arr%d" % r], T.sem.hopsent, pid, rid, m)
-            g.wait_ge(T.sem.hop2, n_in)
-            g.remote_dma(T["lds%d" % r][:, CUT[k]:CUT[k + 1]], T.rls[:, 0:2 * QUART], T.sem["arr%d" % r], T.sem.hopsent, pid, rid, m)
-            g.wait_ge(T.sem.hopsent, 3 * len(topo.engines(core, dst)))
+            for k in mine:
+                g.wait_ge(T.sem["hop%d" % k], len(topo.engines(src, core)))
+                g.remote_dma(piece(T, k, "ldc%d" % r, "lds%d" % r), piece(T, k, "rlq", "rls"), T.sem["arr%d%d" % (r, PIECES[k][0])], T.sem.hopsent, pid, rid, topo.mask(core, dst))
+            g.wait_ge(T.sem.hopsent, len(mine) * len(topo.engines(core, dst)))
 
 
 def rank_program(g, core, T, topo):
@@ -140,7 +152,7 @@ def rank_program(g, core, T, topo):
             readers.append((r[0], s, n))
 
     def op(q, call, W, Rd, own_waw=True):
-        waits(q, W, Rd, own_waw and OWN)
+        waits(q, W, Rd, own_waw)
         s = "q" + q
         cnt[s] = cnt.get(s, 0) + 1
         call().then_inc(T.sem[s], 1)
@@ -167,11 +179,11 @@ def rank_program(g, core, T, topo):
     def tt(o, a, b, f, off=None):
         op("V", lambda: g.vector.tensor_tensor(o[1], a[1] if off is None else a[1].indirect(off[1]), b[1], f), [o], [a, b] + ([off] if off else []))
 
-    def ts(o, a, s1, f, s2=None, f2=None):
+    def ts(o, a, s1, f, s2=None, f2=None, own=True):
         cols = [s for s in (s1, s2) if isinstance(s, tuple)]
         v1, v2 = [s[1] if isinstance(s, tuple) else s for s in (s1, s2)]
         if f2 is None:
-            op("V", lambda: g.vector.tensor_scalar(o[1], a[1], v1, None, f), [o], [a] + cols)
+            op("V", lambda: g.vector.tensor_scalar(o[1], a[1], v1, None, f), [o], [a] + cols, own)
         else:
             op("V", lambda: g.vector.tensor_scalar(o[1], a[1], v1, v2, f, f2), [o], [a] + cols)
 
@@ -217,30 +229,37 @@ def rank_program(g, core, T, topo):
         for e, a, b in shares:
             cp(e, R(out, at + 16 * a, at + 16 * b), R(win, w0, w1), R(off, o0 + a, o0 + b))
 
-    def from_scan(dst, to, src, side, n=1, at=0):
-        ts(R(dst, at, at + NS, 1, 32 * to, 32 * (to + n)), R("sc", 2 * NS * side + 1, 2 * NS * side + 2 * NS, 2, 32 * src, 32 * (src + n)), shift(src, n), A.add)
+    def from_scan(side, parts):
+        for i0, i1, c0 in parts:
+            ts(R(("ea", "eb")[side], c0, c0 + 2 * (i1 - i0) - 1, 2), R("sc", 8 * i0 + 4 * side + 2, 8 * i1, 8), shift(0, 4), A.add)
+
+    def move(dst, to, src, at, n=1, c0=0):
+        cp("V", R(dst, c0, c0 + NS, 1, 32 * to, 32 * (to + n)), R(src, 0, NS, 1, 32 * at, 32 * (at + n)))
 
     def turn(s, src, at, cut, p1=128):
         for a, b in ((0, cut), (cut, NS + 1)):
             tr(R("t%d" % s, 16 * a, 16 * b, 1, 0, p1), R(src, at + 16 * a, at + 16 * b, 1, 0, p1))
 
-    def from_turn(s, to, src, base, a, b):
-        ts(R("kk", 24 * (s + 1) + a, 24 * (s + 1) + b, 1, 32 * to, 32 * to + 32), R("t%d" % s, 16 * a, 16 * b, 16, 32 * src, 32 * src + 32), float(MID + base), A.add, shift(src), A.add)
+    def from_turn(s, to, src, base, a, b, use=None):
+        use = s + 1 if use is None else use
+        ts(R("kk", 24 * use + a, 24 * use + b, 1, 32 * to, 32 * to + 32), R("t%d" % s, 16 * a, 16 * b, 16, 32 * src, 32 * src + 32), float(MID + base), A.add, shift(src), A.add)
 
     HELD = {0: 1, 1: 0, 2: 1, 3: 2, 4: 3, 5: 0, 6: 3, 7: 0}
 
-    def plain(dst, to, li, first, a=0, b=20):
+    def plain(dst, to, li, first, a=0, b=20, own=True):
         n, k, src = (16, 1, HELD[li]) if first else (32, 0, HELD[li])
         o = R(dst, a, b, 1, 32 * to, 32 * to + n)
         if li < 2:
-            cp("V", o, R("sc", 2 * NS + 2 * (k + a) + 1, 2 * NS + 2 * (k + b), 2, 32 * src, 32 * src + n))
+            ts(o, R("eb", k + a, k + b, 1, 32 * src, 32 * src + n), -16.0 * k, A.add)
         else:
-            ts(o, R("t%d" % min(li, 6), 16 * (k + a), 16 * (k + b), 16, 32 * src, 32 * src + n), float(MID), A.add)
+            ts(o, R("t%d" % min(max(li, 3), 6), 16 * (k + a), 16 * (k + b), 16, 32 * src, 32 * src + n), float(MID), A.add, own=own)
 
-    def order_tables():
-        return [lambda: tr(R("tlo", 0, 352, 1, 0, 64), R("glo", 0, 352, 1, 0, 64)), lambda: tr(R("thi", 0, 352, 1, 0, 64), R("ghi", 0, 352, 1, 0, 64)),
-                lambda: ts(R("d1", 2 * NS + 1, 4 * NS, 2, 0, 64), R("tlo", 0, WW, 16, 0, 64), float(MID), A.add),
-                lambda: tt(R("d0", 2 * NS + 1, 4 * NS, 2, 0, 64), R("thi", 0, WW, 16, 0, 64), R("tlo", 0, WW, 16, 0, 64), A.subtract)]
+    def order_tables(q="V"):
+        low, high, at = R("tq", 0, NS, 1, 0, 64), R("tq", 32, 32 + NS, 1, 0, 64), [R("d1", 4 + k, 8 * NS, 8, 0, 64) for k in range(3)]
+        return [lambda: tr(R("tlo", 0, 352), R("glo", 0, 352)), lambda: tr(R("thi", 0, 352), R("ghi", 0, 352)),
+                lambda: cp(q, R("tq", 0, 32), R("tlo", 0, 352), R("so", 2, 4)), lambda: cp(q, R("tq", 32, 64), R("thi", 0, 352), R("so", 2, 4)),
+                lambda: op("S", lambda: g.scalar.activation(at[2][1], low[1], AF.Identity, bias=float(MID)), [at[2]], [low]), lambda: tt(at[1], high, low, A.subtract),
+                lambda: tt(at[0], at[1], R("ng", 1, 2 * NS, 2, 0, 64), A.mult)]
 
     fill(R("mtt", 0, 48), 0)
     fill(R("lab", 0, 24), 0)
@@ -250,7 +269,7 @@ def rank_program(g, core, T, topo):
         if what == "l":
             load([("YS"[k], R("lab", 1 - k, 21 - k, 1, 32 * b + 16 * k, 32 * b + 16 * k + 16), (T.lb, T.la)[b][:, :]) for b in range(2) for k in range(2)])
         if what == "m":
-            load([("YS"[k], R("mtt", NS * side + 1 - k, NS * side + 21 - k, 1, 32 * b + 16 * k, 32 * b + 16 * k + 16), T.mt[16 * SLOT[2 * b + side]:16 * SLOT[2 * b + side] + 16, :])
+            load([("YS"[k], R("mtt", 24 * side + 1 - k, 24 * side + 21 - k, 1, 32 * b + 16 * k, 32 * b + 16 * k + 16), T.mt[16 * SLOT[2 * b + side]:16 * SLOT[2 * b + side] + 16, :])
                   for b in range(4) for side in range(2) for k in range(2)])
         if what in "01":
             h = int(what)
@@ -259,219 +278,333 @@ def rank_program(g, core, T, topo):
     load([("Y", R("vt", 0, 512), T.v[:, :])])
     iota(R("pi", 0, 2), [[0, 2]], 0, 1, True)
     iota(R("idn", 0, WW), [[1, WW]], -MID, 0)
-    iota(R("ct", 0, 2 * NS), [[0, 2], [16, NS]], -16, 1)
-    iota(R("icb", 0, 516), [[1, 516]], 0, -4)
+    iota(R("ct", 0, 24), [[16, 24]], 0, 0)
+    for k, step in ((0, 2), (1, 2), (5, 2)):
+        n = 4 if k == 0 else 2
+        iota(R("uf", k, k + step * n - 1, step), [[16 * (SLOT[k + step] - SLOT[k]), n]], 16 * SLOT[k], 0)
+    iota(R("wi", 0, 32), [[128, 4], [-16, 8]], 112, 0)
+    iota(R("icb", 0, 516), [[1, 516]], 0, 0)
     iota(R("idf"), [[1, C]], 0, 0)
-    for k in range(8):
-        fill(R("uo", k, k + 1), 16 * SLOT[k])
-    ts(R("pi", 2, 4), R("pi", 0, 2), 16, A.bitwise_and)
-    ts(R("pi", 4, 6), R("pi", 0, 2), 96, A.bitwise_and)
-    fill(R("kk", 0, 24 * 7), 0)
-    fill(R("d0", 0, 88), 0.0)
-    cp("V", R("pm", 6, 8), R("pi", 4, 6))
-    ts(R("pm", 0, 2), R("pi", 2, 4), 0.0, A.is_equal, 16.0, A.mult)
-    ts(R("pm", 2, 4), R("pi", 2, 4), 0.0, A.is_equal)
-    ts(R("pm", 4, 6), R("pi", 2, 4), 0.0, A.is_gt)
-    for n, a in (("df", 0), ("df", WW), ("uu", WW), ("glo", WW), ("ghi", WW), ("wb", VV[0] + WW)):
-        fill(R(n, a, a + 16), 0.0)
+    col = lambda n, k: R(n, k, k + 1)
+    fill(R("kk", 0, 24 * 9), 0)
+    for k, m in enumerate((16, 15, 4)):
+        ts(col("pi", 2 + k), col("pi", 0), m, A.bitwise_and)
+    fill(R("d1", 3, 8 * NS, 4), 0.0)
+    ts(col("pm", 0), col("pi", 2), 0.0, A.is_equal, 16.0, A.mult)
+    cp("V", col("pm", 11), col("pi", 3))
+    ts(col("pm", 12), col("pi", 3), 2.0, A.mult, 1.0, A.add)
+    ts(col("pm", 13), col("pi", 3), 2.0, A.mult, 12.0, A.add)
+    ts(col("pm", 14), col("pi", 3), 6.0, A.is_ge, -13.0, A.mult)
+    ts(col("pm", 15), col("pi", 3), 12.0, A.is_ge)
+    ts(col("pm", 8), col("pi", 4), -0.5, A.mult, 1.0, A.add)
+    ts(col("pm", 10), col("pi", 3), 4.0, A.is_lt, 2.0 ** 90, A.mult)
+    ts(col("pm", 13), col("pm", 13), 20.0, A.min)
+    ts(col("pm", 12), col("pm", 12), col("pm", 14), A.add, col("pm", 15), A.add)
     ts(R("wb", ID, ID + WW), R("idn", 0, WW), shift(0, 4), A.subtract)
-    ts(R("ct", 0, 2 * NS), R("ct", 0, 2 * NS), R("pm", 6, 7), A.subtract)
-    ts(R("ed", 0, NS, 1, 0, 32), R("ct", 0, NS, 1, 0, 32), shift(0), A.add)
+    ts(R("ct", 0, 24), R("ct", 0, 24), col("pm", 11), A.add, shift(0, 4), A.subtract)
+    cp("V", R("so", 0, 2), R("pm", 12, 14))
+    ts(R("so", 2, 4), R("pm", 12, 14), 16.0, A.mult)
+    for n, a in (("df", 0), ("df", WW), ("uu", C), ("uu", WW), ("glo", WW), ("ghi", WW), ("wb", VV[0] + WW)):
+        cp("S", R(n, a, a + 16), R("idn", MID, MID + 16), scale=0.0)
+    ts(R("kk", ED, ED + NS, 1, 0, 32), R("ct", 0, NS, 1, 0, 32), shift(0), A.add)
+    ts(col("pm", 16), col("pi", 0), 4.0, A.mult, -448.0, A.add)
+    cp("V", R("uo", 0, 8), R("uf", 0, 8))
+    ts(R("wo", 0, 32), R("wi", 0, 32), col("pm", 11), A.add)
+    ts(col("pm", 17), col("pm", 11), -8.0, A.mult, col("pm", 16), A.add)
+    for side in range(2):
+        cp("S", R("cq", side, 64, 2), R("ct", 0, 24), R("so", 0, 2))
     ALL_S = [("S", 0, NS)]
     ts(R("eb", 0, NS), R("lab", 0, NS), shift(0, 4), A.add)
     gather(ALL_S, "aw", 0, "wb", ID, ID + WW, "eb")
     quant("uq", "us", 0, 128, "ut")
-    tt(R("lo", 0, 2 * NS), R("mtt", 0, 2 * NS), R("ct", 0, 2 * NS), A.min)
-    tt(R("hi", 0, 2 * NS), R("mtt", 0, 2 * NS), R("ct", 0, 2 * NS), A.max)
+    tt(R("lo", 0, NS), R("mtt", 24, 24 + NS), R("ct", 0, NS), A.min)
+    tt(R("lo", 24, 24 + NS), R("mtt", 24, 24 + NS), R("ct", 0, NS), A.max)
     cp("V", R("u2q", 0, 128, cast=dt.uint32), R("uq", 0, 128, cast=dt.uint32), R("uo", 0, 8))
-    ts(R("lh", 0, NS), R("lo", NS, 2 * NS), shift(0, 4), A.add)
-    ts(R("lh", 22, 22 + NS), R("hi", NS, 2 * NS), shift(0, 4), A.add)
+    ts(R("lh", 0, NS), R("lo", 0, NS), shift(0, 4), A.add)
+    ts(R("lh", 22, 22 + NS), R("lo", 24, 24 + NS), shift(0, 4), A.add)
     cp("S", R("u2s", 0, 128), R("us", 0, 128), R("uo", 0, 8))
     gather(ALL_S, "glo", 0, "aw", 0, WW, "lh")
     gather(ALL_S, "ghi", 0, "aw", 0, WW, "lh", 22)
-    cp("V", R("mo", 0, 20), R("mtt", NS, NS + 20))
-    tt(R("thr", 0, 2 * NS), R("mtt", 0, 2 * NS), R("ct", 0, 2 * NS), A.is_lt)
-    cp("V", R("d1", 1, 4 * NS, 2), R("lo", 0, 2 * NS))
-    tt(R("d0", 1, 4 * NS, 2), R("hi", 0, 2 * NS), R("lo", 0, 2 * NS), A.subtract)
-    for h in range(2):
-        quant("xq", "xs", CX[h], CX[h + 1], "xi")
-        mm(4 * h, "u2q", "u2s", 0, "xq", "xs")
+    for side in range(2):
+        cp("V", R("mq", side, 64, 2), R("mtt", 24 * side, 24 * side + 24), R("so", 0, 2))
+    cp("V", R("mo", 0, 20), R("mtt", 24, 44))
+    tt(R("dq", 0, 2 * NS), R("cq", 0, 2 * NS), R("mq", 0, 2 * NS), A.subtract)
+    tt(R("d1", 2, 8 * NS, 4), R("cq", 0, 2 * NS), R("mq", 0, 2 * NS), A.min)
+    tt(R("ng", 0, 2 * NS), R("cq", 0, 2 * NS), R("mq", 0, 2 * NS), A.max)
+    quant("xq", "xs", CX[0], CX[1], "xi")
+    mm(0, "u2q", "u2s", 0, "xq", "xs")
+    ts(R("d1", 0, 8 * NS, 4), R("dq", 0, 2 * NS), 0.0, A.min)
+    tt(R("d1", 1, 8 * NS, 4), R("ng", 0, 2 * NS), R("d1", 2, 8 * NS, 4), A.subtract)
+    quant("xq", "xs", CX[1], CX[2], "xi")
+    mm(4, "u2q", "u2s", 0, "xq", "xs")
+
+    def scores(name, h, after=[]):
+        o, i, sign, big = R(name, CX[h], CX[h + 1]), bank(4 * h), col("pm", 8), col("pm", 10)
+        if name == "ssb":
+            op("S", lambda: g.scalar.activation(o[1], i[1], AF.Identity, scale=sign[1]), [o], [i, sign])
+        else:
+            op("S", lambda: g.scalar.activation(o[1], i[1], AF.Identity, bias=big[1], scale=sign[1]), [o], [i, sign, big] + after)
 
     def first_scores():
-        cp("S", R("ssb", 0, CX[1]), bank(0))
-        cp("S", R("ssm", 0, CX[1]), bank(0))
+        scores("ssb", 0)
+        scores("ssm", 0)
 
     first_scores()
+    order_tables()[0]()
     for b in range(4):
         cp("V", R("mo", 0, 20, 1, 32 * b, 32 * b + 16), R("mtt", 1, 21, 1, 32 * b, 32 * b + 16))
-    ts(R("thr", 0, 2 * NS), R("thr", 0, 2 * NS), -2.0 ** -99, A.mult)
-    order_tables()[0]()
+    order_tables()[1]()
+
+    def turned(k, q):
+        a, b = (0, 6, 12, 18, 24, 28, 32)[k:k + 2]
+        if q == "V":
+            cp("V", R("w2q", 16 * a, 16 * b, cast=dt.uint32), R("wq", 0, 512, cast=dt.uint32), R("wo", a, b))
+        else:
+            cp("S", R("w2s", 16 * a, 16 * b), R("wp", 0, 512), R("wo", a, b))
 
     def send(r, h):
-        dst = T.cores[rank ^ STEP[r]]
-        a, b = CUT[h], CUT[h + 1]
-        hc, sent, arr = "hqc%d" % r, T.sem["sent%d" % r], T.sem["arr%d" % r]
-        waits("G", [], [R(hc, a, b)])
-        if topo.may_write(core, dst):
-            rid, pid = topo.addr(dst, core)
-            g.remote_dma(T["ldc%d" % r][:, a:b].bitcast(dt.uint8), T[hc][:, a:b].bitcast(dt.uint8), arr, sent, pid, rid, topo.mask(core, dst))
-            if h == 1:
-                g.remote_dma(T["lds%d" % r][:, 0:C], T["hqs%d" % r][:, 0:C], arr, sent, pid, rid, topo.mask(core, dst))
-            return (1 + h) * len(topo.engines(core, dst))
-        rel = relays(core, dst, T, topo)
-        ids = [[DstId(rid=topo.addr(to, core)[0], pnc=topo.addr(to, core)[1])] for to in rel]
-        g.remote_dma_fused([RemoteDMATransfer(dst_ids=ids[k], dma_engine_mask=half_mask(core, to, k, topo), remote_sem=T.sem["hop%d" % h],
-                                              src=T[hc][:, a + QUART * k:a + QUART * k + QUART].bitcast(dt.uint8), dst=T.rlq[:, QUART * h:QUART * h + QUART].bitcast(dt.uint8))
-                            for k, to in enumerate(rel)], local_sem=sent)
-        if h == 1:
-            g.remote_dma_fused([RemoteDMATransfer(dst_ids=ids[k], dma_engine_mask=half_mask(core, to, k, topo), remote_sem=T.sem.hop2,
-                                                  src=T["hqs%d" % r][:, CUT[k]:CUT[k + 1]], dst=T.rls[:, 0:2 * QUART]) for k, to in enumerate(rel)], local_sem=sent)
-        return (1 + h) * len(topo.engines(core, rel[0]))
+        dst, n = T.cores[rank ^ STEP[r]], 0
+        waits("G", [], [R("hqc%d" % r, CUT[h], CUT[h + 1])])
+        for k in [k for k, p in enumerate(PIECES) if p[3] == h]:
+            if topo.may_write(core, dst):
+                to, land, sem = dst, piece(T, k, "ldc%d" % r, "lds%d" % r), T.sem["arr%d%d" % (r, PIECES[k][0])]
+            else:
+                to, land, sem = relays(core, dst, T, topo)[PIECES[k][4]], piece(T, k, "rlq", "rls"), T.sem["hop%d" % k]
+            rid, pid = topo.addr(to, core)
+            g.remote_dma(land, piece(T, k, "hqc%d" % r, "hqs%d" % r), sem, T.sem["sent%d" % r], pid, rid, topo.mask(core, to))
+            n += len(topo.engines(core, to))
+        return n
 
-    def arrivals(r):
+    def arrivals(r, kind):
         src = T.cores[rank ^ STEP[r]]
-        if topo.may_write(src, core):
-            return 3 * len(topo.engines(src, core))
-        return sum(3 * len(topo.engines(via, core)) for via in relays(src, core, T, topo))
+        return sum(len(topo.engines(src if topo.may_write(src, core) else relays(src, core, T, topo)[p[4]], core)) for p in PIECES if p[0] == kind)
 
-    KB = {1: 1, 2: 2, 3: 1, 4: 2, 5: 3, 6: 0}
-    WB = {1: 2, 2: 1, 3: 2, 4: 3, 5: 0, 6: 3}
-    W0 = {1: EA, 2: DD, 3: DD, 4: DD, 5: EB, 6: ID}
+    KB = {1: 1, 2: 2, 3: 3, 4: 2, 5: 3, 6: 0}
+    WB = {1: 2, 2: 3, 3: 2, 4: 3, 5: 0, 6: 3}
+    W0 = {1: EA, 2: VV[1], 3: DD, 4: ID, 5: EB, 6: ID}
+    WR = {2: VV[1], 3: DD, 4: DD, 5: EB}
     SHARE = 208
     sent = []
     for r in range(ROUNDS):
-        last = r == ROUNDS - 1
-        cp("V", R("ssb", CX[1], C), bank(4))
+        last, ahead, mate = r == ROUNDS - 1, AHEAD[r], T.cores[rank ^ STEP[r]]
+        ts(R("ssb", CX[1], C), bank(4), col("pm", 8), A.mult)
         if r == 0:
-            order_tables()[1]()
-        cp("S", R("ssm", CX[1], C), R("ssb"), R("mo", CX[1] // 16, 20))
-        tt(R("df", 16, 16 + CX[1]), R("ssb"), R("ssm", 0, CX[1]), A.subtract, off=R("mo", 0, CX[1] // 16))
-        if r == 0:
-            for f in order_tables()[2:]:
+            for f in order_tables("S")[2:4]:
                 f()
-        tt(R("df", 16 + CX[1], 16 + C), R("ssm", CX[1], C), bank(4), A.subtract)
+            ts(R("ng", 0, 2 * NS), R("dq", 0, 2 * NS), 0.0, A.is_lt, -1.0, A.mult)
+        scores("ssm", 1, [R("ssb", CX[1], C)])
+        if r == 0:
+            order_tables()[4]()
+        for h in range(2):
+            tt(R("df", 16 + CX[h], 16 + CX[h + 1]), R("ssb"), R("ssm", CX[h], CX[h + 1]), A.is_ge, off=R("mo", CX[h] // 16, CX[h + 1] // 16))
+            if r == 0:
+                order_tables()[5 + h]()
         for t in range(4):
             cp("S", R("xp", C * t, C * t + C), R("xi", t, 4 * C, 4))
-        for a, b in ((0, CX[1]), (CX[1], 352)):
-            tr(R("ta", a, min(b, C)), R("df", 16 + a, 16 + min(b, C)))
-            tr(R("tb", a, b), R("df", a, b))
-        for side in range(2):
-            tt(R("d1", 2 * (NS * side + 1), 2 * NS * (side + 1), 4), R("ta", 16 * side, C, 32), R("thr", NS * side + 1, NS * (side + 1), 2), A.is_gt)
-            tt(R("d1", 2 * NS * side, 2 * NS * (side + 1), 4), R("tb", 16 * side, 352, 32), R("thr", NS * side, NS * (side + 1), 2), A.is_gt)
-        for side in range(2):
-            o, d0, d1 = [R(n, 2 * NS * side, 2 * NS * (side + 1)) for n in ("sc", "d0", "d1")]
+        if r == 0:
+            for k in range(2):
+                turned(k, "S")
+        n = CX[1]
+        tr(R("tu", 0, n), R("df", 16, 16 + n))
+        tr(R("tu", n, 2 * n), R("df", 0, n))
+        tr(R("tu", 2 * n, n + C), R("df", 16 + n, 16 + C))
+        tr(R("tu", n + C, 352 + C), R("df", n, 352))
+        for a, b in SCANS:
+            o, d0, d1 = R("sc", a // 4, b // 4), R("tu", a, b, 4), R("d1", a // 4, b // 4)
             op("V", lambda: g.vector.tensor_tensor_scan(o[1], d0[1], d1[1], 0.0, A.mult, A.add), [o], [d0, d1])
-        from_scan("ea", 0, 0, 0, 4)
-        from_scan("eb", 0, 0, 1, 4)
-        gather([("S", 0, 10), ("V", 10, NS)], "wb", EA, "wb", ID, ID + WW, "ea")
-        from_scan("ec", 2, 2, 1, 2)
-        from_scan("ec", 0, 2, 1)
-        from_scan("ec", 1, 3, 0)
-        gather(SECOND, "wb", VV[0], "wb", EA, EA + WW, "eb")
-        gather(ALL_S, "wb", EB, "wb", ID, ID + WW, "ec")
-        from_scan("kk", 2, 0, 1, at=24)
-        turn(0, "wb", VV[0], RUN, 32)
-        from_scan("ed", 2, 2, 0, 2)
-        from_turn(0, KB[1], 0, VV[0] - W0[1], 0, RUN)
-        from_scan("ed", 1, 1, 0)
-        from_turn(0, KB[1], 0, VV[0] - W0[1], RUN, NS)
-        def own(b, first):
-            return lambda: plain("ls", b, 2 * b + 1 - first, first)
-
-        def lay(li, first):
-            return lambda: plain(("pb", "pa")[li % 2], (7 - li) // 2, li, first)
-        spare = {1: [own(0, 0), lay(1, 0), lay(0, 0)], 2: [own(0, 1), lay(1, 1), lay(0, 1)], 3: [lay(2, 0)], 4: [own(1, 0), lay(3, 0), lay(2, 1)],
-                 5: [own(1, 1), lay(3, 1), lay(4, 0)], 6: [own(2, 0), lay(5, 0), lay(4, 1)]}
-        behind = {1: lambda: gather(ALL_S, "wb", DD, "wb", EB, EB + WW, "ed")}
+        from_scan(0, PARTS)
+        from_scan(1, PARTS)
+        gather(OPEN, "wb", EA, "wb", ID, ID + WW, "ea")
+        move("kk", 2, "eb", 2, 2, EC)
+        move("kk", 0, "eb", 2, 1, EC)
+        move("kk", 3, "ea", 1, c0=24)
+        behind = {0: ("wb", EB, "wb", ID, ID + WW, "kk", EC), 1: ("wb", DD, "wb", EB, EB + WW, "kk", ED)}
         if not last:
-            behind[2] = lambda: gather(ALL_S, "aw", 0, "wb", ID, ID + WW, "eb")
-            behind[3] = lambda: gather(ALL_S, "glo", 0, "aw", 0, WW, "lh")
-            behind[4] = lambda: gather(ALL_S, "ghi", 0, "aw", 0, WW, "lh", 22)
+            behind.update({2: ("aw", 0, "wb", ID, ID + WW, "eb"), 3: ("glo", 0, "aw", 0, WW, "lh"), 4: ("ghi", 0, "aw", 0, WW, "lh", 22)})
+        gather(LEVEL, "wb", VV[0], "wb", EA, EA + WW, "eb")
+        gather([("S", 0, AWAY)], *behind[0])
+        move("kk", 2, "eb", 0, c0=24)
+        turn(0, "wb", VV[0], RUN, 32)
+        from_turn(0, KB[1], 0, VV[0] - W0[1], 0, RUN)
+        move("kk", 2, "ea", 2, 2, ED)
+        from_turn(0, KB[1], 0, VV[0] - W0[1], RUN, NS)
+        ls = "ls%d" % r
+
+        def own(b, first):
+            return lambda: plain(ls, b, 2 * b + 1 - first, first)
+
+        def both(li, first):
+            plain(("pa", "pb")[li % 2], li // 2, li, first)
+        spare = {1: [own(0, 0)], 2: [lambda: from_turn(1, 1, KB[1], DD - W0[3], 0, NS, 3)], 3: [own(0, 1), lambda: move("kk", 0, "eb", 3, c0=24 * 4)],
+                 4: [own(1, 0)], 5: [own(1, 1)], 6: [own(2, 0)]}
         for s in range(1, 7):
             gather(FIRST, "wb", VV[s], "wb", W0[s], VV[s - 1] + WW, "kk", 24 * s)
+            if s - 1 in behind:
+                gather([("S", AWAY, NS)], *behind[s - 1])
+            if r == 0:
+                turned(s - 1, "V")
+            if not ahead:
+                for li, first in {1: [(0, 0), (1, 0)], 2: [(0, 1), (1, 1)], 3: [], 4: [(2, 0), (3, 0)], 5: [(2, 1), (3, 1), (4, 0)], 6: [(4, 1), (5, 0)]}[s]:
+                    both(li, first)
+            if s == 6:
+                own(2, 0)()
+                break
+            gather(SECOND, "uu", 0, "wb", W0[s] + VV[s] - VV[s - 1], VV[s] + WW, "kk", 24 * s)
             for f in spare[s]:
                 f()
-            gather(SECOND if s < 6 else LAST, "uu", 0, "wb", W0[s] + VV[s] - VV[s - 1], VV[s] + WW, "kk", 24 * s)
             if s in behind:
-                behind[s]()
-            if s == 6:
-                own(2, 1)()
-            turn(s, "uu", 0, RUN if s < 6 else CUT[1] // 16 + 2)
-            if s < 6:
-                for a, b in ((0, RUN), (RUN, NS)):
-                    from_turn(s, KB[s + 1], KB[s], VV[s] - W0[s + 1], a, b)
-                    from_turn(s, WB[s + 1], KB[s], 0, a, b)
-        for first in range(2):
-            for h in range(2):
-                plain("ls", 3, 7 - first, first, CUT[h] // 16, CUT[h + 1] // 16)
-            if not first:
-                lay(5, 1)()
+                gather([("S", 0, AWAY)], *behind[s])
+            if r == 0 and s == 5:
+                for k in range(3, 6):
+                    turned(k, "S")
+            turn(s, "uu", 0, RUN)
+            for a, b in ((0, RUN), (RUN, NS)):
+                from_turn(s, KB[s + 1], KB[s], VV[s] - W0[s + 1], a, b)
+                if s < 5:
+                    from_turn(s, WB[s + 1], KB[s], WR[s + 1] - W0[s + 1], a, b)
+            if s == 5:
+                for k, at in enumerate((VV[4], VV[6])):
+                    ts(R("kk", k, 20, 2, 0, 32), R("t5", 16, C, 32, 32 * KB[5], 32 * KB[5] + 32), float(MID + at - EB), A.add, shift(0), A.add)
+        cz = CZ if ahead else CUT
+        gather(LAST[ahead], "uu", 0, "wb", EB, VV[6] + WW, "kk")
+        own(2, 1)()
+        for h in range(2):
+            tr(R("tm", cz[h], cz[h + 1], 1, 0, 32), R("uu", cz[h], cz[h + 1], 1, 0, 32))
+        for h in range(2):
+            ts(R(ls, cz[h] // 16, cz[h + 1] // 16, 1, 96, 128), R("tm", cz[h], cz[h + 1], 16, 0, 32), float(MID), A.add)
         def zed(q, h, t):
-            cp(q, R("zt", 4 * CUT[h] + t, 4 * CUT[h + 1], 4), R("xp", C * t, C * t + C), R("ls", CUT[h] // 16, CUT[h + 1] // 16))
+            cp(q, R("zt", 4 * cz[h] + t, 4 * cz[h + 1], 4), R("xp", C * t, C * t + C), R(ls, cz[h] // 16, cz[h + 1] // 16))
 
         def layer(h):
-            quant("zq", "zs", CUT[h], CUT[h + 1], "zt")
+            quant("zq", "zs", cz[h], cz[h + 1], "zt")
             for b in range(4):
-                mm(4 * h + b, "wq", "wp", 128 * b, "zq", "zs", cut=CUT)
+                mm(4 * h + b, "w2q", "w2s", 128 * b, "zq", "zs", cut=cz)
 
         def out(q, h, b):
-            o = R("ht", 4 * CUT[h] + b, 4 * CUT[h + 1], 4)
+            o = R("hp", C * b + cz[h], C * b + cz[h + 1]) if ahead else R("ht", 4 * cz[h] + b, 4 * cz[h + 1], 4)
             if q == "S":
-                cp("S", o, bank(4 * h + b, CUT), scale=0.03125)
+                cp("S", o, bank(4 * h + b, cz), scale=0.03125)
             else:
-                ts(o, bank(4 * h + b, CUT), 0.03125, A.mult)
+                ts(o, bank(4 * h + b, cz), 0.03125, A.mult)
 
         def leave(h):
             quant("hqc%d" % r, "hqs%d" % r, CUT[h], CUT[h + 1], "ht")
             return send(r, h)
 
-        for q, h, t in (("V", 0, 0), ("S", 0, 2), ("V", 0, 1), ("S", 0, 3), ("S", 1, 2), ("V", 1, 0)):
+        def lay_out(q, h, t):
+            cp(q, R("ht", 4 * CS[h] + t, 4 * CS[h + 1], 4), R("hp", C * t, C * t + C), R("pn%d" % r, CS[h] // 16, CS[h + 1] // 16))
+
+        def direct(land, src, sem):
+            rid, pid = topo.addr(mate, core)
+            g.remote_dma(land, src, T.sem[sem], T.sem["sent%d" % r], pid, rid, topo.mask(core, mate))
+            return len(topo.engines(core, mate))
+
+        def leave_laid(h):
+            a, b = CS[h], CS[h + 1]
+            quant("hqc%d" % r, "hqs%d" % r, a, b, "ht")
+            waits("G", [], [R("hqc%d" % r, a, b)])
+            return (direct(T["ldc%d" % r][:, a:b].bitcast(dt.uint8), T["hqc%d" % r][:, a:b].bitcast(dt.uint8), "arr%d%d" % (r, h))
+                    + direct(T["lds%d" % r][:, a:b], T["hqs%d" % r][:, a:b], "arr%d%d" % (r, h)))
+
+        def unpackers(par):
+            for odd in range(2):
+                k = 2 * par + odd
+                if par == 2:
+                    ts(R("et", 520 * k, 520 * k + 516), R("icd", 0, 516), float(2 + odd), A.is_equal)
+                else:
+                    ts(R("et", 520 * k, 520 * k + 516), R("icd", 0, 516), float(2 + odd), A.is_equal, col("pm", 2 + 2 * par), A.mult)
+            for b in range(4):
+                k = 4 * par + b
+                quant("eq", "es", 128 * k, 128 * k + 128, "et", 520 * (2 * par + b % 2) + 2 - 2 * (b // 2))
+
+        if r == 0:
+            turned(2, "S")
+        if ahead:
+            waits("G", [], [R(ls, 0, 20)])
+            n_sent = direct(T["pn%d" % r][:, 0:20], T[ls][:, 0:20], "list%d" % r)
+        for q, h, t in (("V", 0, 0), ("S", 0, 2), ("V", 0, 1), ("S", 0, 3), ("S", 1, 2)) + ZED[ahead][0]:
             zed(q, h, t)
         layer(0)
-        zed("S", 1, 3)
-        zed("V", 1, 1)
-        layer(1)
-        for b in range(4):
-            out("VSSV"[b], 0, b)
-        n_sent = leave(0)
-        for b in range(4):
-            out("SSSV"[b], 1, b)
-        sent.append(n_sent + leave(1))
-        for f in [lay(7, 0), lay(6, 0)] + ([] if last else order_tables()[:2]) + [lay(7, 1), lay(6, 1)] + ([] if last else order_tables()[2:]):
-            f()
+        for q, h, t in ZED[ahead][1]:
+            zed(q, h, t)
         if r == 0:
-            for par in range(2):
-                for odd in range(2):
-                    k = 2 * par + odd
-                    ts(R("et", 520 * k, 520 * k + 516), R("icb", 0, 516), float(2 + odd), A.is_equal, R("pm", 2 + 2 * par, 3 + 2 * par), A.mult)
-            for par in range(2):
-                for b in range(4):
-                    k = 4 * par + b
-                    quant("eq", "es", 128 * k, 128 * k + 128, "et", 520 * (2 * par + b % 2) + 2 - 2 * (b // 2))
+            o, i, back = R("icd", 0, 516), R("icb", 0, 516), col("pm", 17)
+            op("S", lambda: g.scalar.activation(o[1], i[1], AF.Identity, bias=back[1]), [o], [i, back])
+        layer(1)
+        if ahead:
+            for k in range(8):
+                out(OUTS[k], k // 4, k % 4)
+            note([R("pn%d" % r, 0, 20)], [], "list%d" % r, len(topo.engines(mate, core)))
+            for q, h, t in LAID:
+                lay_out(q, h, t)
+            n_sent += leave_laid(0)
+            for q, h, t in LAID2:
+                lay_out(q, h, t)
+            sent.append(n_sent + leave_laid(1))
+        else:
+            for b in range(4):
+                out(OUTS2[b], 0, b)
+            n_sent = leave(0)
+            for b in range(4):
+                out(OUTS2[4 + b], 1, b)
+            sent.append(n_sent + leave(1))
+        if not last:
+            for f in order_tables("S")[:4]:
+                f()
+        if r == 0 and any(AHEAD):
+            unpackers(2)
+        if not ahead:
+            from_turn(5, WB[6], KB[5], 0, 0, NS)
+            gather(ALL_S, "uu", 0, "wb", EB, VV[6] + WW, "kk", 24 * 6)
+            both(5, 1)
+        if not last:
+            for f in order_tables()[4:]:
+                f()
+        if r == (2 if AHEAD[1] else 0):
+            ts(col("pm", 2), col("pi", 2), 0.0, A.is_equal)
+            ts(col("pm", 4), col("pi", 2), 0.0, A.is_gt)
+            unpackers(0)
+        if not ahead:
+            tr(R("t6", 0, 352), R("uu", 0, 352))
+        if r == (2 if AHEAD[1] else 0):
+            unpackers(1)
+        if not ahead:
+            for first in range(2):
+                for li in (6, 7):
+                    both(li, first)
         if r == 1:
             quant("vq", "vs", 0, 128, "vt")
         if last:
-            cp("S", R("llw"), R("idf"), R("ls", 0, 20))
+            cp("S", R("llw"), R("idf"), R(ls, 0, 20))
             g.sync.wait_ge(T.sem["sent%d" % r], sent[r])
             store("Y", T.ll[:, :], (R("llw")[0], T.llw[0:128:16, 0:C]))
         ldc, lds = R("ldc%d" % r, cast=dt.uint32), R("lds%d" % r)
-        note([ldc, lds], [], "arr%d" % r, arrivals(r))
-        for h in range(2):
-            for n, ls in (("ga", "pa"), ("gb", "pb")):
-                off = R(ls, CX[h] // 16, CX[h + 1] // 16)
-                cp("V", R("%sc%d" % (n, r), CX[h], CX[h + 1], cast=dt.uint32), ldc, off)
-                cp("S", R("%ss%d" % (n, r), CX[h], CX[h + 1]), lds, off)
-        for h in range(2):
-            for par, b in UNPACK[h]:
-                n = ("ga", "gb")[par]
-                mm(4 * h + b, "eq", "es", 512 * par + 128 * b, "%sc%d" % (n, r), "%ss%d" % (n, r), par == 0, par == 1)
+        if not ahead:
+            note([ldc], [], "arr%d0" % r, arrivals(r, 0))
+            note([lds], [], "arr%d1" % r, arrivals(r, 1))
+            for h in range(2):
+                for n, by in (("ga", "pa"), ("gb", "pb")):
+                    off = R(by, CX[h] // 16, CX[h + 1] // 16)
+                    cp("V", R("%sc%d" % (n, r), CX[h], CX[h + 1], cast=dt.uint32), ldc, off)
+                    cp("S", R("%ss%d" % (n, r), CX[h], CX[h + 1]), lds, off)
+            for h in range(2):
+                for par, b in UNPACK[h]:
+                    n = ("ga", "gb")[par]
+                    mm(4 * h + b, "eq", "es", 512 * par + 128 * b, "%sc%d" % (n, r), "%ss%d" % (n, r), par == 0, par == 1)
 
         def add(k):
-            x = R("xi", 4 * CX[k // 4] + k % 4, 4 * CX[k // 4 + 1], 4)
-            tt(x, bank(k), x, A.add)
+            cut = CS if ahead else CX
+            x = R("xi", 4 * cut[k // 4] + k % 4, 4 * cut[k // 4 + 1], 4)
+            tt(x, bank(k, cut), x, A.add)
 
+        adds = ADDS[r]
         for h in range(2):
-            for k in range(*((0, ADDS[last]), (ADDS[last], 8))[h]):
+            if ahead:
+                note([R("ldc%d" % r, CS[h], CS[h + 1]), R("lds%d" % r, CS[h], CS[h + 1])], [], "arr%d%d" % (r, h), 2 * len(topo.engines(mate, core)))
+                for b in range(4):
+                    mm(4 * h + b, "eq", "es", 1024 + 128 * b, "ldc%d" % r, "lds%d" % r, cut=CS)
+        for h in range(2):
+            for k in range(*((0, adds), (adds, 8))[h]):
                 add(k)
             quant("xq", "xs", CX[h], CX[h + 1], "xi")
             if last:

@@ -1,86 +1,113 @@
-from concourse.bass import DstId, RemoteDMATransfer, IndirectOffsetOnAxis
-from concourse.mybir import dt, AluOpType, AxisListType, ActivationFunctionType
+from concourse.mybir import dt, AluOpType, ActivationFunctionType
 
 C, ROUNDS, STEP = 320, 3, [4, 1, 2]
-CUT = [0, 128, 320]
-CX = [0, 192, 320]
-QUART = 80
 MID = 160
 NS, WW = 21, 336
-SLOT = [1, 7, 2, 0, 3, 5, 4, 6]
-ID, EB, DD, EA = 0, WW, 2 * WW, 3 * WW
-VV = [4 * WW] + [4 * WW + 352 + WW * s for s in range(7)]
-EC, ED = 24 * 7, 24 * 8
-AWAY = 16
-RUN = 8
+SLOT = [1, 6, 2, 5, 3, 7, 4, 0]
+GATHERS = "EA M0 X0 G1 M1 X1 M2 X2 M3 X3 G4 M4 X4 M5 X5".split()
+TURNED = {"X2": ("x2", 1, 1), "X3": ("x3", 0, 4)}
+AT, TILE = {"ID": 0}, {n: 32 * k + 4 for k, n in enumerate(GATHERS + ["MIX", "TH"])}
+for _a, _b in zip(["ID"] + GATHERS, GATHERS + ["END"]):
+    AT[_b] = AT[_a] + WW + 16 * (_a[0] == "M" or _a in TURNED)
+HELD = {"k1": ("t0", 0), "w1": ("t0", 1), "w2": ("t0", 2), "k2": ("t1", 1), "k3": ("t2", 2), "w4": ("x2", 1), "k4": ("t3", 3), "L2": ("t3", 1), "L3": ("t3", 2), "w5": ("x3", 0),
+        "k5": ("t4", 1), "L5": ("t4", 2), "L4": ("t4", 3), "k6": ("t5", 0), "e6": ("X0", 0), "L1": ("X0", 2), "L0": ("X0", 3)}
+LANES = {"G1": "L0.X0 k1.M0 w1.M0 k1.M0", "M1": "k1.G1 k1.G1 k1.G1 k1.G1", "X1": "k1.M1 L1.X0 k1.M1 w2.M1", "M2": "w2.X1 k2.X1 k2.X1 k2.X1", "X2": "k2.M2 k2.M2 e6.ID k2.M2",
+         "M3": "k2.X2 k2.EA k3.EA k3.X2", "X3": "k3.M3 - - -", "G4": "w4.X3 k4.X2 k4.M3 -", "M4": "k4.G4 k4.G4 k4.G4 k4.EA", "X4": "k4.M4 - w5.M4 -",
+         "M5": "k5.X4 - k5.X4 -", "X5": "- - - -"}
+TILE["X5"], START = TILE["M5"], {"M0": AT["EA"], "X5": AT["M5"] - AT["X4"]}
+PAIRED = {"M1": (2, "M1", 0), "X2": (0, "M2", 2), "M3": (0, "M2", 2), "M4": (2, "M4", 0)}
+CX = [0, 192, 320]
+CZ = [0, 192, 320]
+RUNS = [[0, 8, 22]] * 6
 FIRST = [("S", 0, 4), ("V", 4, 8), ("S", 8, 14), ("V", 14, NS)]
 SECOND = [("V", 0, 8), ("S", 10, NS), ("V", 8, 10)]
-CZ = [0, 192, 320]
-LAST = [[("S", 0, 4), ("V", 4, 8), ("S", 8, 14), ("V", 14, 20)], [("S", 0, 6), ("V", 6, 12), ("S", 12, 16), ("V", 16, 20)]]
-UNPACK = [[(0, 0), (0, 1), (0, 2), (1, 0), (1, 1), (0, 3), (1, 2), (1, 3)], [(k % 2, k // 2) for k in range(8)]]
-ADDS = [4, 8, 6]
-AHEAD = [True, True, False]
-CS = CX
-OUTS = "VSSVSVSV"
-LAID = [("S", 0, 0), ("V", 0, 1), ("S", 0, 2), ("V", 0, 3), ("S", 1, 0)]
-LAID2 = [("S", 1, 2), ("V", 1, 1), ("S", 1, 3)]
-OUTS2 = "SSSVSVSV"
-ZED = [((("V", 1, 0),), (("S", 1, 3), ("V", 1, 1)))] * 2
-PIECES = [(0, 0, 64, 0, 0), (0, 64, 128, 0, 1), (0, 128, 320, 1, 0), (1, 0, 320, 1, 1)]
-PARTS = [(0, 6, 1), (6, 12, 0), (12, 16, 13), (16, 21, 12)]
+BESIDE = [("S", 0, 16), ("V", 16, NS)]
+XRUNS = [0, 352]
+WHOLE = [0, 1, 2, 3, 4]
+SHARE = {n: SECOND if n[0] == "M" else FIRST for n in GATHERS}
+SHARE.update(EA=[("S", 0, 10), ("V", 10, 18), ("S", 18, NS)], X0=[("S", 0, 4), ("S", 4, NS)], X1=[("S", 0, 14), ("V", 14, NS)], X2=[("S", 0, 14), ("V", 14, NS)], X3=[("S", 0, 18), ("V", 18, NS)],
+             X4=[("S", 0, 14), ("V", 14, NS)], X5=[("S", 0, 14), ("V", 14, NS)],
+             G1=[("V", 0, 8), ("S", 8, NS)], G4=[("V", 0, 10), ("S", 10, NS)], M2=[("V", 0, 10), ("S", 10, NS)], M5=[("V", 0, 10), ("S", 10, NS)])
+TABS = 1
+CONV = "E0 M0 E1 M1 g m2 X0 X1"
+CS = [[0, 192, 320]] * 3
+UNPACK = [0, 1, 2, 3, 4, 5, 6, 7]
+SCAT, SCATC = [0, 6, 12, 20], 4
+ADDS = [8, 8, 8]
+LAST = [("S", 0, 6), ("V", 6, 12), ("S", 12, 16), ("V", 16, 20)]
+BACK, SPLIT = True, 0
+CF = [0, 128, 320]
+ZED = ["0V 1V 2S 3S 4S 0q 5S 6S 7S 1q", "0V 1V 2S 3S 4S 0q 5S 6S 7V 1q", "0V 1S 2V 3S 5S 0q 7V 6V 4S 1q"]
+OUTS = ["0S 1S 2S 4V 3V 5S 6V 7V", "0V 1S 2V 3S 4V 5S 6V 7V", "2V 3S 0S 1S 0q 4S 5S 7S 6S 1q"]
+if not BACK:
+    ZED[2], OUTS[2] = ZED[1], OUTS[1]
+LAID = ["0V 4S 1S 2V 3S 5S 0q 6S 7V 1q"] * 3
+AWAY = "0V 1S 2V 3S 4V 5S 6S 7S"
+HOME = "4S 0S 2V 1S 3V 5S 7V 6S 0q 1q"
 SCANS = [(0, 192), (192, 384), (384, 512), (512, 672)]
-LEVEL = SECOND
-OPEN = [("S", 0, 12), ("V", 12, NS)]
-OWN = False
-LOADS = "ulm01"
+LOADS = "lm01"
+TAB1 = [("S", 0, NS)]
+TAB2 = [("S", 0, NS)]
+LATE, WS, U2S, XL, XG = 0, 5, "S", 2.0, 4
+XCUT = [0, 160, 320]
+WCUT = [0, 2, 4, 8, 16, 24, 28, 32]
+MARGIN = 0.3
+XS = 160
+CYC, GAT, WAKE, TRIP = 0.00087, 1.5, 0.2, 1.1
 X4 = "float8_e4m3fn_x4"
 SCRATCH = {
     "xi": ("sbuf", [128, 4 * C], "bfloat16"), "xp": ("sbuf", [128, 4 * C], "bfloat16"),
-    "zt": ("sbuf", [128, 4 * C], "bfloat16"), "ht": ("sbuf", [128, 4 * C], "bfloat16"),
+    "zt": ("sbuf", [128, 4 * C], "bfloat16"), "ht": ("sbuf", [128, 4 * C], "bfloat16"), "hp": ("sbuf", [128, 4 * C], "bfloat16"),
     "ut": ("sbuf", [128, 512], "bfloat16"), "vt": ("sbuf", [128, 512], "bfloat16"),
-    "icb": ("sbuf", [128, 520], "float32"), "icd": ("sbuf", [128, 520], "bfloat16"), "et": ("sbuf", [128, 6 * 520], "bfloat16"), "hp": ("sbuf", [128, 4 * C], "bfloat16"),
+    "icd": ("sbuf", [128, 520], "bfloat16"), "et": ("sbuf", [128, 2 * 520], "bfloat16"),
     "uq": ("sbuf", [128, 128], X4), "us": ("sbuf", [128, 128], "uint8"), "u2q": ("sbuf", [128, 128], X4), "u2s": ("sbuf", [128, 128], "uint8"),
     "vq": ("sbuf", [128, 128], X4), "vs": ("sbuf", [128, 128], "uint8"),
-    "wq": ("sbuf", [128, 512], X4), "wp": ("sbuf", [128, 512], "uint8"),
-    "eq": ("sbuf", [128, 1536], X4), "es": ("sbuf", [128, 1536], "uint8"),
-    "xq": ("sbuf", [128, C], X4), "xs": ("sbuf", [128, C], "uint8"),
-    "zq": ("sbuf", [128, C], X4), "zs": ("sbuf", [128, C], "uint8"),
+    "wq": ("sbuf", [128, 512], X4), "wp": ("sbuf", [128, 512], "uint8"), "w2q": ("sbuf", [128, 512], X4), "w2s": ("sbuf", [128, 512], "uint8"),
+    "eq": ("sbuf", [128, 512], X4), "es": ("sbuf", [128, 512], "uint8"),
+    "xq": ("sbuf", [128, C], X4), "xs": ("sbuf", [128, C], "uint8"), "zq": ("sbuf", [128, C], X4), "zs": ("sbuf", [128, C], "uint8"),
     "ssb": ("sbuf", [128, C], "float32"), "ssm": ("sbuf", [128, C], "float32"),
-    "df": ("sbuf", [128, 352], "bfloat16"), "tu": ("sbuf", [128, 352 + C], "bfloat16"), "tq": ("sbuf", [128, 64], "float32"),
-    "d1": ("sbuf", [128, 8 * NS], "float32"), "sc": ("sbuf", [128, 8 * NS], "float32"), "so": ("sbuf", [128, 4], "uint16"),
-    "ct": ("sbuf", [128, 24], "float32"), "lo": ("sbuf", [128, 48], "float32"), "cq": ("sbuf", [128, 64], "float32"), "mq": ("sbuf", [128, 64], "float32"),
-    "dq": ("sbuf", [128, 48], "float32"), "ng": ("sbuf", [128, 48], "float32"),
-    "mtt": ("sbuf", [128, 48], "int32"), "lab": ("sbuf", [128, 24], "int32"), "pi": ("sbuf", [128, 8], "int32"), "pm": ("sbuf", [128, 24], "float32"),
-    "mo": ("sbuf", [128, 24], "uint16"), "lh": ("sbuf", [128, 48], "uint16"), "uo": ("sbuf", [128, 8], "uint16"),
-    "ea": ("sbuf", [128, 24], "uint16"), "eb": ("sbuf", [128, 24], "uint16"), "uf": ("sbuf", [128, 8], "float32"),
-    "kk": ("sbuf", [128, 24 * 9], "uint16"), "wo": ("sbuf", [128, 32], "uint16"), "wi": ("sbuf", [128, 32], "float32"),
-    "tm": ("sbuf", [128, C], "bfloat16"), "w2q": ("sbuf", [128, 512], X4), "w2s": ("sbuf", [128, 512], "uint8"), "pa": ("sbuf", [128, 24], "uint16"), "pb": ("sbuf", [128, 24], "uint16"),
-    "idn": ("sbuf", [128, WW], "bfloat16"), "wb": ("sbuf", [128, VV[7]], "bfloat16"), "uu": ("sbuf", [128, 352], "bfloat16"),
-    "aw": ("sbuf", [128, WW], "bfloat16"), "glo": ("sbuf", [128, 352], "bfloat16"), "ghi": ("sbuf", [128, 352], "bfloat16"),
-    "tlo": ("sbuf", [128, 352], "bfloat16"), "thi": ("sbuf", [128, 352], "bfloat16"),
+    "df": ("sbuf", [128, 352], "bfloat16"), "tu": ("sbuf", [128, 352 + C], "bfloat16"),
+    "d1": ("sbuf", [128, 8 * NS], "float32"), "sc": ("sbuf", [128, 208], "float32"),
+    "tq": ("sbuf", [128, 96], "float32"), "cr": ("sbuf", [128, 40], "float32"), "cp": ("sbuf", [128, 40], "float32"),
+    "cq": ("sbuf", [128, 64], "float32"), "mq": ("sbuf", [128, 64], "float32"), "dq": ("sbuf", [128, 48], "float32"), "ng": ("sbuf", [128, 96], "float32"),
+    "mtt": ("sbuf", [128, 64], "int32"), "lab": ("sbuf", [128, 24], "int32"), "pi": ("sbuf", [128, 8], "int32"), "pm": ("sbuf", [128, 24], "float32"), "pd": ("sbuf", [128, 8], "float32"),
+    "so": ("sbuf", [128, 4], "uint16"), "sx": ("sbuf", [128, 10], "uint16"), "mo": ("sbuf", [128, 32], "uint16"), "uo": ("sbuf", [128, 8], "uint16"),
+    "sy": ("sbuf", [128, 2], "uint16"), "lr": ("sbuf", [128, 24], "uint16"), "li": ("sbuf", [128, 32], "uint16"),
+    "uf": ("sbuf", [128, 8], "float32"), "kk": ("sbuf", [128, 32 * len(TILE) + 4], "uint16"), "wo": ("sbuf", [128, 32], "uint16"), "wi": ("sbuf", [128, 32], "float32"),
+    "idn": ("sbuf", [128, WW], "bfloat16"), "wb": ("sbuf", [128, AT["END"]], "bfloat16"), "uu": ("sbuf", [128, 352], "bfloat16"), "tm": ("sbuf", [128, C], "bfloat16"),
     "idf": ("sbuf", [128, C], "float32"), "llw": ("sbuf", [128, C], "float32"), "ysb": ("sbuf", [128, C], "float32"),
-    "rlq": ("sbuf", [128, C], X4), "rls": ("sbuf", [128, C], "uint8"),
+    "rlq": ("sbuf", [128, C], X4), "rls": ("sbuf", [128, C], "uint8"), "rll": ("sbuf", [128, 24], "uint16"),
     "ps": ("psum", [128, 4096], "float32"),
 }
-for _k in range(7):
-    SCRATCH["t%d" % _k] = ("sbuf", [128, 352], "bfloat16")
+for _k in "t0 t1 t2 t3 t4 t5 x2 x3".split():
+    SCRATCH[_k] = ("sbuf", [128, 352], "bfloat16")
 for _r in range(ROUNDS):
     SCRATCH["ls%d" % _r] = SCRATCH["pn%d" % _r] = ("sbuf", [128, 24], "uint16")
-    for _n in ("hq", "ld", "ga", "gb"):
+    for _n in ("hq", "ld"):
         SCRATCH["%sc%d" % (_n, _r)] = ("sbuf", [128, C], X4)
         SCRATCH["%ss%d" % (_n, _r)] = ("sbuf", [128, C], "uint8")
 QUEUES = ("V", "S", "P", "G")
-SEMAPHORES = (["qV", "qS", "qP", "qG"] + ["dm%d" % k for k in range(8)] + ["arr%d%d" % (r, k) for r in range(ROUNDS) for k in range(2)] + ["sent%d" % r for r in range(ROUNDS)]
-              + ["list%d" % r for r in range(ROUNDS)] + ["hop0", "hop1", "hop2", "hop3", "hop4", "hop5", "hopsent", "stored"])
+SEMAPHORES = (["qV", "qS", "qP", "qG"] + ["dm%d" % k for k in range(8)] + ["arr%d%d" % (r, k) for r in range(ROUNDS) for k in range(3)] + ["sent%d" % r for r in range(ROUNDS)]
+              + ["hop%d" % k for k in range(6)] + ["hopsent", "stored"])
+PLAN = {}
+
+
+def pieces(far, r):
+    lists = ([] if BACK else [(0, "l", 0, 10, 0), (0, "l", 10, 20, 1)]) if far else [(0, "l", 0, 20, 0)]
+    cut = CF if far and BACK else CS[r]
+    if far and SPLIT:
+        return lists + [(1, "c", 0, cut[1], 0), (1, "s", 0, cut[1], 1), (2, "c", SPLIT, C, 1), (2, "c", cut[1], SPLIT, 0), (2, "s", cut[1], C, SPLIT % 4 // 2)]
+    return lists + [(1 + h, kind, cut[h], cut[h + 1], (h + k) % 2) for h in range(2) for k, kind in enumerate("cs")]
+
+
+def side(T, names, piece):
+    kind, a, b = piece[1:4]
+    ap = T[names["lcs".index(kind)]][:, a:b]
+    return ap.bitcast(dt.uint8) if kind == "c" else ap
 
 
 def relays(core, dst, T, topo):
     return [c for c in topo.cores_of(core) if c != core and T.rank_of(c) is None and topo.die(c) == topo.die(core) and topo.may_write(c, dst)][:2]
-
-
-def piece(T, k, codes, plane):
-    kind, a, b = PIECES[k][:3]
-    return T[plane][:, a:b] if kind else T[codes][:, a:b].bitcast(dt.uint8)
 
 
 def hand_on(g, core, T, topo):
@@ -89,12 +116,36 @@ def hand_on(g, core, T, topo):
             src, dst = T.cores[i], T.cores[i ^ s]
             if topo.may_write(src, dst) or core not in relays(src, dst, T, topo):
                 continue
-            mine = [k for k, p in enumerate(PIECES) if relays(src, dst, T, topo)[p[4]] == core]
+            mine = [(k, p) for k, p in enumerate(pieces(True, r)) if relays(src, dst, T, topo)[p[4]] == core]
             rid, pid = topo.addr(dst, core)
-            for k in mine:
+            for k, p in mine:
                 g.wait_ge(T.sem["hop%d" % k], len(topo.engines(src, core)))
-                g.remote_dma(piece(T, k, "ldc%d" % r, "lds%d" % r), piece(T, k, "rlq", "rls"), T.sem["arr%d%d" % (r, PIECES[k][0])], T.sem.hopsent, pid, rid, topo.mask(core, dst))
+                g.remote_dma(side(T, ["pn%d" % r, "ldc%d" % r, "lds%d" % r], p), side(T, ["rll", "rlq", "rls"], p), T.sem["arr%d%d" % (r, p[0])], T.sem.hopsent, pid, rid, topo.mask(core, dst))
             g.wait_ge(T.sem.hopsent, len(mine) * len(topo.engines(core, dst)))
+
+
+def plan(nodes):
+    busy, start, end = {}, {}, {}
+
+    def place(i):
+        n = nodes[i]
+        for p in n["pre"] + n["after"]:
+            if p not in end:
+                place(p)
+        t = max([0.0] + [end[p] + WAKE for p in n["pre"]] + [end[p] - nodes[p]["lat"] for p in n["after"]])
+        if n["q"]:
+            slots, room = busy.setdefault(n["q"], []), n["cost"] * (1 + MARGIN * n["spare"])
+            for a, b in slots:
+                if t + room <= a + 1e-9:
+                    break
+                t = max(t, b)
+            slots.append((t, t + n["cost"]))
+            slots.sort()
+        start[i], end[i] = t, t + n["cost"] + n["lat"]
+    for i in sorted(range(len(nodes)), key=lambda i: (nodes[i]["spare"], i)):
+        if i not in end:
+            place(i)
+    return sorted(range(len(nodes)), key=lambda i: (start[i], i))
 
 
 def rank_program(g, core, T, topo):
@@ -103,8 +154,7 @@ def rank_program(g, core, T, topo):
         return hand_on(g, core, T, topo)
     A, AF = AluOpType, ActivationFunctionType
     eng = {"V": g.vector, "S": g.scalar, "P": g.tensor, "G": g, "Y": g.sync}
-    cnt, known, snap = {}, {q: {} for q in eng}, {}
-    writers, readers = [], []
+    nodes, writers, readers, spare, strict = [], {}, {}, [0], [0]
 
     def R(name, c0=0, c1=None, step=1, p0=0, p1=128, cast=None):
         c1 = (C if c1 is None else c1)
@@ -114,88 +164,85 @@ def rank_program(g, core, T, topo):
         return ((name, p0, p1, c0, c1, step), ap)
 
     def hit(a, b):
-        return (a[0] == b[0] and a[1] < b[2] and b[1] < a[2] and a[3] < b[4] and b[3] < a[4]
-                and not (a[5] == b[5] and a[5] > 1 and (a[3] - b[3]) % a[5]))
+        return a[1] < b[2] and b[1] < a[2] and a[3] < b[4] and b[3] < a[4] and not (a[5] == b[5] and a[5] > 1 and (a[3] - b[3]) % a[5])
 
     def inside(a, b):
-        return a[0] == b[0] and b[1] <= a[1] and a[2] <= b[2] and b[3] <= a[3] and a[4] <= b[4] and (b[5] == 1 or (a[5] == b[5] and (a[3] - b[3]) % a[5] == 0))
+        return b[1] <= a[1] and a[2] <= b[2] and b[3] <= a[3] and a[4] <= b[4] and (b[5] == 1 or (a[5] == b[5] and (a[3] - b[3]) % a[5] == 0))
 
-    def waits(q, W, Rd, own_waw=True):
-        need = {}
-        for r in Rd:
-            for (b, s, n) in writers:
-                if hit(r[0], b):
-                    need[s] = max(need.get(s, 0), n)
-        for w in W:
-            for (b, s, n) in writers + readers:
-                if hit(w[0], b) and (own_waw or s != "q" + q):
-                    need[s] = max(need.get(s, 0), n)
-        k = known[q]
-        need = {s: n for s, n in need.items() if k.get(s, 0) < n}
-        for s in list(need):
-            for s2 in list(need):
-                if s2 != s and s in need and snap.get((s2, need[s2]), {}).get(s, 0) >= need[s]:
-                    del need[s]
-        for s, n in need.items():
-            eng[q].wait_ge(T.sem[s], n)
-            for a, b in snap.get((s, n), {}).items():
-                k[a] = max(k.get(a, 0), b)
-            k[s] = max(k.get(s, 0), n)
+    def note(W, Rd, who):
+        for w, _ in W:
+            writers[w[0]] = [e for e in writers.get(w[0], []) if not inside(e[0], w)] + [(w, who)]
+            readers[w[0]] = [e for e in readers.get(w[0], []) if not inside(e[0], w)]
+        for r, _ in Rd:
+            readers.setdefault(r[0], []).append((r, who))
 
-    def note(W, Rd, s, n):
-        for w in W:
-            writers[:] = [e for e in writers if not inside(e[0], w[0])]
-            readers[:] = [e for e in readers if not inside(e[0], w[0])]
-            writers.append((w[0], s, n))
-        for r in Rd:
-            readers[:] = [e for e in readers if not (e[1] == s and inside(e[0], r[0]))]
-            readers.append((r[0], s, n))
+    def add(q, call, W, Rd, cost, lat=0.0, sig=None, pre=(), after=()):
+        pre = set(pre)
+        if "pre" not in PLAN:
+            for r, _ in Rd:
+                pre.update(i for b, who in writers.get(r[0], []) if hit(r, b) for i in who)
+            for w, _ in W:
+                pre.update(i for b, who in writers.get(w[0], []) + readers.get(w[0], []) if hit(w, b) for i in who)
+            note(W, Rd, [len(nodes)])
+        after = list(after) + [i for i in range(len(nodes) - 1, -1, -1) if strict[0] and nodes[i]["q"] == q and not nodes[i]["spare"]][:1]
+        nodes.append({"q": q, "call": call, "cost": cost, "lat": lat, "sig": sig, "pre": sorted(pre), "after": after, "spare": spare[0]})
+        return len(nodes) - 1
 
-    def op(q, call, W, Rd, own_waw=True):
-        waits(q, W, Rd, own_waw)
-        s = "q" + q
-        cnt[s] = cnt.get(s, 0) + 1
-        call().then_inc(T.sem[s], 1)
-        snap[(s, cnt[s])] = dict(known[q])
-        note(W, Rd, s, cnt[s])
+    def aside(f, *args):
+        spare[0] = 1
+        f(*args)
+        spare[0] = 0
 
-    loaded = []
+    def width(a):
+        return len(range(a[0][3], a[0][4], a[0][5]))
 
-    def load(items):
-        s = "dm%d" % len(loaded)
+    def op(q, call, W, Rd, off=None, rate=1.0):
+        n = width(W[0])
+        if off:
+            cost = (0.05 if q == "V" else 0.065) + n * GAT * CYC
+        else:
+            short = q == "V" and all(SCRATCH[a[0][0]][2] in ("bfloat16", "uint16") for a in W + Rd if width(a) > 1)
+            cost = max(64, n * (0.5 if short and rate == 1.0 else rate)) * CYC
+        return add(q, call, W, Rd + ([off] if off else []), cost)
+
+    loaded, stores, rest = [], [0], []
+
+    def load(items, after=()):
+        s, n = "dm%d" % len(loaded), 16 * len(items)
+        loaded.append(n)
+        who = []
         for q, dst, src in items:
-            waits(q, [dst], [])
-            eng[q].dma_start(dst[1], src).then_inc(T.sem[s], 16)
-        loaded.append(16 * len(items))
-        note([dst for q, dst, src in items], [], s, loaded[-1])
+            ap, rd = (src[1], [src]) if isinstance(src, tuple) else (src, [])
+            who.append(add(q, (lambda q=q, dst=dst, ap=ap: eng[q].dma_start(dst[1], ap).then_inc(T.sem[s], 16)), [dst], rd, 0.05, TRIP + width(dst) * 0.001, (s, n), after=after))
+        note([dst for q, dst, src in items], [], who)
+        return who
 
-    stores = [0]
-
-    def store(q, out, src):
-        waits(q, [], [src])
-        eng[q].dma_start(out, src[1]).then_inc(T.sem.stored, 16)
+    def store(q, out, src, pre=()):
         stores[0] += 16
+        add(q, lambda: eng[q].dma_start(out, src[1]).then_inc(T.sem.stored, 16), [], [src], 0.05, TRIP, ("stored", 0), pre)
+
+    def at(a, off):
+        return a[1] if off is None else a[1].indirect(off[1])
 
     def tt(o, a, b, f, off=None):
-        op("V", lambda: g.vector.tensor_tensor(o[1], a[1] if off is None else a[1].indirect(off[1]), b[1], f), [o], [a, b] + ([off] if off else []))
+        op("V", lambda: g.vector.tensor_tensor(o[1], at(a, off), b[1], f), [o], [a, b], off, 1.001 if "ps" in (a[0][0], b[0][0]) else 2.0)
 
-    def ts(o, a, s1, f, s2=None, f2=None, own=True):
+    def ts(o, a, s1, f, s2=None, f2=None, off=None):
         cols = [s for s in (s1, s2) if isinstance(s, tuple)]
         v1, v2 = [s[1] if isinstance(s, tuple) else s for s in (s1, s2)]
         if f2 is None:
-            op("V", lambda: g.vector.tensor_scalar(o[1], a[1], v1, None, f), [o], [a] + cols, own)
+            op("V", lambda: g.vector.tensor_scalar(o[1], at(a, off), v1, None, f), [o], [a] + cols, off)
         else:
-            op("V", lambda: g.vector.tensor_scalar(o[1], a[1], v1, v2, f, f2), [o], [a] + cols)
+            op("V", lambda: g.vector.tensor_scalar(o[1], at(a, off), v1, v2, f, f2), [o], [a] + cols, off)
 
-    def cp(q, o, a, off=None, scale=None):
-        src = a[1] if off is None else a[1].indirect(off[1])
-        rd = [a] + ([off] if off else [])
+    def cp(q, o, a, off=None, scale=None, bias=None, func=None):
         if q == "V":
-            op("V", lambda: g.vector.tensor_copy(o[1], src), [o], rd)
-        elif scale is not None:
-            op("S", lambda: g.scalar.activation(o[1], src, AF.Copy, scale=scale), [o], rd)
-        else:
-            op("S", lambda: g.scalar.activation(o[1], src, AF.Copy), [o], rd)
+            return op("V", lambda: g.vector.tensor_copy(o[1], at(a, off)), [o], [a], off)
+        kw = {k: (v[1] if isinstance(v, tuple) else v) for k, v in (("scale", scale), ("bias", bias)) if v is not None}
+        cols = [v for v in (scale, bias) if isinstance(v, tuple)]
+        if func is None:
+            func = AF.Identity if cols or bias is not None else AF.Copy
+        return op("S", lambda: g.scalar.activation(o[1], at(a, off), func, **kw), [o], [a] + cols, off)
 
     def tr(o, a):
         op("V", lambda: g.vector.transpose(o[1], a[1]), [o], [a])
@@ -204,427 +251,388 @@ def rank_program(g, core, T, topo):
         op("V", lambda: g.vector.memset(o[1], v), [o], [])
 
     def iota(o, pat, base, cm, whole=False):
-        if whole:
-            op("G", lambda: g.iota(o[1], pat, base, cm), [o], [])
-        else:
-            op("G", lambda: g.iota(o[1], pat, base, cm, allow_small_or_imprecise_dtypes=True), [o], [])
+        kw = {} if whole else {"allow_small_or_imprecise_dtypes": True}
+        add("G", lambda: g.iota(o[1], pat, base, cm, **kw), [o], [], 0.13 + 2 * CYC * width(o))
+
+    def scan(o, d0, d1):
+        op("V", lambda: g.vector.tensor_tensor_scan(o[1], d0[1], d1[1], 0.0, A.mult, A.add), [o], [d0, d1])
 
     def quant(qc, qs, a, b, tile, ta=None):
         ta = 4 * a if ta is None else ta
         o, s, i = R(qc, a, b), R(qs, a, b), R(tile, ta, ta + 4 * (b - a))
-        op("V", lambda: g.vector.quantize_mx(o[1], s[1], i[1]), [o, s], [i])
+        add("V", lambda: g.vector.quantize_mx(o[1], s[1], i[1]), [o, s], [i], 0.014 + 0.001 * (b - a))
 
-    def bank(k, cut=CX):
-        return R("ps", 512 * k, 512 * k + cut[k // 4 + 1] - cut[k // 4])
+    def bank(k, n):
+        return (("ps", 0, 128, 512 * k, 512 * k + n, 1), T.ps[:, 512 * k:512 * k + n])
 
-    def mm(k, lq, lsc, la, rq, rsc, start=True, stop=True, cut=CX):
-        o, r0, r1 = bank(k, cut), cut[k // 4], cut[k // 4 + 1]
-        a, b, c, d = R(lq, la, la + 128), R(lsc, la, la + 128), R(rq, r0, r1), R(rsc, r0, r1)
-        op("P", lambda: g.tensor.matmul_mx(o[1], a[1], b[1], c[1], d[1], start, stop), [o], [a, b, c, d], own_waw=start)
+    def mm(k, lq, lsc, la, rq, rsc, r0, r1):
+        o, a, b, c, d = bank(k, r1 - r0), R(lq, la, la + 128), R(lsc, la, la + 128), R(rq, r0, r1), R(rsc, r0, r1)
+        add("P", lambda: g.tensor.matmul_mx(o[1], a[1], b[1], c[1], d[1], True, True), [bank(k, 512)], [a, b, c, d], (r1 - r0 + 16) * CYC * 1.2)
 
-    def shift(b, n=1):
-        return R("pm", 0, 1, 1, 32 * b, 32 * (b + n))
+    def col(n, k, b=0, blocks=4):
+        return R(n, k, k + 1, 1, 32 * b, 32 * (b + blocks))
 
-    def gather(shares, out, at, win, w0, w1, off, o0=0):
+    def shift(b=0, n=4):
+        return col("pm", 0, b, n)
+
+    def tile(t, b=0, n=4, a=0, e=NS):
+        return R("kk", TILE[t] + a, TILE[t] + e, 1, 32 * b, 32 * (b + n))
+
+    def gather(shares, name, w0=0, w1=None, out=None):
+        out, o0 = out or ("wb", AT[name])
         for e, a, b in shares:
-            cp(e, R(out, at + 16 * a, at + 16 * b), R(win, w0, w1), R(off, o0 + a, o0 + b))
+            cp(e, R(out, o0 + 16 * a, o0 + 16 * b), R("wb", w0, w1 or AT[name]), tile(name, 0, 4, a, b))
 
-    def from_scan(side, parts):
-        for i0, i1, c0 in parts:
-            ts(R(("ea", "eb")[side], c0, c0 + 2 * (i1 - i0) - 1, 2), R("sc", 8 * i0 + 4 * side + 2, 8 * i1, 8), shift(0, 4), A.add)
+    def offsets(name, lists, a=0, b=NS):
+        lanes = LANES[name].split()
+        to, src, frm = PAIRED.get(name, (9, None, 0))
+        for to, lane in [(k, lane) for k, lane in enumerate(lanes) if k // 2 != to // 2]:
+            if lane[:2] in lists:
+                (buf, src), base = HELD[lane[:2]], AT[lane[3:]]
+                if buf in TILE:
+                    ts(tile(name, to, 1, a, b), tile(buf, src, 1, a, b), float(base), A.add)
+                else:
+                    ts(tile(name, to, 1, a, b), R(buf, 16 * a, 16 * b, 16, 32 * src, 32 * src + 32), float(MID + base), A.add, shift(src, 1), A.add)
+        if name in PAIRED and lanes[PAIRED[name][0]][:2] in lists:
+            to, src, frm = PAIRED[name]
+            ts(tile(name, to, 2), tile(src, frm, 2), col("pd", 2 * list(PAIRED).index(name), frm, 2), A.add)
 
-    def move(dst, to, src, at, n=1, c0=0):
-        cp("V", R(dst, c0, c0 + NS, 1, 32 * to, 32 * (to + n)), R(src, 0, NS, 1, 32 * at, 32 * (at + n)))
+    def turn(s, between):
+        runs = RUNS[s]
+        for a, b in zip(runs, runs[1:]):
+            tr(R("t%d" % s, 16 * a, 16 * b), R("wb", AT["M%d" % s] + 16 * a, AT["M%d" % s] + 16 * b))
+        between()
+        if s == 5:
+            for k, w in enumerate(("X2", "X5")):
+                ts(R("kk", TILE["MIX"] + k, TILE["MIX"] + 20, 2, 64, 96), R("t5", 16, C, 32, 0, 32), float(MID + AT[w]), A.add, shift(0, 1), A.add)
+            return
+        runs = [0, NS] if s in WHOLE else runs
+        for a, b in zip(runs, runs[1:]):
+            offsets(GATHERS[GATHERS.index("X%d" % s) + 1], [n for n in HELD if HELD[n][0] == "t%d" % s], a, min(b, NS))
 
-    def turn(s, src, at, cut, p1=128):
-        for a, b in ((0, cut), (cut, NS + 1)):
-            tr(R("t%d" % s, 16 * a, 16 * b, 1, 0, p1), R(src, at + 16 * a, at + 16 * b, 1, 0, p1))
+    def others(buf, first):
+        for name in GATHERS[GATHERS.index(first) + 1:]:
+            spare[0] = int(GATHERS.index(name) > GATHERS.index(first) + 1)
+            offsets(name, [n for n in HELD if HELD[n][0] == buf])
+        spare[0] = 0
 
-    def from_turn(s, to, src, base, a, b, use=None):
-        use = s + 1 if use is None else use
-        ts(R("kk", 24 * use + a, 24 * use + b, 1, 32 * to, 32 * to + 32), R("t%d" % s, 16 * a, 16 * b, 16, 32 * src, 32 * src + 32), float(MID + base), A.add, shift(src), A.add)
-
-    HELD = {0: 1, 1: 0, 2: 1, 3: 2, 4: 3, 5: 0, 6: 3, 7: 0}
-
-    def plain(dst, to, li, first, a=0, b=20, own=True):
-        n, k, src = (16, 1, HELD[li]) if first else (32, 0, HELD[li])
-        o = R(dst, a, b, 1, 32 * to, 32 * to + n)
-        if li < 2:
-            ts(o, R("eb", k + a, k + b, 1, 32 * src, 32 * src + n), -16.0 * k, A.add)
+    def own(ls, li):
+        n, k, (buf, src), to = 32 if li % 2 else 16, 1 - li % 2, HELD["L%d" % li], li // 2
+        o = R(ls, 0, 20, 1, 32 * to, 32 * to + n)
+        if buf in TILE:
+            ts(o, R("kk", TILE[buf] + k, TILE[buf] + k + 20, 1, 32 * src, 32 * src + n), -16.0 * k, A.add)
         else:
-            ts(o, R("t%d" % min(max(li, 3), 6), 16 * (k + a), 16 * (k + b), 16, 32 * src, 32 * src + n), float(MID), A.add, own=own)
+            ts(o, R(buf, 16 * k, 16 * (k + 20), 16, 32 * src, 32 * src + n), float(MID), A.add)
 
-    def order_tables(q="V"):
-        low, high, at = R("tq", 0, NS, 1, 0, 64), R("tq", 32, 32 + NS, 1, 0, 64), [R("d1", 4 + k, 8 * NS, 8, 0, 64) for k in range(3)]
-        return [lambda: tr(R("tlo", 0, 352), R("glo", 0, 352)), lambda: tr(R("thi", 0, 352), R("ghi", 0, 352)),
-                lambda: cp(q, R("tq", 0, 32), R("tlo", 0, 352), R("so", 2, 4)), lambda: cp(q, R("tq", 32, 64), R("thi", 0, 352), R("so", 2, 4)),
-                lambda: op("S", lambda: g.scalar.activation(at[2][1], low[1], AF.Identity, bias=float(MID)), [at[2]], [low]), lambda: tt(at[1], high, low, A.subtract),
-                lambda: tt(at[0], at[1], R("ng", 1, 2 * NS, 2, 0, 64), A.mult)]
+    def order_tables(mine):
+        far, gap, to = R("tq", 0, NS, 1, 64), R("tq", 64, 64 + NS, 1, 64), [R("d1", 4 + k, 8 * NS, 8, 64) for k in range(3)]
+        cp("S", R("tq", 0, 32), R("x3", 0, 352), R("so", 2, 4), bias=col("pm", 1))
+        tt(gap, far, mine, A.subtract)
+        tt(to[0], gap, R("ng", 48, 48 + NS, 1, 64), A.mult)
+        tt(to[1], gap, R("ng", 72, 72 + NS, 1, 64), A.mult)
+        tt(to[2], far, to[0], A.add)
 
-    fill(R("mtt", 0, 48), 0)
+    def scores(h, first=False):
+        a, b = CX[h], CX[h + 1]
+        quant("xq", "xs", a, b, "xi")
+        for k in range(h + 1):
+            mm(4 * h + k, "u2q", "u2s", 0, "xq", "xs", a, b)
+        if h == 0:
+            cp("S", R("ssb", a, b), bank(0, b - a), scale=col("pm", 8))
+        else:
+            ts(R("ssb", a, b), bank(4, b - a), col("pm", 8), A.mult)
+        cp("S", R("ssm", a, b), bank(5 * h, b - a), scale=col("pm", 8), bias=col("pm", 10))
+        done = len(nodes) - 1
+        for t in range(XG * h if first else 0):
+            o, i = R("xp", C * t, C * t + C), R("xi", t, 4 * C, 4)
+            add("G", lambda o=o, i=i: g.affine_select(o[1], i[1], [[0, C]], A.is_ge, 0.0, 0, 0), [o], [i], 0.17 + 2 * C * CYC)
+        for t, a in [(t, a) for t in range(XG if first else 0, 4 * h) for a in range(0, C, XS)]:
+            aside(cp, "S", R("xp", C * t + a, C * t + a + XS), R("xi", 4 * a + t, 4 * (a + XS), 4))
+            nodes[-1]["after"].append(done)
+
+    def results(h):
+        a, b = CX[h], CX[h + 1]
+        quant("xq", "xs", a, b, "xi")
+        mm(4 * h, "vq", "vs", 0, "xq", "xs", a, b)
+        store("Y", T.oc[:, 4 * a:4 * b], R("xq", a, b, cast=dt.uint8))
+        cp("SV"[h], R("ysb", a, b), bank(4 * h, b - a))
+        store("S", T.y[:, a:b], R("ysb", a, b))
+
+    fill(R("mtt", 0, 64), 0)
     fill(R("lab", 0, 24), 0)
+    load([("S", R("ut", 0, 512), T.u[:, :])])
     for what in LOADS:
-        if what == "u":
-            load([("S", R("ut", 0, 512), T.u[:, :])])
         if what == "l":
-            load([("YS"[k], R("lab", 1 - k, 21 - k, 1, 32 * b + 16 * k, 32 * b + 16 * k + 16), (T.lb, T.la)[b][:, :]) for b in range(2) for k in range(2)])
-        if what == "m":
-            load([("YS"[k], R("mtt", 24 * side + 1 - k, 24 * side + 21 - k, 1, 32 * b + 16 * k, 32 * b + 16 * k + 16), T.mt[16 * SLOT[2 * b + side]:16 * SLOT[2 * b + side] + 16, :])
-                  for b in range(4) for side in range(2) for k in range(2)])
-        if what in "01":
-            h = int(what)
-            load([("YS"[h], R("xi", 4 * CX[h], 4 * CX[h + 1]), T.x[:, 4 * CX[h]:4 * CX[h + 1]])])
-    load([("Y", R("wq", 0, 512, cast=dt.uint8), T.wc[:, :]), ("Y", R("wp", 0, 512), T.ws[:, :])])
-    load([("Y", R("vt", 0, 512), T.v[:, :])])
+            load([("YS"[k], R("lab", 1 - k, 21 - k, 1, 64 + 32 * b + 16 * k, 64 + 32 * b + 16 * k + 16), (T.lb, T.la)[b][:, :]) for b in range(2) for k in range(2)])
+        elif what == "m":
+            load([("YS"[k], R("mtt", 24 * sd + 1 - k, 24 * sd + 21 - k, 1, 32 * b + 16 * k, 32 * b + 16 * k + 16), T.mt[16 * SLOT[2 * b + sd]:16 * SLOT[2 * b + sd] + 16, :])
+                  for b in range(4) for sd in range(2) for k in range(2)])
+        else:
+            a, b = CX[int(what)], CX[int(what) + 1]
+            load([("YS"[int(what)], R("xi", 4 * a, 4 * b), T.x[:, 4 * a:4 * b])], range(2, len(nodes)))
+            nodes[-1]["lat"] = XL + 0.001 * b
+    load([("Y", R("wq", 0, 512, cast=dt.uint8), T.wc[:, :]), ("Y", R("wp", 0, 512), T.ws[:, :])], range(2, len(nodes)))
+    load([("Y", R("vt", 0, 512), T.v[:, :])], range(2, len(nodes)))
     iota(R("pi", 0, 2), [[0, 2]], 0, 1, True)
     iota(R("idn", 0, WW), [[1, WW]], -MID, 0)
-    iota(R("ct", 0, 24), [[16, 24]], 0, 0)
+    iota(R("cr", 0, 24), [[16, 24]], 0, 0)
     for k, step in ((0, 2), (1, 2), (5, 2)):
         n = 4 if k == 0 else 2
         iota(R("uf", k, k + step * n - 1, step), [[16 * (SLOT[k + step] - SLOT[k]), n]], 16 * SLOT[k], 0)
     iota(R("wi", 0, 32), [[128, 4], [-16, 8]], 112, 0)
-    iota(R("icb", 0, 516), [[1, 516]], 0, 0)
+    iota(R("icd", 0, 516), [[1, 516]], -448, 4)
     iota(R("idf"), [[1, C]], 0, 0)
-    col = lambda n, k: R(n, k, k + 1)
-    fill(R("kk", 0, 24 * 9), 0)
-    for k, m in enumerate((16, 15, 4)):
+    fill(R("kk", TILE["X3"], 32 * len(TILE)), 0)
+    cp("V", tile("X0"), R("lab", 0, NS))
+    for e, a, b in TAB1:
+        cp(e, R("wb", AT["X0"] + 16 * a, AT["X0"] + 16 * b), R("idn", 0, WW), tile("X0", 0, 4, a, b))
+    for k, m in enumerate((16, 15, 4, 1)):
         ts(col("pi", 2 + k), col("pi", 0), m, A.bitwise_and)
     fill(R("d1", 3, 8 * NS, 4), 0.0)
     ts(col("pm", 0), col("pi", 2), 0.0, A.is_equal, 16.0, A.mult)
     cp("V", col("pm", 11), col("pi", 3))
     ts(col("pm", 12), col("pi", 3), 2.0, A.mult, 1.0, A.add)
-    ts(col("pm", 13), col("pi", 3), 2.0, A.mult, 12.0, A.add)
+    ts(col("pm", 13), col("pi", 3), 2.0, A.mult, 8.0, A.min)
     ts(col("pm", 14), col("pi", 3), 6.0, A.is_ge, -13.0, A.mult)
     ts(col("pm", 15), col("pi", 3), 12.0, A.is_ge)
     ts(col("pm", 8), col("pi", 4), -0.5, A.mult, 1.0, A.add)
     ts(col("pm", 10), col("pi", 3), 4.0, A.is_lt, 2.0 ** 90, A.mult)
-    ts(col("pm", 13), col("pm", 13), 20.0, A.min)
-    ts(col("pm", 12), col("pm", 12), col("pm", 14), A.add, col("pm", 15), A.add)
-    ts(R("wb", ID, ID + WW), R("idn", 0, WW), shift(0, 4), A.subtract)
-    ts(R("ct", 0, 24), R("ct", 0, 24), col("pm", 11), A.add, shift(0, 4), A.subtract)
-    cp("V", R("so", 0, 2), R("pm", 12, 14))
-    ts(R("so", 2, 4), R("pm", 12, 14), 16.0, A.mult)
-    for n, a in (("df", 0), ("df", WW), ("uu", C), ("uu", WW), ("glo", WW), ("ghi", WW), ("wb", VV[0] + WW)):
-        cp("S", R(n, a, a + 16), R("idn", MID, MID + 16), scale=0.0)
-    ts(R("kk", ED, ED + NS, 1, 0, 32), R("ct", 0, NS, 1, 0, 32), shift(0), A.add)
-    ts(col("pm", 16), col("pi", 0), 4.0, A.mult, -448.0, A.add)
+    ts(R("wb", 0, WW), R("idn", 0, WW), shift(), A.subtract)
+    ts(col("so", 0), col("pm", 12), col("pm", 14), A.add, col("pm", 15), A.add)
+    ts(col("so", 1), col("pm", 13), 12.0, A.add)
+    ts(R("cp", 0, 24), R("cr", 0, 24), col("pm", 11), A.add)
+    ts(col("pm", 6), col("pm", 0), -23.0 / 16, A.mult, 24.0, A.add)
     cp("V", R("uo", 0, 8), R("uf", 0, 8))
-    ts(R("wo", 0, 32), R("wi", 0, 32), col("pm", 11), A.add)
-    ts(col("pm", 17), col("pm", 11), -8.0, A.mult, col("pm", 16), A.add)
-    for side in range(2):
-        cp("S", R("cq", side, 64, 2), R("ct", 0, 24), R("so", 0, 2))
-    ALL_S = [("S", 0, NS)]
-    ts(R("eb", 0, NS), R("lab", 0, NS), shift(0, 4), A.add)
-    gather(ALL_S, "aw", 0, "wb", ID, ID + WW, "eb")
+    ts(R("so", 2, 4), R("so", 0, 2), 16.0, A.mult)
+    ts(R("sx", 8, 10), R("cp", 0, 2), col("pm", 6), A.add)
+    cp("S", col("pm", 1), col("pm", 0), bias=float(MID))
+    for sd in range(2):
+        cp("S", R("cq", sd, 64, 2), R("cp", 0, 24), R("so", 0, 2))
+    for n, a in [("uu", WW), ("df", 0), ("df", WW)] + [("wb", AT[k] + WW) for k in GATHERS if k[0] == "M" or k in TURNED]:
+        aside(cp, "S", R(n, a, a + 16), R("cr", 0, 16), None, 0.0)
+    spare[0] = 1
+    for k, (name, (to, src, frm)) in enumerate(PAIRED.items()):
+        for b in range(2):
+            cp("S", col("pd", 2 * k, frm + b, 1), col("cr", 0, frm + b, 1), scale=0.0, bias=float(AT[LANES[name].split()[to + b][3:]] - AT[LANES[src].split()[frm + b][3:]]))
+    for h, (odd, most) in enumerate(((-18.0, 90.0), (-2.0, 66.0))):
+        ts(col("pm", 2 + h), col("pi", 5), odd - 34.0, A.mult, 34.0, A.add)
+        cp("S", col("pm", 4 + h), col("pm", 11), scale=4.0, bias=col("pm", 2 + h))
+        for sd in range(2):
+            ts(col("sx", 4 * sd + 2 * h), col("pm", 4 + h), most, A.min, 4.0 * sd, A.add)
+    spare[0] = 0
+    ts(tile("TH", 2, 2), R("mtt", 24, 24 + NS, 1, 64), shift(2, 2), A.add)
     quant("uq", "us", 0, 128, "ut")
-    tt(R("lo", 0, NS), R("mtt", 24, 24 + NS), R("ct", 0, NS), A.min)
-    tt(R("lo", 24, 24 + NS), R("mtt", 24, 24 + NS), R("ct", 0, NS), A.max)
     cp("V", R("u2q", 0, 128, cast=dt.uint32), R("uq", 0, 128, cast=dt.uint32), R("uo", 0, 8))
-    ts(R("lh", 0, NS), R("lo", 0, NS), shift(0, 4), A.add)
-    ts(R("lh", 22, 22 + NS), R("lo", 24, 24 + NS), shift(0, 4), A.add)
-    cp("S", R("u2s", 0, 128), R("us", 0, 128), R("uo", 0, 8))
-    gather(ALL_S, "glo", 0, "aw", 0, WW, "lh")
-    gather(ALL_S, "ghi", 0, "aw", 0, WW, "lh", 22)
-    for side in range(2):
-        cp("V", R("mq", side, 64, 2), R("mtt", 24 * side, 24 * side + 24), R("so", 0, 2))
-    cp("V", R("mo", 0, 20), R("mtt", 24, 44))
+    cp(U2S, R("u2s", 0, 128), R("us", 0, 128), R("uo", 0, 8))
+    gather(TAB2, "TH", AT["X0"], AT["G1"], ("uu", 0))
+    tr(R("x3", 0, 352), R("uu", 0, 352))
+    scores(0)
+    scores(1, True)
+    cp("V", R("mo", 0, 32), R("mtt", 0, 64), R("sx", 8, 10))
+    spare[0] = LATE
+    for sd in range(2):
+        ts(R("mq", sd, 64, 2), R("mtt", 24 * sd, 24 * sd + 24), shift(), A.add, off=R("so", 0, 2))
     tt(R("dq", 0, 2 * NS), R("cq", 0, 2 * NS), R("mq", 0, 2 * NS), A.subtract)
     tt(R("d1", 2, 8 * NS, 4), R("cq", 0, 2 * NS), R("mq", 0, 2 * NS), A.min)
-    tt(R("ng", 0, 2 * NS), R("cq", 0, 2 * NS), R("mq", 0, 2 * NS), A.max)
-    quant("xq", "xs", CX[0], CX[1], "xi")
-    mm(0, "u2q", "u2s", 0, "xq", "xs")
+    ts(R("tq", 32, 64), R("lab", 0, 24), shift(), A.add, off=R("so", 0, 2))
     ts(R("d1", 0, 8 * NS, 4), R("dq", 0, 2 * NS), 0.0, A.min)
-    tt(R("d1", 1, 8 * NS, 4), R("ng", 0, 2 * NS), R("d1", 2, 8 * NS, 4), A.subtract)
-    quant("xq", "xs", CX[1], CX[2], "xi")
-    mm(4, "u2q", "u2s", 0, "xq", "xs")
+    cp("S", R("d1", 1, 8 * NS, 4), R("dq", 0, 2 * NS), func=AF.Abs)
+    cp("S", R("ng", 72, 72 + NS), R("dq", 1, 2 * NS, 2), scale=-1.0, func=AF.Sign)
+    cp("S", R("ng", 48, 48 + NS), R("ng", 72, 72 + NS), scale=-0.5, bias=-0.5)
+    order_tables(R("tq", 32, 32 + NS, 1, 64))
+    spare[0] = 1
+    ts(tile("X3", 2, 2), R("mtt", 24, 24 + NS, 1, 64), shift(2, 2), A.add, float(AT["X0"]), A.add)
+    ts(R("wo", 0, 32), R("wi", 0, 32), col("pm", 11), A.add)
+    for k in range(2):
+        cp("S", col("pm", 16 + k), col("pm", 11), scale=8.0, bias=2.0 + k)
+    ts(col("pm", 18), col("pi", 5), 16.0, A.mult, shift(), A.is_equal)
+    cp("S", col("pm", 19), col("pm", 18), scale=float(WW))
+    ts(R("pm", 20, 22), R("cp", 0, 2), 16.0, A.mult, col("pm", 19), A.add)
+    ts(R("sy", 0, 2), R("pm", 20, 22), float(C + 351), A.min)
+    spare[0] = 0
 
-    def scores(name, h, after=[]):
-        o, i, sign, big = R(name, CX[h], CX[h + 1]), bank(4 * h), col("pm", 8), col("pm", 10)
-        if name == "ssb":
-            op("S", lambda: g.scalar.activation(o[1], i[1], AF.Identity, scale=sign[1]), [o], [i, sign])
-        else:
-            op("S", lambda: g.scalar.activation(o[1], i[1], AF.Identity, bias=big[1], scale=sign[1]), [o], [i, sign, big] + after)
-
-    def first_scores():
-        scores("ssb", 0)
-        scores("ssm", 0)
-
-    first_scores()
-    order_tables()[0]()
-    for b in range(4):
-        cp("V", R("mo", 0, 20, 1, 32 * b, 32 * b + 16), R("mtt", 1, 21, 1, 32 * b, 32 * b + 16))
-    order_tables()[1]()
-
-    def turned(k, q):
-        a, b = (0, 6, 12, 18, 24, 28, 32)[k:k + 2]
-        if q == "V":
-            cp("V", R("w2q", 16 * a, 16 * b, cast=dt.uint32), R("wq", 0, 512, cast=dt.uint32), R("wo", a, b))
-        else:
-            cp("S", R("w2s", 16 * a, 16 * b), R("wp", 0, 512), R("wo", a, b))
-
-    def send(r, h):
-        dst, n = T.cores[rank ^ STEP[r]], 0
-        waits("G", [], [R("hqc%d" % r, CUT[h], CUT[h + 1])])
-        for k in [k for k, p in enumerate(PIECES) if p[3] == h]:
-            if topo.may_write(core, dst):
-                to, land, sem = dst, piece(T, k, "ldc%d" % r, "lds%d" % r), T.sem["arr%d%d" % (r, PIECES[k][0])]
-            else:
-                to, land, sem = relays(core, dst, T, topo)[PIECES[k][4]], piece(T, k, "rlq", "rls"), T.sem["hop%d" % k]
-            rid, pid = topo.addr(to, core)
-            g.remote_dma(land, piece(T, k, "hqc%d" % r, "hqs%d" % r), sem, T.sem["sent%d" % r], pid, rid, topo.mask(core, to))
-            n += len(topo.engines(core, to))
-        return n
-
-    def arrivals(r, kind):
-        src = T.cores[rank ^ STEP[r]]
-        return sum(len(topo.engines(src if topo.may_write(src, core) else relays(src, core, T, topo)[p[4]], core)) for p in PIECES if p[0] == kind)
-
-    KB = {1: 1, 2: 2, 3: 3, 4: 2, 5: 3, 6: 0}
-    WB = {1: 2, 2: 3, 3: 2, 4: 3, 5: 0, 6: 3}
-    W0 = {1: EA, 2: VV[1], 3: DD, 4: ID, 5: EB, 6: ID}
-    WR = {2: VV[1], 3: DD, 4: DD, 5: EB}
-    SHARE = 208
     sent = []
     for r in range(ROUNDS):
-        last, ahead, mate = r == ROUNDS - 1, AHEAD[r], T.cores[rank ^ STEP[r]]
-        ts(R("ssb", CX[1], C), bank(4), col("pm", 8), A.mult)
-        if r == 0:
-            for f in order_tables("S")[2:4]:
-                f()
-            ts(R("ng", 0, 2 * NS), R("dq", 0, 2 * NS), 0.0, A.is_lt, -1.0, A.mult)
-        scores("ssm", 1, [R("ssb", CX[1], C)])
-        if r == 0:
-            order_tables()[4]()
+        last, mate, ls = r == ROUNDS - 1, T.cores[rank ^ STEP[r]], "ls%d" % r
+        far = not topo.may_write(core, mate)
+        back = int(far and BACK)
+        sent.append(0)
+
+        def send(m, r=r, mate=mate, far=far):
+            names, land, who, n = ["ls%d" % r, "hqc%d" % r, "hqs%d" % r], ["pn%d" % r, "ldc%d" % r, "lds%d" % r], [], 0
+            mine = [(k, p) for k, p in enumerate(pieces(far, r)) if p[0] == m]
+            for k, p in mine:
+                to = relays(core, mate, T, topo)[p[4]] if far else mate
+                rid, pid = topo.addr(to, core)
+                args = (side(T, ["rll", "rlq", "rls"] if far else land, p), side(T, names, p), T.sem["hop%d" % k if far else "arr%d%d" % (r, m)], T.sem["sent%d" % r], pid, rid, topo.mask(core, to))
+                who.append(add("G", (lambda args=args: g.remote_dma(*args)), [], [R(names["lcs".index(p[1])], p[2], p[3])], 0.15, 0.0, ("none", 0)))
+                sent[r] += len(topo.engines(core, to))
+                n += len(topo.engines(relays(mate, core, T, topo)[p[4]] if far else mate, core))
+            add(None, None, [R(land["lcs".index(p[1])], p[2], p[3]) for k, p in mine], [], 0.0, (TRIP + (0.8 if m else 0.1)) * (2 if far else 1), ("arr%d%d" % (r, m), n), after=who)
+            return who
+
+        n = CX[1]
         for h in range(2):
             tt(R("df", 16 + CX[h], 16 + CX[h + 1]), R("ssb"), R("ssm", CX[h], CX[h + 1]), A.is_ge, off=R("mo", CX[h] // 16, CX[h + 1] // 16))
-            if r == 0:
-                order_tables()[5 + h]()
-        for t in range(4):
-            cp("S", R("xp", C * t, C * t + C), R("xi", t, 4 * C, 4))
-        if r == 0:
-            for k in range(2):
-                turned(k, "S")
-        n = CX[1]
+        compared = len(nodes) - 2
+        for k, (a, b) in enumerate(zip(WCUT, WCUT[1:]) if r == 0 else ()):
+            spare[0] = int(k >= WS)
+            cp("S", R("w2s", 16 * a, 16 * b), R("wp", 0, 512), R("wo", a, b))
+            nodes[-1]["after"].append(compared)
+        spare[0] = 0
         tr(R("tu", 0, n), R("df", 16, 16 + n))
         tr(R("tu", n, 2 * n), R("df", 0, n))
         tr(R("tu", 2 * n, n + C), R("df", 16 + n, 16 + C))
-        tr(R("tu", n + C, 352 + C), R("df", n, 352))
+        tr(R("tu", n + C, C + 352), R("df", n, 352))
         for a, b in SCANS:
-            o, d0, d1 = R("sc", a // 4, b // 4), R("tu", a, b, 4), R("d1", a // 4, b // 4)
-            op("V", lambda: g.vector.tensor_tensor_scan(o[1], d0[1], d1[1], 0.0, A.mult, A.add), [o], [d0, d1])
-        from_scan(0, PARTS)
-        from_scan(1, PARTS)
-        gather(OPEN, "wb", EA, "wb", ID, ID + WW, "ea")
-        move("kk", 2, "eb", 2, 2, EC)
-        move("kk", 0, "eb", 2, 1, EC)
-        move("kk", 3, "ea", 1, c0=24)
-        behind = {0: ("wb", EB, "wb", ID, ID + WW, "kk", EC), 1: ("wb", DD, "wb", EB, EB + WW, "kk", ED)}
-        if not last:
-            behind.update({2: ("aw", 0, "wb", ID, ID + WW, "eb"), 3: ("glo", 0, "aw", 0, WW, "lh"), 4: ("ghi", 0, "aw", 0, WW, "lh", 22)})
-        gather(LEVEL, "wb", VV[0], "wb", EA, EA + WW, "eb")
-        gather([("S", 0, AWAY)], *behind[0])
-        move("kk", 2, "eb", 0, c0=24)
-        turn(0, "wb", VV[0], RUN, 32)
-        from_turn(0, KB[1], 0, VV[0] - W0[1], 0, RUN)
-        move("kk", 2, "ea", 2, 2, ED)
-        from_turn(0, KB[1], 0, VV[0] - W0[1], RUN, NS)
-        ls = "ls%d" % r
+            scan(R("sc", a // 4, b // 4), R("tu", a, b, 4), R("d1", a // 4, b // 4))
 
-        def own(b, first):
-            return lambda: plain(ls, b, 2 * b + 1 - first, first)
-
-        def both(li, first):
-            plain(("pa", "pb")[li % 2], li // 2, li, first)
-        spare = {1: [own(0, 0)], 2: [lambda: from_turn(1, 1, KB[1], DD - W0[3], 0, NS, 3)], 3: [own(0, 1), lambda: move("kk", 0, "eb", 3, c0=24 * 4)],
-                 4: [own(1, 0)], 5: [own(1, 1)], 6: [own(2, 0)]}
-        for s in range(1, 7):
-            gather(FIRST, "wb", VV[s], "wb", W0[s], VV[s - 1] + WW, "kk", 24 * s)
-            if s - 1 in behind:
-                gather([("S", AWAY, NS)], *behind[s - 1])
-            if r == 0:
-                turned(s - 1, "V")
-            if not ahead:
-                for li, first in {1: [(0, 0), (1, 0)], 2: [(0, 1), (1, 1)], 3: [], 4: [(2, 0), (3, 0)], 5: [(2, 1), (3, 1), (4, 0)], 6: [(4, 1), (5, 0)]}[s]:
-                    both(li, first)
-            if s == 6:
-                own(2, 0)()
-                break
-            gather(SECOND, "uu", 0, "wb", W0[s] + VV[s] - VV[s - 1], VV[s] + WW, "kk", 24 * s)
-            for f in spare[s]:
-                f()
-            if s in behind:
-                gather([("S", 0, AWAY)], *behind[s])
-            if r == 0 and s == 5:
-                for k in range(3, 6):
-                    turned(k, "S")
-            turn(s, "uu", 0, RUN)
-            for a, b in ((0, RUN), (RUN, NS)):
-                from_turn(s, KB[s + 1], KB[s], VV[s] - W0[s + 1], a, b)
-                if s < 5:
-                    from_turn(s, WB[s + 1], KB[s], WR[s + 1] - W0[s + 1], a, b)
-            if s == 5:
-                for k, at in enumerate((VV[4], VV[6])):
-                    ts(R("kk", k, 20, 2, 0, 32), R("t5", 16, C, 32, 32 * KB[5], 32 * KB[5] + 32), float(MID + at - EB), A.add, shift(0), A.add)
-        cz = CZ if ahead else CUT
-        gather(LAST[ahead], "uu", 0, "wb", EB, VV[6] + WW, "kk")
-        own(2, 1)()
-        for h in range(2):
-            tr(R("tm", cz[h], cz[h + 1], 1, 0, 32), R("uu", cz[h], cz[h + 1], 1, 0, 32))
-        for h in range(2):
-            ts(R(ls, cz[h] // 16, cz[h + 1] // 16, 1, 96, 128), R("tm", cz[h], cz[h + 1], 16, 0, 32), float(MID), A.add)
-        def zed(q, h, t):
-            cp(q, R("zt", 4 * cz[h] + t, 4 * cz[h + 1], 4), R("xp", C * t, C * t + C), R(ls, cz[h] // 16, cz[h + 1] // 16))
-
-        def layer(h):
-            quant("zq", "zs", cz[h], cz[h + 1], "zt")
-            for b in range(4):
-                mm(4 * h + b, "w2q", "w2s", 128 * b, "zq", "zs", cut=cz)
-
-        def out(q, h, b):
-            o = R("hp", C * b + cz[h], C * b + cz[h + 1]) if ahead else R("ht", 4 * cz[h] + b, 4 * cz[h + 1], 4)
-            if q == "S":
-                cp("S", o, bank(4 * h + b, cz), scale=0.03125)
+        def from_scan(name, sd, h):
+            cp("V", tile(name, 0, 4, n // 16 + 16 * h - 16, n // 16 + 16 * h), R("sc", n // 2 * h, (n // 2, 8 * NS)[h]), col("sx", 4 * sd + 2 * h))
+        for word in CONV.split():
+            if word[0] == "m":
+                a, b = {"0": (0, n // 16), "1": (n // 16, NS), "2": (0, NS)}[word[1]]
+                cp("V", tile("M0", 0, 2, a, b), tile("M0", 2, 2, a, b))
+            elif word[0] == "g":
+                gather(SHARE["EA"], "EA")
             else:
-                ts(o, bank(4 * h + b, cz), 0.03125, A.mult)
+                spare[0] = int(word[0] == "X")
+                from_scan({"E": "EA", "M": "M0", "X": "X0"}[word[0]], int(word[0] != "E"), int(word[1]))
+                spare[0] = 0
+        gather(SHARE["M0"], "M0", AT["EA"])
+        here = len(nodes) - 1
+        for a, b in zip(WCUT, WCUT[1:]) if r == 0 else ():
+            aside(cp, "V", R("w2q", 16 * a, 16 * b, cast=dt.uint32), R("wq", 0, 512, cast=dt.uint32), R("wo", a, b))
+            nodes[-1]["after"].append(here)
+        for name, lists in (("G1", ["L0"]), ("X1", ["L1"]), ("X2", ["e6"])):
+            aside(offsets, name, lists)
+        for before, name in zip(GATHERS[1:], GATHERS[2:]):
+            s, end = int(name[1]), AT["EA"] if name == "X0" else None
+            if name[0] == "X":
+                gather([p for p in SHARE[name] if p[0] == "S"], name, START.get(name, 0), end)
+                turn(s, lambda: gather([p for p in SHARE[name] if p[0] == "V"], name, START.get(name, 0), end))
+            else:
+                gather(SHARE[name], name)
+                if before[0] == "X":
+                    others("t%d" % (s - 1), name)
+                if before in TURNED:
+                    buf, b, n = TURNED[before]
+                    for a, e in zip(XRUNS, XRUNS[1:]):
+                        tr(R(buf, a, e, 1, 32 * b, 32 * (b + n)), R("wb", AT[before] + a, AT[before] + e, 1, 32 * b, 32 * (b + n)))
+                    for later in LANES:
+                        offsets(later, [n for n in HELD if HELD[n][0] == buf])
+            for li in {"X0": (1, 0), "X3": (3, 2), "X4": (5, 4)}.get(name, ()):
+                aside(own, ls, li)
+        gather(LAST, "MIX", 0, AT["END"], ("uu", 0))
+        cz, cs = (CF, CF) if back else (CZ, CS[r])
+        for a, b in zip(cz, cz[1:]):
+            tr(R("tm", a, b, 1, 64, 96), R("uu", a, b, 1, 64, 96))
+            ts(R(ls, a // 16, b // 16, 1, 96, 128), R("tm", a, b, 16, 64, 96), float(MID), A.add)
+        if back:
+            load([("Y", R("lr", 0, 20, 1, 16 * k, 16 * k + 16), R(ls, 0, 20, 1, 112 - 16 * k, 128 - 16 * k)) for k in range(8)])
+        else:
+            send(0)
+
+        def in_turn(seq, cut, one, whole):
+            for word in seq.split():
+                k = int(word[0])
+                if word[1] == "q":
+                    whole(k)
+                else:
+                    one(word[1], k % 4, cut[k // 4], cut[k // 4 + 1])
+
+        def product(q, t, a, b):
+            k, o = 4 * cz.index(a) + t, R("ht", 4 * a + t, 4 * b, 4) if back else R("hp", C * t + a, C * t + b)
+            mm(k, "w2q", "w2s", 128 * t, "zq", "zs", a, b)
+            if q == "S":
+                cp("S", o, bank(k, b - a), scale=0.03125)
+            else:
+                ts(o, bank(k, b - a), 0.03125, A.mult)
 
         def leave(h):
-            quant("hqc%d" % r, "hqs%d" % r, CUT[h], CUT[h + 1], "ht")
-            return send(r, h)
+            quant("hqc%d" % r, "hqs%d" % r, cs[h], cs[h + 1], "ht")
+            gone[:] = send(1 + h)
 
-        def lay_out(q, h, t):
-            cp(q, R("ht", 4 * CS[h] + t, 4 * CS[h + 1], 4), R("hp", C * t, C * t + C), R("pn%d" % r, CS[h] // 16, CS[h + 1] // 16))
-
-        def direct(land, src, sem):
-            rid, pid = topo.addr(mate, core)
-            g.remote_dma(land, src, T.sem[sem], T.sem["sent%d" % r], pid, rid, topo.mask(core, mate))
-            return len(topo.engines(core, mate))
-
-        def leave_laid(h):
-            a, b = CS[h], CS[h + 1]
-            quant("hqc%d" % r, "hqs%d" % r, a, b, "ht")
-            waits("G", [], [R("hqc%d" % r, a, b)])
-            return (direct(T["ldc%d" % r][:, a:b].bitcast(dt.uint8), T["hqc%d" % r][:, a:b].bitcast(dt.uint8), "arr%d%d" % (r, h))
-                    + direct(T["lds%d" % r][:, a:b], T["hqs%d" % r][:, a:b], "arr%d%d" % (r, h)))
-
-        def unpackers(par):
-            for odd in range(2):
-                k = 2 * par + odd
-                if par == 2:
-                    ts(R("et", 520 * k, 520 * k + 516), R("icd", 0, 516), float(2 + odd), A.is_equal)
-                else:
-                    ts(R("et", 520 * k, 520 * k + 516), R("icd", 0, 516), float(2 + odd), A.is_equal, col("pm", 2 + 2 * par), A.mult)
-            for b in range(4):
-                k = 4 * par + b
-                quant("eq", "es", 128 * k, 128 * k + 128, "et", 520 * (2 * par + b % 2) + 2 - 2 * (b // 2))
-
-        if r == 0:
-            turned(2, "S")
-        if ahead:
-            waits("G", [], [R(ls, 0, 20)])
-            n_sent = direct(T["pn%d" % r][:, 0:20], T[ls][:, 0:20], "list%d" % r)
-        for q, h, t in (("V", 0, 0), ("S", 0, 2), ("V", 0, 1), ("S", 0, 3), ("S", 1, 2)) + ZED[ahead][0]:
-            zed(q, h, t)
-        layer(0)
-        for q, h, t in ZED[ahead][1]:
-            zed(q, h, t)
-        if r == 0:
-            o, i, back = R("icd", 0, 516), R("icb", 0, 516), col("pm", 17)
-            op("S", lambda: g.scalar.activation(o[1], i[1], AF.Identity, bias=back[1]), [o], [i, back])
-        layer(1)
-        if ahead:
-            for k in range(8):
-                out(OUTS[k], k // 4, k % 4)
-            note([R("pn%d" % r, 0, 20)], [], "list%d" % r, len(topo.engines(mate, core)))
-            for q, h, t in LAID:
-                lay_out(q, h, t)
-            n_sent += leave_laid(0)
-            for q, h, t in LAID2:
-                lay_out(q, h, t)
-            sent.append(n_sent + leave_laid(1))
+        gone = []
+        in_turn(ZED[r], cz, lambda q, t, a, b: cp(q, R("zt", 4 * a + t, 4 * b, 4), R("xp", C * t, C * t + C), R(ls, a // 16, b // 16)), lambda h: quant("zq", "zs", cz[h], cz[h + 1], "zt"))
+        in_turn(OUTS[r], cz, product, leave)
+        if back:
+            for a, b in zip(SCAT, SCAT[1:]):
+                o, i, by = R("df", 16, 16 + C), R("idn", 16 * a, 16 * b), R("lr", a, b)
+                add("V", lambda o=o, i=i, by=by: g.vector.tensor_copy(at(o, by), i[1]), [o], [i, by], 0.05 + SCATC * 16 * (b - a) * CYC)
+            tr(R("tu"), R("df", 16, 16 + C))
+            tr(R("tu", C, C + 352), R("df", 0, 352))
+            ts(R("li", 0, 32), R("tu", 0, C + 352), float(MID), A.add, off=R("sy", 0, 2))
+            in_turn(AWAY, cs, lambda q, t, a, b: cp(q, R("hp", C * t + a, C * t + b), R("xp", C * t, C * t + C), R("li", a // 16, b // 16)), None)
         else:
+            in_turn(LAID[r], cs, lambda q, t, a, b: cp(q, R("ht", 4 * a + t, 4 * b, 4), R("hp", C * t, C * t + C), R("pn%d" % r, a // 16, b // 16)), leave)
+        strict[0] = 1
+        if r == 0:
+            for k in range(2):
+                ts(R("et", 520 * k, 520 * k + 516), R("icd", 0, 516), col("pm", 16 + k), A.is_equal)
             for b in range(4):
-                out(OUTS2[b], 0, b)
-            n_sent = leave(0)
-            for b in range(4):
-                out(OUTS2[4 + b], 1, b)
-            sent.append(n_sent + leave(1))
-        if not last:
-            for f in order_tables("S")[:4]:
-                f()
-        if r == 0 and any(AHEAD):
-            unpackers(2)
-        if not ahead:
-            from_turn(5, WB[6], KB[5], 0, 0, NS)
-            gather(ALL_S, "uu", 0, "wb", EB, VV[6] + WW, "kk", 24 * 6)
-            both(5, 1)
-        if not last:
-            for f in order_tables()[4:]:
-                f()
-        if r == (2 if AHEAD[1] else 0):
-            ts(col("pm", 2), col("pi", 2), 0.0, A.is_equal)
-            ts(col("pm", 4), col("pi", 2), 0.0, A.is_gt)
-            unpackers(0)
-        if not ahead:
-            tr(R("t6", 0, 352), R("uu", 0, 352))
-        if r == (2 if AHEAD[1] else 0):
-            unpackers(1)
-        if not ahead:
-            for first in range(2):
-                for li in (6, 7):
-                    both(li, first)
+                quant("eq", "es", 128 * b, 128 * b + 128, "et", 520 * (b % 2) + 2 - 2 * (b // 2))
         if r == 1:
             quant("vq", "vs", 0, 128, "vt")
+        strict[0] = 0
+        if not last:
+            here = len(nodes)
+            aside(order_tables, R("sc", 6, 8 * NS, 8, 64))
+            for n in nodes[here + 1:]:
+                n["after"] += gone[:TABS]
         if last:
             cp("S", R("llw"), R("idf"), R(ls, 0, 20))
-            g.sync.wait_ge(T.sem["sent%d" % r], sent[r])
-            store("Y", T.ll[:, :], (R("llw")[0], T.llw[0:128:16, 0:C]))
-        ldc, lds = R("ldc%d" % r, cast=dt.uint32), R("lds%d" % r)
-        if not ahead:
-            note([ldc], [], "arr%d0" % r, arrivals(r, 0))
-            note([lds], [], "arr%d1" % r, arrivals(r, 1))
-            for h in range(2):
-                for n, by in (("ga", "pa"), ("gb", "pb")):
-                    off = R(by, CX[h] // 16, CX[h + 1] // 16)
-                    cp("V", R("%sc%d" % (n, r), CX[h], CX[h + 1], cast=dt.uint32), ldc, off)
-                    cp("S", R("%ss%d" % (n, r), CX[h], CX[h + 1]), lds, off)
-            for h in range(2):
-                for par, b in UNPACK[h]:
-                    n = ("ga", "gb")[par]
-                    mm(4 * h + b, "eq", "es", 512 * par + 128 * b, "%sc%d" % (n, r), "%ss%d" % (n, r), par == 0, par == 1)
+            nodes[-1]["after"] += gone
+            left = add(None, None, [], [], 0.0, TRIP, ("sent%d" % r, sent[r]), after=gone)
+            store("Y", T.ll[:, :], (R("llw")[0], T.llw[0:128:16, 0:C]), [left])
+        strict[0] = 1
+        for k in UNPACK if back else range(8):
+            mm(k, "eq", "es", 128 * (k % 4), "ldc%d" % r, "lds%d" % r, cs[k // 4], cs[k // 4 + 1])
+        for k in UNPACK if back else range(8):
+            t, a, b = k % 4, cs[k // 4], cs[k // 4 + 1]
+            x = R("hp", C * t + a, C * t + b) if back else R("xi", 4 * a + t, 4 * b, 4)
+            tt(x, bank(k, b - a), x, A.add)
+            if not back and k + 1 == ADDS[r]:
+                (results if last else scores)(0)
+        strict[0] = 0
+        if not back:
+            (results if last else scores)(1)
+        if back:
+            in_turn(HOME, CX, lambda q, t, a, b: cp(q, R("xi", 4 * a + t, 4 * b, 4), R("hp", C * t, C * t + C), R("lr", a // 16, b // 16)), results if last else scores)
+    for k in range(4):
+        store("Y", T.osc[4 * k:4 * k + 4, :], R("xs", 0, C, 1, 32 * k, 32 * k + 4))
 
-        def add(k):
-            cut = CS if ahead else CX
-            x = R("xi", 4 * cut[k // 4] + k % 4, 4 * cut[k // 4 + 1], 4)
-            tt(x, bank(k, cut), x, A.add)
-
-        adds = ADDS[r]
-        for h in range(2):
-            if ahead:
-                note([R("ldc%d" % r, CS[h], CS[h + 1]), R("lds%d" % r, CS[h], CS[h + 1])], [], "arr%d%d" % (r, h), 2 * len(topo.engines(mate, core)))
-                for b in range(4):
-                    mm(4 * h + b, "eq", "es", 1024 + 128 * b, "ldc%d" % r, "lds%d" % r, cut=CS)
-        for h in range(2):
-            for k in range(*((0, adds), (adds, 8))[h]):
-                add(k)
-            quant("xq", "xs", CX[h], CX[h + 1], "xi")
-            if last:
-                mm(4 * h, "vq", "vs", 0, "xq", "xs")
-                a, b = CX[h], CX[h + 1]
-                store("Y", T.oc[:, 4 * a:4 * b], R("xq", a, b, cast=dt.uint8))
-                cp("S" if h == 0 else "V", R("ysb", a, b), bank(4 * h))
-                if h == 1:
-                    for k in range(4):
-                        store("Y", T.osc[4 * k:4 * k + 4, :], R("xs", 0, C, 1, 32 * k, 32 * k + 4))
-                store("S", T.y[:, a:b], R("ysb", a, b))
-            else:
-                mm(4 * h, "u2q", "u2s", 0, "xq", "xs")
-                if h == 0:
-                    first_scores()
+    if "pre" not in PLAN:
+        PLAN.update(pre=[n["pre"] for n in nodes], order=plan(nodes))
+    cnt, known, snap, sig = {q: 0 for q in QUEUES}, {q: {} for q in eng}, {}, {}
+    for i in PLAN["order"]:
+        n, q = nodes[i], nodes[i]["q"]
+        sig[i] = n["sig"]
+        if q is None:
+            continue
+        need, k = {}, known[q]
+        for s, v in (sig[p] for p in PLAN["pre"][i]):
+            if k.get(s, 0) < v:
+                need[s] = max(need.get(s, 0), v)
+        for s in list(need):
+            if any(s2 != s and snap.get((s2, v2), {}).get(s, 0) >= need[s] for s2, v2 in need.items()):
+                del need[s]
+        for s, v in need.items():
+            eng[q].wait_ge(T.sem[s], v)
+            for a, b in snap.get((s, v), {}).items():
+                k[a] = max(k.get(a, 0), b)
+            k[s] = max(k.get(s, 0), v)
+        if n["sig"] is None:
+            cnt[q] += 1
+            sig[i] = ("q" + q, cnt[q])
+            snap[sig[i]] = dict(k)
+            n["call"]().then_inc(T.sem["q" + q], 1)
+        else:
+            n["call"]()
     for r in range(ROUNDS):
         g.wait_ge(T.sem["sent%d" % r], sent[r])
     for q in QUEUES:
-        if cnt.get("q" + q, 0):
-            g.wait_ge(T.sem["q" + q], cnt["q" + q])
+        g.wait_ge(T.sem["q" + q], cnt[q])
     for k, n in enumerate(loaded):
         g.wait_ge(T.sem["dm%d" % k], n)
     g.wait_ge(T.sem.stored, stores[0])

from concourse.mybir import dt, AluOpType, ActivationFunctionType

C, ROUNDS, STEP = 320, 3, [4, 1, 2]
MID = 160
NS, WW = 21, 336
SLOT = [1, 6, 2, 5, 3, 7, 4, 0]
GATHERS = "EA M0 X0 G1 M1 X1 M2 X2 M3 X3 G4 M4 X4 M5 X5".split()
TURNED = {"X2": ("x2", 1, 1), "X3": ("x3", 0, 4)}
AT, TILE = {"ID": 0}, {n: 32 * k + 4 for k, n in enumerate(GATHERS + ["MIX", "TH"])}
for _a, _b in zip(["ID"] + GATHERS, GATHERS + ["END"]):
    AT[_b] = AT[_a] + WW + 16 * (_a[0] == "M" or _a in TURNED)
HELD = {"k1": ("t0", 0), "w1": ("t0", 1), "w2": ("t0", 2), "k2": ("t1", 1), "k3": ("t2", 2), "w4": ("x2", 1), "k4": ("t3", 3), "L2": ("t3", 1), "L3": ("t3", 2), "w5": ("x3", 0),
        "k5": ("t4", 1), "L5": ("t4", 2), "L4": ("t4", 3), "k6": ("t5", 0), "e6": ("X0", 0), "L1": ("X0", 2), "L0": ("X0", 3)}
LANES = {"G1": "L0.X0 k1.M0 w1.M0 k1.M0", "M1": "k1.G1 k1.G1 k1.G1 k1.G1", "X1": "k1.M1 L1.X0 k1.M1 w2.M1", "M2": "w2.X1 k2.X1 k2.X1 k2.X1", "X2": "k2.M2 k2.M2 e6.ID k2.M2",
         "M3": "k2.X2 k2.EA k3.EA k3.X2", "X3": "k3.M3 - - -", "G4": "w4.X3 k4.X2 k4.M3 -", "M4": "k4.G4 k4.G4 k4.G4 k4.EA", "X4": "k4.M4 - w5.M4 -",
         "M5": "k5.X4 - k5.X4 -", "X5": "- - - -"}
TILE["X5"], START = TILE["M5"], {"M0": AT["EA"], "X5": AT["M5"] - AT["X4"]}
PAIRED = {"M1": (2, "M1", 0), "X2": (0, "M2", 2), "M3": (0, "M2", 2), "M4": (2, "M4", 0)}
CX = [0, 192, 320]
CZ = [0, 192, 320]
RUNS = [[0, 8, 22]] * 6
FIRST = [("S", 0, 4), ("V", 4, 8), ("S", 8, 14), ("V", 14, NS)]
SECOND = [("V", 0, 8), ("S", 10, NS), ("V", 8, 10)]
BESIDE = [("S", 0, 16), ("V", 16, NS)]
XRUNS = [0, 352]
WHOLE = [0, 1, 2, 3, 4]
SHARE = {n: SECOND if n[0] == "M" else FIRST for n in GATHERS}
SHARE.update(EA=[("S", 0, 10), ("V", 10, 18), ("S", 18, NS)], X0=[("S", 0, 4), ("S", 4, NS)], X1=[("S", 0, 14), ("V", 14, NS)], X2=[("S", 0, 14), ("V", 14, NS)], X3=[("S", 0, 18), ("V", 18, NS)],
             X4=[("S", 0, 14), ("V", 14, NS)], X5=[("S", 0, 14), ("V", 14, NS)],
             G1=[("V", 0, 8), ("S", 8, NS)], G4=[("V", 0, 10), ("S", 10, NS)], M2=[("V", 0, 10), ("S", 10, NS)], M5=[("V", 0, 10), ("S", 10, NS)])
TABS = 1
CONV = "E0 M0 E1 M1 g m2 X0 X1"
CS = [[0, 192, 320]] * 3
UNPACK = [0, 1, 2, 3, 4, 5, 6, 7]
SCAT, SCATC = [0, 6, 12, 20], 4
ADDS = [8, 8, 8]
LAST = [("S", 0, 6), ("V", 6, 12), ("S", 12, 16), ("V", 16, 20)]
BACK, SPLIT = True, 0
CF = [0, 128, 320]
ZED = ["0V 1V 2S 3S 4S 0q 5S 6S 7S 1q", "0V 1V 2S 3S 4S 0q 5S 6S 7V 1q", "0V 1S 2V 3S 5S 0q 7V 6V 4S 1q"]
OUTS = ["0S 1S 2S 4V 3V 5S 6V 7V", "0V 1S 2V 3S 4V 5S 6V 7V", "2V 3S 0S 1S 0q 4S 5S 7S 6S 1q"]
if not BACK:
    ZED[2], OUTS[2] = ZED[1], OUTS[1]
LAID = ["0V 4S 1S 2V 3S 5S 0q 6S 7V 1q"] * 3
AWAY = "0V 1S 2V 3S 4V 5S 6S 7S"
HOME = "4S 0S 2V 1S 3V 5S 7V 6S 0q 1q"
SCANS = [(0, 192), (192, 384), (384, 512), (512, 672)]
LOADS = "lm01"
TAB1 = [("S", 0, NS)]
TAB2 = [("S", 0, NS)]
LATE, WS, U2S, XL, XG = 0, 5, "S", 2.0, 4
XCUT = [0, 160, 320]
WCUT = [0, 2, 4, 8, 16, 24, 28, 32]
MARGIN = 0.3
XS = 160
CYC, GAT, WAKE, TRIP = 0.00087, 1.5, 0.2, 1.1
X4 = "float8_e4m3fn_x4"
SCRATCH = {
    "xi": ("sbuf", [128, 4 * C], "bfloat16"), "xp": ("sbuf", [128, 4 * C], "bfloat16"),
    "zt": ("sbuf", [128, 4 * C], "bfloat16"), "ht": ("sbuf", [128, 4 * C], "bfloat16"), "hp": ("sbuf", [128, 4 * C], "bfloat16"),
    "ut": ("sbuf", [128, 512], "bfloat16"), "vt": ("sbuf", [128, 512], "bfloat16"),
    "icd": ("sbuf", [128, 520], "bfloat16"), "et": ("sbuf", [128, 2 * 520], "bfloat16"),
    "uq": ("sbuf", [128, 128], X4), "us": ("sbuf", [128, 128], "uint8"), "u2q": ("sbuf", [128, 128], X4), "u2s": ("sbuf", [128, 128], "uint8"),
    "vq": ("sbuf", [128, 128], X4), "vs": ("sbuf", [128, 128], "uint8"),
    "wq": ("sbuf", [128, 512], X4), "wp": ("sbuf", [128, 512], "uint8"), "w2q": ("sbuf", [128, 512], X4), "w2s": ("sbuf", [128, 512], "uint8"),
    "eq": ("sbuf", [128, 512], X4), "es": ("sbuf", [128, 512], "uint8"),
    "xq": ("sbuf", [128, C], X4), "xs": ("sbuf", [128, C], "uint8"), "zq": ("sbuf", [128, C], X4), "zs": ("sbuf", [128, C], "uint8"),
    "ssb": ("sbuf", [128, C], "float32"), "ssm": ("sbuf", [128, C], "float32"),
    "df": ("sbuf", [128, 352], "bfloat16"), "tu": ("sbuf", [128, 352 + C], "bfloat16"),
    "d1": ("sbuf", [128, 8 * NS], "float32"), "sc": ("sbuf", [128, 208], "float32"),
    "tq": ("sbuf", [128, 96], "float32"), "cr": ("sbuf", [128, 40], "float32"), "cp": ("sbuf", [128, 40], "float32"),
    "cq": ("sbuf", [128, 64], "float32"), "mq": ("sbuf", [128, 64], "float32"), "dq": ("sbuf", [128, 48], "float32"), "ng": ("sbuf", [128, 96], "float32"),
    "mtt": ("sbuf", [128, 64], "int32"), "lab": ("sbuf", [128, 24], "int32"), "pi": ("sbuf", [128, 8], "int32"), "pm": ("sbuf", [128, 24], "float32"), "pd": ("sbuf", [128, 8], "float32"),
    "so": ("sbuf", [128, 4], "uint16"), "sx": ("sbuf", [128, 10], "uint16"), "mo": ("sbuf", [128, 32], "uint16"), "uo": ("sbuf", [128, 8], "uint16"),
    "sy": ("sbuf", [128, 2], "uint16"), "lr": ("sbuf", [128, 24], "uint16"), "li": ("sbuf", [128, 32], "uint16"),
    "uf": ("sbuf", [128, 8], "float32"), "kk": ("sbuf", [128, 32 * len(TILE) + 4], "uint16"), "wo": ("sbuf", [128, 32], "uint16"), "wi": ("sbuf", [128, 32], "float32"),
    "idn": ("sbuf", [128, WW], "bfloat16"), "wb": ("sbuf", [128, AT["END"]], "bfloat16"), "uu": ("sbuf", [128, 352], "bfloat16"), "tm": ("sbuf", [128, C], "bfloat16"),
    "idf": ("sbuf", [128, C], "float32"), "llw": ("sbuf", [128, C], "float32"), "ysb": ("sbuf", [128, C], "float32"),
    "rlq": ("sbuf", [128, C], X4), "rls": ("sbuf", [128, C], "uint8"), "rll": ("sbuf", [128, 24], "uint16"),
    "ps": ("psum", [128, 4096], "float32"),
}
for _k in "t0 t1 t2 t3 t4 t5 x2 x3".split():
    SCRATCH[_k] = ("sbuf", [128, 352], "bfloat16")
for _r in range(ROUNDS):
    SCRATCH["ls%d" % _r] = SCRATCH["pn%d" % _r] = ("sbuf", [128, 24], "uint16")
    for _n in ("hq", "ld"):
        SCRATCH["%sc%d" % (_n, _r)] = ("sbuf", [128, C], X4)
        SCRATCH["%ss%d" % (_n, _r)] = ("sbuf", [128, C], "uint8")
QUEUES = ("V", "S", "P", "G")
SEMAPHORES = (["qV", "qS", "qP", "qG"] + ["dm%d" % k for k in range(8)] + ["arr%d%d" % (r, k) for r in range(ROUNDS) for k in range(3)] + ["sent%d" % r for r in range(ROUNDS)]
              + ["hop%d" % k for k in range(6)] + ["hopsent", "stored"])
PLAN = {}


def pieces(far, r):
    lists = ([] if BACK else [(0, "l", 0, 10, 0), (0, "l", 10, 20, 1)]) if far else [(0, "l", 0, 20, 0)]
    cut = CF if far and BACK else CS[r]
    if far and SPLIT:
        return lists + [(1, "c", 0, cut[1], 0), (1, "s", 0, cut[1], 1), (2, "c", SPLIT, C, 1), (2, "c", cut[1], SPLIT, 0), (2, "s", cut[1], C, SPLIT % 4 // 2)]
    return lists + [(1 + h, kind, cut[h], cut[h + 1], (h + k) % 2) for h in range(2) for k, kind in enumerate("cs")]


def side(T, names, piece):
    kind, a, b = piece[1:4]
    ap = T[names["lcs".index(kind)]][:, a:b]
    return ap.bitcast(dt.uint8) if kind == "c" else ap


def relays(core, dst, T, topo):
    return [c for c in topo.cores_of(core) if c != core and T.rank_of(c) is None and topo.die(c) == topo.die(core) and topo.may_write(c, dst)][:2]


def hand_on(g, core, T, topo):
    for r, s in enumerate(STEP):
        for i in range(len(T.cores)):
            src, dst = T.cores[i], T.cores[i ^ s]
            if topo.may_write(src, dst) or core not in relays(src, dst, T, topo):
                continue
            mine = [(k, p) for k, p in enumerate(pieces(True, r)) if relays(src, dst, T, topo)[p[4]] == core]
            rid, pid = topo.addr(dst, core)
            for k, p in mine:
                g.wait_ge(T.sem["hop%d" % k], len(topo.engines(src, core)))
                g.remote_dma(side(T, ["pn%d" % r, "ldc%d" % r, "lds%d" % r], p), side(T, ["rll", "rlq", "rls"], p), T.sem["arr%d%d" % (r, p[0])], T.sem.hopsent, pid, rid, topo.mask(core, dst))
            g.wait_ge(T.sem.hopsent, len(mine) * len(topo.engines(core, dst)))


def plan(nodes):
    busy, start, end = {}, {}, {}

    def place(i):
        n = nodes[i]
        for p in n["pre"] + n["after"]:
            if p not in end:
                place(p)
        t = max([0.0] + [end[p] + WAKE for p in n["pre"]] + [end[p] - nodes[p]["lat"] for p in n["after"]])
        if n["q"]:
            slots, room = busy.setdefault(n["q"], []), n["cost"] * (1 + MARGIN * n["spare"])
            for a, b in slots:
                if t + room <= a + 1e-9:
                    break
                t = max(t, b)
            slots.append((t, t + n["cost"]))
            slots.sort()
        start[i], end[i] = t, t + n["cost"] + n["lat"]
    for i in sorted(range(len(nodes)), key=lambda i: (nodes[i]["spare"], i)):
        if i not in end:
            place(i)
    return sorted(range(len(nodes)), key=lambda i: (start[i], i))


def rank_program(g, core, T, topo):
    rank = T.rank_of(core)
    if rank is None:
        return hand_on(g, core, T, topo)
    A, AF = AluOpType, ActivationFunctionType
    eng = {"V": g.vector, "S": g.scalar, "P": g.tensor, "G": g, "Y": g.sync}
    nodes, writers, readers, spare, strict = [], {}, {}, [0], [0]

    def R(name, c0=0, c1=None, step=1, p0=0, p1=128, cast=None):
        c1 = (C if c1 is None else c1)
        ap = T[name][p0:p1, c0:c1] if step == 1 else T[name][p0:p1, c0:c1:step]
        if cast is not None:
            ap = ap.bitcast(cast)
        return ((name, p0, p1, c0, c1, step), ap)

    def hit(a, b):
        return a[1] < b[2] and b[1] < a[2] and a[3] < b[4] and b[3] < a[4] and not (a[5] == b[5] and a[5] > 1 and (a[3] - b[3]) % a[5])

    def inside(a, b):
        return b[1] <= a[1] and a[2] <= b[2] and b[3] <= a[3] and a[4] <= b[4] and (b[5] == 1 or (a[5] == b[5] and (a[3] - b[3]) % a[5] == 0))

    def note(W, Rd, who):
        for w, _ in W:
            writers[w[0]] = [e for e in writers.get(w[0], []) if not inside(e[0], w)] + [(w, who)]
            readers[w[0]] = [e for e in readers.get(w[0], []) if not inside(e[0], w)]
        for r, _ in Rd:
            readers.setdefault(r[0], []).append((r, who))

    def add(q, call, W, Rd, cost, lat=0.0, sig=None, pre=(), after=()):
        pre = set(pre)
        if "pre" not in PLAN:
            for r, _ in Rd:
                pre.update(i for b, who in writers.get(r[0], []) if hit(r, b) for i in who)
            for w, _ in W:
                pre.update(i for b, who in writers.get(w[0], []) + readers.get(w[0], []) if hit(w, b) for i in who)
            note(W, Rd, [len(nodes)])
        after = list(after) + [i for i in range(len(nodes) - 1, -1, -1) if strict[0] and nodes[i]["q"] == q and not nodes[i]["spare"]][:1]
        nodes.append({"q": q, "call": call, "cost": cost, "lat": lat, "sig": sig, "pre": sorted(pre), "after": after, "spare": spare[0]})
        return len(nodes) - 1

    def aside(f, *args):
        spare[0] = 1
        f(*args)
        spare[0] = 0

    def width(a):
        return len(range(a[0][3], a[0][4], a[0][5]))

    def op(q, call, W, Rd, off=None, rate=1.0):
        n = width(W[0])
        if off:
            cost = (0.05 if q == "V" else 0.065) + n * GAT * CYC
        else:
            short = q == "V" and all(SCRATCH[a[0][0]][2] in ("bfloat16", "uint16") for a in W + Rd if width(a) > 1)
            cost = max(64, n * (0.5 if short and rate == 1.0 else rate)) * CYC
        return add(q, call, W, Rd + ([off] if off else []), cost)

    loaded, stores, rest = [], [0], []

    def load(items, after=()):
        s, n = "dm%d" % len(loaded), 16 * len(items)
        loaded.append(n)
        who = []
        for q, dst, src in items:
            ap, rd = (src[1], [src]) if isinstance(src, tuple) else (src, [])
            who.append(add(q, (lambda q=q, dst=dst, ap=ap: eng[q].dma_start(dst[1], ap).then_inc(T.sem[s], 16)), [dst], rd, 0.05, TRIP + width(dst) * 0.001, (s, n), after=after))
        note([dst for q, dst, src in items], [], who)
        return who

    def store(q, out, src, pre=()):
        stores[0] += 16
        add(q, lambda: eng[q].dma_start(out, src[1]).then_inc(T.sem.stored, 16), [], [src], 0.05, TRIP, ("stored", 0), pre)

    def at(a, off):
        return a[1] if off is None else a[1].indirect(off[1])

    def tt(o, a, b, f, off=None):
        op("V", lambda: g.vector.tensor_tensor(o[1], at(a, off), b[1], f), [o], [a, b], off, 1.001 if "ps" in (a[0][0], b[0][0]) else 2.0)

    def ts(o, a, s1, f, s2=None, f2=None, off=None):
        cols = [s for s in (s1, s2) if isinstance(s, tuple)]
        v1, v2 = [s[1] if isinstance(s, tuple) else s for s in (s1, s2)]
        if f2 is None:
            op("V", lambda: g.vector.tensor_scalar(o[1], at(a, off), v1, None, f), [o], [a] + cols, off)
        else:
            op("V", lambda: g.vector.tensor_scalar(o[1], at(a, off), v1, v2, f, f2), [o], [a] + cols, off)

    def cp(q, o, a, off=None, scale=None, bias=None, func=None):
        if q == "V":
            return op("V", lambda: g.vector.tensor_copy(o[1], at(a, off)), [o], [a], off)
        kw = {k: (v[1] if isinstance(v, tuple) else v) for k, v in (("scale", scale), ("bias", bias)) if v is not None}
        cols = [v for v in (scale, bias) if isinstance(v, tuple)]
        if func is None:
            func = AF.Identity if cols or bias is not None else AF.Copy
        return op("S", lambda: g.scalar.activation(o[1], at(a, off), func, **kw), [o], [a] + cols, off)

    def tr(o, a):
        op("V", lambda: g.vector.transpose(o[1], a[1]), [o], [a])

    def fill(o, v):
        op("V", lambda: g.vector.memset(o[1], v), [o], [])

    def iota(o, pat, base, cm, whole=False):
        kw = {} if whole else {"allow_small_or_imprecise_dtypes": True}
        add("G", lambda: g.iota(o[1], pat, base, cm, **kw), [o], [], 0.13 + 2 * CYC * width(o))

    def scan(o, d0, d1):
        op("V", lambda: g.vector.tensor_tensor_scan(o[1], d0[1], d1[1], 0.0, A.mult, A.add), [o], [d0, d1])

    def quant(qc, qs, a, b, tile, ta=None):
        ta = 4 * a if ta is None else ta
        o, s, i = R(qc, a, b), R(qs, a, b), R(tile, ta, ta + 4 * (b - a))
        add("V", lambda: g.vector.quantize_mx(o[1], s[1], i[1]), [o, s], [i], 0.014 + 0.001 * (b - a))

    def bank(k, n):
        return (("ps", 0, 128, 512 * k, 512 * k + n, 1), T.ps[:, 512 * k:512 * k + n])

    def mm(k, lq, lsc, la, rq, rsc, r0, r1):
        o, a, b, c, d = bank(k, r1 - r0), R(lq, la, la + 128), R(lsc, la, la + 128), R(rq, r0, r1), R(rsc, r0, r1)
        add("P", lambda: g.tensor.matmul_mx(o[1], a[1], b[1], c[1], d[1], True, True), [bank(k, 512)], [a, b, c, d], (r1 - r0 + 16) * CYC * 1.2)

    def col(n, k, b=0, blocks=4):
        return R(n, k, k + 1, 1, 32 * b, 32 * (b + blocks))

    def shift(b=0, n=4):
        return col("pm", 0, b, n)

    def tile(t, b=0, n=4, a=0, e=NS):
        return R("kk", TILE[t] + a, TILE[t] + e, 1, 32 * b, 32 * (b + n))

    def gather(shares, name, w0=0, w1=None, out=None):
        out, o0 = out or ("wb", AT[name])
        for e, a, b in shares:
            cp(e, R(out, o0 + 16 * a, o0 + 16 * b), R("wb", w0, w1 or AT[name]), tile(name, 0, 4, a, b))

    def offsets(name, lists, a=0, b=NS):
        lanes = LANES[name].split()
        to, src, frm = PAIRED.get(name, (9, None, 0))
        for to, lane in [(k, lane) for k, lane in enumerate(lanes) if k // 2 != to // 2]:
            if lane[:2] in lists:
                (buf, src), base = HELD[lane[:2]], AT[lane[3:]]
                if buf in TILE:
                    ts(tile(name, to, 1, a, b), tile(buf, src, 1, a, b), float(base), A.add)
                else:
                    ts(tile(name, to, 1, a, b), R(buf, 16 * a, 16 * b, 16, 32 * src, 32 * src + 32), float(MID + base), A.add, shift(src, 1), A.add)
        if name in PAIRED and lanes[PAIRED[name][0]][:2] in lists:
            to, src, frm = PAIRED[name]
            ts(tile(name, to, 2), tile(src, frm, 2), col("pd", 2 * list(PAIRED).index(name), frm, 2), A.add)

    def turn(s, between):
        runs = RUNS[s]
        for a, b in zip(runs, runs[1:]):
            tr(R("t%d" % s, 16 * a, 16 * b), R("wb", AT["M%d" % s] + 16 * a, AT["M%d" % s] + 16 * b))
        between()
        if s == 5:
            for k, w in enumerate(("X2", "X5")):
                ts(R("kk", TILE["MIX"] + k, TILE["MIX"] + 20, 2, 64, 96), R("t5", 16, C, 32, 0, 32), float(MID + AT[w]), A.add, shift(0, 1), A.add)
            return
        runs = [0, NS] if s in WHOLE else runs
        for a, b in zip(runs, runs[1:]):
            offsets(GATHERS[GATHERS.index("X%d" % s) + 1], [n for n in HELD if HELD[n][0] == "t%d" % s], a, min(b, NS))

    def others(buf, first):
        for name in GATHERS[GATHERS.index(first) + 1:]:
            spare[0] = int(GATHERS.index(name) > GATHERS.index(first) + 1)
            offsets(name, [n for n in HELD if HELD[n][0] == buf])
        spare[0] = 0

    def own(ls, li):
        n, k, (buf, src), to = 32 if li % 2 else 16, 1 - li % 2, HELD["L%d" % li], li // 2
        o = R(ls, 0, 20, 1, 32 * to, 32 * to + n)
        if buf in TILE:
            ts(o, R("kk", TILE[buf] + k, TILE[buf] + k + 20, 1, 32 * src, 32 * src + n), -16.0 * k, A.add)
        else:
            ts(o, R(buf, 16 * k, 16 * (k + 20), 16, 32 * src, 32 * src + n), float(MID), A.add)

    def order_tables(mine):
        far, gap, to = R("tq", 0, NS, 1, 64), R("tq", 64, 64 + NS, 1, 64), [R("d1", 4 + k, 8 * NS, 8, 64) for k in range(3)]
        cp("S", R("tq", 0, 32), R("x3", 0, 352), R("so", 2, 4), bias=col("pm", 1))
        tt(gap, far, mine, A.subtract)
        tt(to[0], gap, R("ng", 48, 48 + NS, 1, 64), A.mult)
        tt(to[1], gap, R("ng", 72, 72 + NS, 1, 64), A.mult)
        tt(to[2], far, to[0], A.add)

    def scores(h, first=False):
        a, b = CX[h], CX[h + 1]
        quant("xq", "xs", a, b, "xi")
        for k in range(h + 1):
            mm(4 * h + k, "u2q", "u2s", 0, "xq", "xs", a, b)
        if h == 0:
            cp("S", R("ssb", a, b), bank(0, b - a), scale=col("pm", 8))
        else:
            ts(R("ssb", a, b), bank(4, b - a), col("pm", 8), A.mult)
        cp("S", R("ssm", a, b), bank(5 * h, b - a), scale=col("pm", 8), bias=col("pm", 10))
        done = len(nodes) - 1
        for t in range(XG * h if first else 0):
            o, i = R("xp", C * t, C * t + C), R("xi", t, 4 * C, 4)
            add("G", lambda o=o, i=i: g.affine_select(o[1], i[1], [[0, C]], A.is_ge, 0.0, 0, 0), [o], [i], 0.17 + 2 * C * CYC)
        for t, a in [(t, a) for t in range(XG if first else 0, 4 * h) for a in range(0, C, XS)]:
            aside(cp, "S", R("xp", C * t + a, C * t + a + XS), R("xi", 4 * a + t, 4 * (a + XS), 4))
            nodes[-1]["after"].append(done)

    def results(h):
        a, b = CX[h], CX[h + 1]
        quant("xq", "xs", a, b, "xi")
        mm(4 * h, "vq", "vs", 0, "xq", "xs", a, b)
        store("Y", T.oc[:, 4 * a:4 * b], R("xq", a, b, cast=dt.uint8))
        cp("SV"[h], R("ysb", a, b), bank(4 * h, b - a))
        store("S", T.y[:, a:b], R("ysb", a, b))

    fill(R("mtt", 0, 64), 0)
    fill(R("lab", 0, 24), 0)
    load([("S", R("ut", 0, 512), T.u[:, :])])
    for what in LOADS:
        if what == "l":
            load([("YS"[k], R("lab", 1 - k, 21 - k, 1, 64 + 32 * b + 16 * k, 64 + 32 * b + 16 * k + 16), (T.lb, T.la)[b][:, :]) for b in range(2) for k in range(2)])
        elif what == "m":
            load([("YS"[k], R("mtt", 24 * sd + 1 - k, 24 * sd + 21 - k, 1, 32 * b + 16 * k, 32 * b + 16 * k + 16), T.mt[16 * SLOT[2 * b + sd]:16 * SLOT[2 * b + sd] + 16, :])
                  for b in range(4) for sd in range(2) for k in range(2)])
        else:
            a, b = CX[int(what)], CX[int(what) + 1]
            load([("YS"[int(what)], R("xi", 4 * a, 4 * b), T.x[:, 4 * a:4 * b])], range(2, len(nodes)))
            nodes[-1]["lat"] = XL + 0.001 * b
    load([("Y", R("wq", 0, 512, cast=dt.uint8), T.wc[:, :]), ("Y", R("wp", 0, 512), T.ws[:, :])], range(2, len(nodes)))
    load([("Y", R("vt", 0, 512), T.v[:, :])], range(2, len(nodes)))
    iota(R("pi", 0, 2), [[0, 2]], 0, 1, True)
    iota(R("idn", 0, WW), [[1, WW]], -MID, 0)
    iota(R("cr", 0, 24), [[16, 24]], 0, 0)
    for k, step in ((0, 2), (1, 2), (5, 2)):
        n = 4 if k == 0 else 2
        iota(R("uf", k, k + step * n - 1, step), [[16 * (SLOT[k + step] - SLOT[k]), n]], 16 * SLOT[k], 0)
    iota(R("wi", 0, 32), [[128, 4], [-16, 8]], 112, 0)
    iota(R("icd", 0, 516), [[1, 516]], -448, 4)
    iota(R("idf"), [[1, C]], 0, 0)
    fill(R("kk", TILE["X3"], 32 * len(TILE)), 0)
    cp("V", tile("X0"), R("lab", 0, NS))
    for e, a, b in TAB1:
        cp(e, R("wb", AT["X0"] + 16 * a, AT["X0"] + 16 * b), R("idn", 0, WW), tile("X0", 0, 4, a, b))
    for k, m in enumerate((16, 15, 4, 1)):
        ts(col("pi", 2 + k), col("pi", 0), m, A.bitwise_and)
    fill(R("d1", 3, 8 * NS, 4), 0.0)
    ts(col("pm", 0), col("pi", 2), 0.0, A.is_equal, 16.0, A.mult)
    cp("V", col("pm", 11), col("pi", 3))
    ts(col("pm", 12), col("pi", 3), 2.0, A.mult, 1.0, A.add)
    ts(col("pm", 13), col("pi", 3), 2.0, A.mult, 8.0, A.min)
    ts(col("pm", 14), col("pi", 3), 6.0, A.is_ge, -13.0, A.mult)
    ts(col("pm", 15), col("pi", 3), 12.0, A.is_ge)
    ts(col("pm", 8), col("pi", 4), -0.5, A.mult, 1.0, A.add)
    ts(col("pm", 10), col("pi", 3), 4.0, A.is_lt, 2.0 ** 90, A.mult)
    ts(R("wb", 0, WW), R("idn", 0, WW), shift(), A.subtract)
    ts(col("so", 0), col("pm", 12), col("pm", 14), A.add, col("pm", 15), A.add)
    ts(col("so", 1), col("pm", 13), 12.0, A.add)
    ts(R("cp", 0, 24), R("cr", 0, 24), col("pm", 11), A.add)
    ts(col("pm", 6), col("pm", 0), -23.0 / 16, A.mult, 24.0, A.add)
    cp("V", R("uo", 0, 8), R("uf", 0, 8))
    ts(R("so", 2, 4), R("so", 0, 2), 16.0, A.mult)
    ts(R("sx", 8, 10), R("cp", 0, 2), col("pm", 6), A.add)
    cp("S", col("pm", 1), col("pm", 0), bias=float(MID))
    for sd in range(2):
        cp("S", R("cq", sd, 64, 2), R("cp", 0, 24), R("so", 0, 2))
    for n, a in [("uu", WW), ("df", 0), ("df", WW)] + [("wb", AT[k] + WW) for k in GATHERS if k[0] == "M" or k in TURNED]:
        aside(cp, "S", R(n, a, a + 16), R("cr", 0, 16), None, 0.0)
    spare[0] = 1
    for k, (name, (to, src, frm)) in enumerate(PAIRED.items()):
        for b in range(2):
            cp("S", col("pd", 2 * k, frm + b, 1), col("cr", 0, frm + b, 1), scale=0.0, bias=float(AT[LANES[name].split()[to + b][3:]] - AT[LANES[src].split()[frm + b][3:]]))
    for h, (odd, most) in enumerate(((-18.0, 90.0), (-2.0, 66.0))):
        ts(col("pm", 2 + h), col("pi", 5), odd - 34.0, A.mult, 34.0, A.add)
        cp("S", col("pm", 4 + h), col("pm", 11), scale=4.0, bias=col("pm", 2 + h))
        for sd in range(2):
            ts(col("sx", 4 * sd + 2 * h), col("pm", 4 + h), most, A.min, 4.0 * sd, A.add)
    spare[0] = 0
    ts(tile("TH", 2, 2), R("mtt", 24, 24 + NS, 1, 64), shift(2, 2), A.add)
    quant("uq", "us", 0, 128, "ut")
    cp("V", R("u2q", 0, 128, cast=dt.uint32), R("uq", 0, 128, cast=dt.uint32), R("uo", 0, 8))
    cp(U2S, R("u2s", 0, 128), R("us", 0, 128), R("uo", 0, 8))
    gather(TAB2, "TH", AT["X0"], AT["G1"], ("uu", 0))
    tr(R("x3", 0, 352), R("uu", 0, 352))
    scores(0)
    scores(1, True)
    cp("V", R("mo", 0, 32), R("mtt", 0, 64), R("sx", 8, 10))
    spare[0] = LATE
    for sd in range(2):
        ts(R("mq", sd, 64, 2), R("mtt", 24 * sd, 24 * sd + 24), shift(), A.add, off=R("so", 0, 2))
    tt(R("dq", 0, 2 * NS), R("cq", 0, 2 * NS), R("mq", 0, 2 * NS), A.subtract)
    tt(R("d1", 2, 8 * NS, 4), R("cq", 0, 2 * NS), R("mq", 0, 2 * NS), A.min)
    ts(R("tq", 32, 64), R("lab", 0, 24), shift(), A.add, off=R("so", 0, 2))
    ts(R("d1", 0, 8 * NS, 4), R("dq", 0, 2 * NS), 0.0, A.min)
    cp("S", R("d1", 1, 8 * NS, 4), R("dq", 0, 2 * NS), func=AF.Abs)
    cp("S", R("ng", 72, 72 + NS), R("dq", 1, 2 * NS, 2), scale=-1.0, func=AF.Sign)
    cp("S", R("ng", 48, 48 + NS), R("ng", 72, 72 + NS), scale=-0.5, bias=-0.5)
    order_tables(R("tq", 32, 32 + NS, 1, 64))
    spare[0] = 1
    ts(tile("X3", 2, 2), R("mtt", 24, 24 + NS, 1, 64), shift(2, 2), A.add, float(AT["X0"]), A.add)
    ts(R("wo", 0, 32), R("wi", 0, 32), col("pm", 11), A.add)
    for k in range(2):
        cp("S", col("pm", 16 + k), col("pm", 11), scale=8.0, bias=2.0 + k)
    ts(col("pm", 18), col("pi", 5), 16.0, A.mult, shift(), A.is_equal)
    cp("S", col("pm", 19), col("pm", 18), scale=float(WW))
    ts(R("pm", 20, 22), R("cp", 0, 2), 16.0, A.mult, col("pm", 19), A.add)
    ts(R("sy", 0, 2), R("pm", 20, 22), float(C + 351), A.min)
    spare[0] = 0

    sent = []
    for r in range(ROUNDS):
        last, mate, ls = r == ROUNDS - 1, T.cores[rank ^ STEP[r]], "ls%d" % r
        far = not topo.may_write(core, mate)
        back = int(far and BACK)
        sent.append(0)

        def send(m, r=r, mate=mate, far=far):
            names, land, who, n = ["ls%d" % r, "hqc%d" % r, "hqs%d" % r], ["pn%d" % r, "ldc%d" % r, "lds%d" % r], [], 0
            mine = [(k, p) for k, p in enumerate(pieces(far, r)) if p[0] == m]
            for k, p in mine:
                to = relays(core, mate, T, topo)[p[4]] if far else mate
                rid, pid = topo.addr(to, core)
                args = (side(T, ["rll", "rlq", "rls"] if far else land, p), side(T, names, p), T.sem["hop%d" % k if far else "arr%d%d" % (r, m)], T.sem["sent%d" % r], pid, rid, topo.mask(core, to))
                who.append(add("G", (lambda args=args: g.remote_dma(*args)), [], [R(names["lcs".index(p[1])], p[2], p[3])], 0.15, 0.0, ("none", 0)))
                sent[r] += len(topo.engines(core, to))
                n += len(topo.engines(relays(mate, core, T, topo)[p[4]] if far else mate, core))
            add(None, None, [R(land["lcs".index(p[1])], p[2], p[3]) for k, p in mine], [], 0.0, (TRIP + (0.8 if m else 0.1)) * (2 if far else 1), ("arr%d%d" % (r, m), n), after=who)
            return who

        n = CX[1]
        for h in range(2):
            tt(R("df", 16 + CX[h], 16 + CX[h + 1]), R("ssb"), R("ssm", CX[h], CX[h + 1]), A.is_ge, off=R("mo", CX[h] // 16, CX[h + 1] // 16))
        compared = len(nodes) - 2
        for k, (a, b) in enumerate(zip(WCUT, WCUT[1:]) if r == 0 else ()):
            spare[0] = int(k >= WS)
            cp("S", R("w2s", 16 * a, 16 * b), R("wp", 0, 512), R("wo", a, b))
            nodes[-1]["after"].append(compared)
        spare[0] = 0
        tr(R("tu", 0, n), R("df", 16, 16 + n))
        tr(R("tu", n, 2 * n), R("df", 0, n))
        tr(R("tu", 2 * n, n + C), R("df", 16 + n, 16 + C))
        tr(R("tu", n + C, C + 352), R("df", n, 352))
        for a, b in SCANS:
            scan(R("sc", a // 4, b // 4), R("tu", a, b, 4), R("d1", a // 4, b // 4))

        def from_scan(name, sd, h):
            cp("V", tile(name, 0, 4, n // 16 + 16 * h - 16, n // 16 + 16 * h), R("sc", n // 2 * h, (n // 2, 8 * NS)[h]), col("sx", 4 * sd + 2 * h))
        for word in CONV.split():
            if word[0] == "m":
                a, b = {"0": (0, n // 16), "1": (n // 16, NS), "2": (0, NS)}[word[1]]
                cp("V", tile("M0", 0, 2, a, b), tile("M0", 2, 2, a, b))
            elif word[0] == "g":
                gather(SHARE["EA"], "EA")
            else:
                spare[0] = int(word[0] == "X")
                from_scan({"E": "EA", "M": "M0", "X": "X0"}[word[0]], int(word[0] != "E"), int(word[1]))
                spare[0] = 0
        gather(SHARE["M0"], "M0", AT["EA"])
        here = len(nodes) - 1
        for a, b in zip(WCUT, WCUT[1:]) if r == 0 else ():
            aside(cp, "V", R("w2q", 16 * a, 16 * b, cast=dt.uint32), R("wq", 0, 512, cast=dt.uint32), R("wo", a, b))
            nodes[-1]["after"].append(here)
        for name, lists in (("G1", ["L0"]), ("X1", ["L1"]), ("X2", ["e6"])):
            aside(offsets, name, lists)
        for before, name in zip(GATHERS[1:], GATHERS[2:]):
            s, end = int(name[1]), AT["EA"] if name == "X0" else None
            if name[0] == "X":
                gather([p for p in SHARE[name] if p[0] == "S"], name, START.get(name, 0), end)
                turn(s, lambda: gather([p for p in SHARE[name] if p[0] == "V"], name, START.get(name, 0), end))
            else:
                gather(SHARE[name], name)
                if before[0] == "X":
                    others("t%d" % (s - 1), name)
                if before in TURNED:
                    buf, b, n = TURNED[before]
                    for a, e in zip(XRUNS, XRUNS[1:]):
                        tr(R(buf, a, e, 1, 32 * b, 32 * (b + n)), R("wb", AT[before] + a, AT[before] + e, 1, 32 * b, 32 * (b + n)))
                    for later in LANES:
                        offsets(later, [n for n in HELD if HELD[n][0] == buf])
            for li in {"X0": (1, 0), "X3": (3, 2), "X4": (5, 4)}.get(name, ()):
                aside(own, ls, li)
        gather(LAST, "MIX", 0, AT["END"], ("uu", 0))
        cz, cs = (CF, CF) if back else (CZ, CS[r])
        for a, b in zip(cz, cz[1:]):
            tr(R("tm", a, b, 1, 64, 96), R("uu", a, b, 1, 64, 96))
            ts(R(ls, a // 16, b // 16, 1, 96, 128), R("tm", a, b, 16, 64, 96), float(MID), A.add)
        if back:
            load([("Y", R("lr", 0, 20, 1, 16 * k, 16 * k + 16), R(ls, 0, 20, 1, 112 - 16 * k, 128 - 16 * k)) for k in range(8)])
        else:
            send(0)

        def in_turn(seq, cut, one, whole):
            for word in seq.split():
                k = int(word[0])
                if word[1] == "q":
                    whole(k)
                else:
                    one(word[1], k % 4, cut[k // 4], cut[k // 4 + 1])

        def product(q, t, a, b):
            k, o = 4 * cz.index(a) + t, R("ht", 4 * a + t, 4 * b, 4) if back else R("hp", C * t + a, C * t + b)
            mm(k, "w2q", "w2s", 128 * t, "zq", "zs", a, b)
            if q == "S":
                cp("S", o, bank(k, b - a), scale=0.03125)
            else:
                ts(o, bank(k, b - a), 0.03125, A.mult)

        def leave(h):
            quant("hqc%d" % r, "hqs%d" % r, cs[h], cs[h + 1], "ht")
            gone[:] = send(1 + h)

        gone = []
        in_turn(ZED[r], cz, lambda q, t, a, b: cp(q, R("zt", 4 * a + t, 4 * b, 4), R("xp", C * t, C * t + C), R(ls, a // 16, b // 16)), lambda h: quant("zq", "zs", cz[h], cz[h + 1], "zt"))
        in_turn(OUTS[r], cz, product, leave)
        if back:
            for a, b in zip(SCAT, SCAT[1:]):
                o, i, by = R("df", 16, 16 + C), R("idn", 16 * a, 16 * b), R("lr", a, b)
                add("V", lambda o=o, i=i, by=by: g.vector.tensor_copy(at(o, by), i[1]), [o], [i, by], 0.05 + SCATC * 16 * (b - a) * CYC)
            tr(R("tu"), R("df", 16, 16 + C))
            tr(R("tu", C, C + 352), R("df", 0, 352))
            ts(R("li", 0, 32), R("tu", 0, C + 352), float(MID), A.add, off=R("sy", 0, 2))
            in_turn(AWAY, cs, lambda q, t, a, b: cp(q, R("hp", C * t + a, C * t + b), R("xp", C * t, C * t + C), R("li", a // 16, b // 16)), None)
        else:
            in_turn(LAID[r], cs, lambda q, t, a, b: cp(q, R("ht", 4 * a + t, 4 * b, 4), R("hp", C * t, C * t + C), R("pn%d" % r, a // 16, b // 16)), leave)
        strict[0] = 1
        if r == 0:
            for k in range(2):
                ts(R("et", 520 * k, 520 * k + 516), R("icd", 0, 516), col("pm", 16 + k), A.is_equal)
            for b in range(4):
                quant("eq", "es", 128 * b, 128 * b + 128, "et", 520 * (b % 2) + 2 - 2 * (b // 2))
        if r == 1:
            quant("vq", "vs", 0, 128, "vt")
        strict[0] = 0
        if not last:
            here = len(nodes)
            aside(order_tables, R("sc", 6, 8 * NS, 8, 64))
            for n in nodes[here + 1:]:
                n["after"] += gone[:TABS]
        if last:
            cp("S", R("llw"), R("idf"), R(ls, 0, 20))
            nodes[-1]["after"] += gone
            left = add(None, None, [], [], 0.0, TRIP, ("sent%d" % r, sent[r]), after=gone)
            store("Y", T.ll[:, :], (R("llw")[0], T.llw[0:128:16, 0:C]), [left])
        strict[0] = 1
        for k in UNPACK if back else range(8):
            mm(k, "eq", "es", 128 * (k % 4), "ldc%d" % r, "lds%d" % r, cs[k // 4], cs[k // 4 + 1])
        for k in UNPACK if back else range(8):
            t, a, b = k % 4, cs[k // 4], cs[k // 4 + 1]
            x = R("hp", C * t + a, C * t + b) if back else R("xi", 4 * a + t, 4 * b, 4)
            tt(x, bank(k, b - a), x, A.add)
            if not back and k + 1 == ADDS[r]:
                (results if last else scores)(0)
        strict[0] = 0
        if not back:
            (results if last else scores)(1)
        if back:
            in_turn(HOME, CX, lambda q, t, a, b: cp(q, R("xi", 4 * a + t, 4 * b, 4), R("hp", C * t, C * t + C), R("lr", a // 16, b // 16)), results if last else scores)
    for k in range(4):
        store("Y", T.osc[4 * k:4 * k + 4, :], R("xs", 0, C, 1, 32 * k, 32 * k + 4))

    if "pre" not in PLAN:
        PLAN.update(pre=[n["pre"] for n in nodes], order=plan(nodes))
    cnt, known, snap, sig = {q: 0 for q in QUEUES}, {q: {} for q in eng}, {}, {}
    for i in PLAN["order"]:
        n, q = nodes[i], nodes[i]["q"]
        sig[i] = n["sig"]
        if q is None:
            continue
        need, k = {}, known[q]
        for s, v in (sig[p] for p in PLAN["pre"][i]):
            if k.get(s, 0) < v:
                need[s] = max(need.get(s, 0), v)
        for s in list(need):
            if any(s2 != s and snap.get((s2, v2), {}).get(s, 0) >= need[s] for s2, v2 in need.items()):
                del need[s]
        for s, v in need.items():
            eng[q].wait_ge(T.sem[s], v)
            for a, b in snap.get((s, v), {}).items():
                k[a] = max(k.get(a, 0), b)
            k[s] = max(k.get(s, 0), v)
        if n["sig"] is None:
            cnt[q] += 1
            sig[i] = ("q" + q, cnt[q])
            snap[sig[i]] = dict(k)
            n["call"]().then_inc(T.sem["q" + q], 1)
        else:
            n["call"]()
    for r in range(ROUNDS):
        g.wait_ge(T.sem["sent%d" % r], sent[r])
    for q in QUEUES:
        g.wait_ge(T.sem["q" + q], cnt[q])
    for k, n in enumerate(loaded):
        g.wait_ge(T.sem["dm%d" % k], n)
    g.wait_ge(T.sem.stored, stores[0])
